import numpy as np, ml_dtypes
CORES = [3,11,19,27,35,43,51,59]
N = 8
BF = ml_dtypes.bfloat16
W, L, VI, HOP = 4096, 192, 4, 3
def cols(a, j):
    return np.take_along_axis(a, j[:, :, None, :], 3)
def deal(rng, lo, hi, ends=0, two=False):
    o = rng.permutation(W); n = rng.integers(lo, hi + 1, W)
    if two: n = rng.choice(np.array([lo, hi]), W)
    rest = o[(o > 0) & (o < W - 1)]
    if ends == 1: o = np.concatenate([np.array([0, W - 1]), rest]); n[0] = 16
    if ends == 2: o = np.concatenate([np.array([0]), rest[:15], np.array([W - 1]), rest[15:]]); n[:2] = 16
    start = np.add.accumulate(n) - n; nc = int(np.searchsorted(start, W)); start = start[:nc]
    size = np.minimum(n[:nc], W - start); cid = np.repeat(np.arange(nc), size); pos = np.arange(W) - start[cid]
    sl = np.argsort(rng.random((nc, 16)), axis=1); head = o[start + (size * rng.random(nc)).astype(np.int64)]
    if ends == 1: sl[0] = np.concatenate([np.array([0, 15]), 1 + rng.permutation(14)]); head[0] = (W - 1) * int(rng.integers(0, 2))
    if ends == 2: sl[0] = np.concatenate([np.array([0]), 1 + rng.permutation(15)]); sl[1] = np.concatenate([np.array([15]), rng.permutation(15)]); head[0] = 0; head[1] = W - 1
    r = np.zeros(W, np.int64); r[o] = head[cid]
    cl = np.full((16, W), -1, np.int64); cl[sl[cid, pos], r[o]] = o
    return cl, r
def parts(rng):
    x = rng.integers(0, 256, (N, 8, 16, W)); cl = np.zeros((N, 8, 16, W), np.int64); r = np.zeros((N, 8, W), np.int64)
    for a in range(N):
        for g in range(8):
            lo, hi = ((1, 16), (1, 16), (8, 16), (1, 6))[int(rng.integers(0, 4)) if g else 0]
            cl[a, g], r[a, g] = deal(rng, lo, hi)
    o = rng.integers(0, W, (N, 8, 16, L)); z = rng.integers(0, 256, (N, 8, 16, L))
    t = np.stack([rng.integers(1300, 1800, (N, 8)), rng.integers(1000, 1600, (N, 8))], axis=-1)
    return x, cl, r, o, z, t
def hold(rng, x, cl, r, o, z, t, g, q, v):
    P = rng.permutation(W); w = np.arange(W); n = max(q)
    zero = P[:16]; due = P[16:16 + N]; hot = P[16 + N:16 + N + N * n].reshape(N, n)
    x[:, g][:, :, P[:16 + N + N * n]] = 0
    o[:, g] = rng.choice(zero, (N, 16, L)); z[:, g] = 0
    t[:, g, 0] = rng.integers(0, 13, N); t[:, g, 1] = 4080
    for a in range(N):
        k = np.full((16, W), -1, np.int64); k[rng.integers(0, 16, W), w] = w; cl[a, g] = k; r[a, g] = w
        c = hot[a, :q[a % 4]]; x[a, g][:, c] = 1; o[a, g, 0, rng.permutation(L - 1)[:len(c)]] = c
        d = int(t[a, g, 0]) + q[a % 4] + (1 if a % 4 == 3 else 0)
        x[a, g, :, int(due[a])] = (d >> 4) + (np.arange(16) < (d & 15))
        o[(a - HOP * v) % N, g, 0, L - 1] = due[a]
def pack(x, cl, r, o, z, t):
    return {"feat": x.reshape(N, 128, W).astype(np.float32).astype(BF), "memb": cl.reshape(N, 128, W).astype(np.int32), "rep": r.astype(np.int32),
            "fact": o.reshape(N, 128, L).astype(np.int32), "z": z.reshape(N, 128, L).astype(np.float32).astype(BF), "thr": t.astype(np.int32)}
def setup_inputs(rng):
    return pack(*parts(rng))
def setup_inputs_spread(rng):
    x, cl, r, o, z, t = parts(rng)
    x = np.floor(rng.random((N, 8, 16, W)) * np.exp2(rng.integers(0, 9, (N, 8, 1, W)))).astype(np.int64)
    z = np.floor(rng.random((N, 8, 16, L)) * np.exp2(rng.integers(0, 9, (N, 8, 1, L)))).astype(np.int64)
    o = np.minimum(np.floor(W * rng.random((N, 8, 16, L)) ** 3).astype(np.int64), W - 1)
    t = np.minimum(np.exp2(12 * rng.random((N, 8, 2))).astype(np.int64), 4080)
    t[:, :2, 0] = rng.integers(200, 1200, (N, 2))
    hold(rng, x, cl, r, o, z, t, 3, (127, 127, 127, 127), 1)
    hold(rng, x, cl, r, o, z, t, 5, (127, 127, 127, 127), min(VI, N) - 1)
    return pack(x, cl, r, o, z, t)
def setup_inputs_ends(rng):
    x, cl, r, o, z, t = parts(rng)
    x = 255 * np.where(rng.random((N, 8, 1, W)) < 0.6, rng.integers(0, 2, (N, 8, 1, W)), rng.integers(0, 2, (N, 8, 16, W)))
    z = 255 * np.where(rng.random((N, 8, 1, L)) < 0.6, rng.integers(0, 2, (N, 8, 1, L)), rng.integers(0, 2, (N, 8, 16, L)))
    o = np.where(rng.random((N, 8, 16, L)) < 0.7, (W - 1) * rng.integers(0, 2, (N, 8, 16, L)), o)
    far = ((((W - 1) * (W - 1)) >> 5) + W - 1) & (W - 1)
    for a in range(N):
        for g in range(8):
            both = 1 if g % 2 == 0 else 2
            cl[a, g], r[a, g] = deal(rng, 1, 16, both)
            t[a, g, 0] = 4080 if (g + a) % 4 == 1 else 0
            t[a, g, 1] = 4080 if (g + a) % 2 == 0 else 0
            x[a, g, :, far] = 255; x[a, g, :, W - 1] = 255
            if both == 1:
                x[a, g, :, int(r[a, g, 0])] = 255
                for b in (0, L - 1):
                    z[a, g, :, b] = 0; o[a, g, 0, b] = 0; o[a, g, 15, b] = W - 1
            else: x[a, g, :, 0] = 0
            if g == 7:
                z[a, g] = 255; z[a, g, :, L - 1] = 0; o[a, g, :, L - 1] = 0; o[a, g, 15, L - 1] = W - 1; o[a, g, int(rng.integers(0, 16)), :L - 1] = 0
    return pack(x, cl, r, o, z, t)
def setup_inputs_corners(rng):
    x, cl, r, o, z, t = parts(rng); w = np.arange(W)
    for a in range(N):
        for g in range(8):
            kind = (g + a) % 4; how = (3 * g + a) % 8
            if kind == 0: cl[a, g], r[a, g] = deal(rng, 16, 16)
            elif kind == 1:
                k = np.full((16, W), -1, np.int64); k[15 * rng.integers(0, 2, W), w] = w; cl[a, g] = k; r[a, g] = w
            elif kind == 2: cl[a, g], r[a, g] = deal(rng, 1, 16, 0, True)
            else: cl[a, g], r[a, g] = deal(rng, 15, 16)
            if how == 0: o[a, g] = r[a, g][o[a, g]]
            elif how == 1:
                no = np.flatnonzero(r[a, g] != w)
                if len(no): o[a, g] = rng.choice(no, (16, L))
            elif how == 2: o[a, g] = (W - 1) * rng.integers(0, 2, (16, L))
            elif how == 3: o[a, g] = rng.integers(0, W, (1, L))
            elif how == 4: o[a, g] = np.arange(L)[None, :]
            t[a, g, 0] = (1300, 0, 4080, 1600)[(g // 2 + a) % 4]
            t[a, g, 1] = (0, 1300, 4080, 1100)[(g + a // 2) % 4]
    z[..., 0::4] = 0; z[..., 1::4] = 255; z[..., 2::4] = cols(x, o[:, :, 0, 2::4])
    mm = W - 3; oo = W - 21; s = (((mm * oo) >> 5) + mm) & (W - 1)
    for a in range(N):
        n = (17, 16, 127, 40)[a % 4]; cl[a, 6], r[a, 6] = deal(rng, 2, 6)
        c = rng.permutation(np.flatnonzero(r[a, 6] == w))[:n]
        x[a, 6][:, c] = 0; z[a, 6, :, :n] = 255; o[a, 6, 0, :n] = c; t[a, 6, 0] = 4079; t[a, 6, 1] = 0
        k, e = deal(rng, 1, 16, 1); h = int(e[0]); p = np.arange(W)
        p[h] = oo; p[oo] = h; p[W - 1 - h] = mm; p[mm] = W - 1 - h
        cl[a, 7] = np.where(k >= 0, p[np.maximum(k, 0)], -1)[:, p]; r[a, 7] = p[e[p]]
        x[a, 7][:, np.array([int(r[a, 7, W - 1]), int(r[a, 7, W - 5]), oo, s])] = 0; x[a, 7][:, np.array([mm, s + 1])] = 255
        z[a, 7, :, 0] = 255; o[a, 7, :, 0] = oo; t[a, 7, 0] = 1000; t[a, 7, 1] = 4079
        z[a, 7, :, L - 8:] = 255; i = int(rng.integers(0, 16)); z[a, 7, i, L - 8:L - 4] = 240; z[a, 7, i, L - 4:] = 252
        o[a, 7, :, L - 8:L - 4] = W - 1; o[a, 7, :, L - 4:] = W - 5
    return pack(x, cl, r, o, z, t)
def setup_inputs_crowd(rng):
    x, cl, r, o, z, t = parts(rng); f = rng.integers(0, W, 8); f[5] = W - 1
    for g in (0, 1, 5): o[:, g] = f[g]
    o[:, 1, :, L - 1] = rng.integers(0, W, (N, 16))
    o[:, 2] = rng.choice(np.array([0, int(f[2]), W - 1]), (N, 16, L))
    t[:, (0, 1, 2, 5), 0] = rng.integers(0, 200, (N, 4))
    h = int(rng.integers(0, N))
    for g in (3, 4):
        j = int(rng.integers(0, W - 37)); w = j + 37
        P = rng.permutation(W); P = np.concatenate([P[(P != j) & (P != w)], np.array([j, w])])
        c = P[:4 * L]; b = P[4 * L:8 * L]; rest = P[8 * L:]; zero = rest[:16]; y = int(rest[-3])
        for a in range(N):
            x[a, g][:, c] = 128; x[a, g][:, b] = 0; x[a, g][:, zero] = 0; x[a, g][:, np.array([j, w, y])] = 0
            sl = np.sort(np.argsort(rng.random((4 * L, 16)), axis=1)[:, :2], axis=1)
            k = np.full((16, W), -1, np.int64); k[sl[:, 0], c] = b; k[sl[:, 1], c] = c; k[rng.integers(0, 16, len(rest)), rest] = rest
            k[:, y] = -1; k[:, w] = -1; k[0, w] = y; k[15, w] = w
            cl[a, g] = k; r[a, g] = np.arange(W); r[a, g][b] = c; r[a, g, y] = w
            p = (a % 4) * L + np.arange(L)
            o[a, g] = rng.choice(zero, (16, L)); o[a, g, 0] = np.where(rng.random(L) < 0.5, c[p], b[p])
            if g == 4: o[a, g, 0, L - 1] = zero[0]
            z[a, g] = 0
        q = L if g == 3 else L - 1
        t[:, g, 0] = 2047 - max([(v * q) & 127 for v in range(VI)]); t[:, g, 1] = 0
        if g == 3:
            x[h, g][:, np.array([j, w])] = 128; o[h, g, 1] = j
        else:
            d = int(t[h, g, 0]) + ((q & 127) >> 1); x[h, g, :, w] = (d >> 4) + (np.arange(16) < (d & 15)); o[(h - HOP) % N, g, 0, L - 1] = w
    n = W >> 4
    for a in range(N):
        for g in (6, 7):
            K = rng.permutation(W).reshape(16, n); c = K[rng.integers(1, 16, n), np.arange(n)]
            k = np.full((16, W), -1, np.int64); k[:, c] = K; cl[a, g] = k; r[a, g][K] = c[None, :]
            p = rng.permutation(n)[:L]; o[a, g] = K[rng.integers(0, 16, (16, L)), p[None, :]]
            if g == 6:
                x[a, g][:, c] = 0; z[a, g] = 255; t[a, g] = rng.integers(0, 200, 2)
            else:
                x[a, g][:, c] = 255; x[a, g][:, K[0]] = 0; z[a, g] = 0; t[a, g, 0] = int(rng.integers(1000, 3000)); t[a, g, 1] = 4080
    return pack(x, cl, r, o, z, t)
def setup_inputs_ties(rng):
    x, cl, r, o, z, t = parts(rng)
    x = 64 * rng.integers(0, 4, x.shape); z = 64 * rng.integers(0, 4, z.shape)
    for g in range(0, 8, 2):
        few = rng.permutation(W)[:64]; o[:, g] = rng.choice(few, (N, 16, L))
    t = np.stack([64 * rng.integers(20, 28, (N, 8)), 64 * rng.integers(16, 25, (N, 8))], axis=-1)
    hold(rng, x, cl, r, o, z, t, 1, (1, 2, 3, 0), 1)
    hold(rng, x, cl, r, o, z, t, 5, (1, 2, 3, 0), min(VI, N) - 1)
    return pack(x, cl, r, o, z, t)
def check_inputs(d):
    bad = []
    for k, lo, hi in (("feat", 0, 255), ("memb", -1, W - 1), ("rep", 0, W - 1), ("fact", 0, W - 1), ("z", 0, 255), ("thr", 0, 4080)):
        v = np.asarray(d[k]).astype(np.float64)
        if not (np.all(v >= lo) and np.all(v <= hi)): bad.append("range of " + k)
        elif not np.all(v == np.floor(v)): bad.append("whole numbers in " + k)
    if bad: return bad
    cl = np.asarray(d["memb"]).astype(np.int64).reshape(N, 8, 16, W); r = np.asarray(d["rep"]).astype(np.int64)
    for a in range(N):
        for g in range(8):
            k, c = np.nonzero(cl[a, g] >= 0); m = cl[a, g][k, c]; q = r[a, g]
            if not np.all(np.bincount(m, minlength=W) == 1): bad.append("memb: every column in exactly one class")
            if not np.all(q[m] == c): bad.append("rep and memb agree")
            if not np.all(q[q] == q): bad.append("rep: a representative is a member of its own class")
    return sorted(set(bad))
def reference(feat, memb, rep, fact, z, thr):
    x = feat.astype(np.float32).astype(np.int64).reshape(N, 8, 16, W); cl = memb.astype(np.int64).reshape(N, 8, 16, W); r = rep.astype(np.int64)
    o = fact.astype(np.int64).reshape(N, 8, 16, L); y = z.astype(np.float32).astype(np.int64).reshape(N, 8, 16, L)
    t1 = thr[:, :, 0].astype(np.int64); t2 = thr[:, :, 1].astype(np.int64); A = np.zeros((N, 8), np.int64)
    row = np.arange(16)[None, None, :, None]
    for v in range(VI):
        n = np.take_along_axis(r, o.reshape(N, 8, 16 * L), 2)
        D = np.sum(np.abs(cols(x, n).reshape(N, 8, 16, 16, L) - y[:, :, :, None, :]), axis=2)
        n = n.reshape(N, 8, 16, L); ks = np.argmax(D, axis=2)[:, :, None, :]
        ds = np.take_along_axis(D, ks, 2)[:, :, 0]; c = np.take_along_axis(n, ks, 2)[:, :, 0]; ob = np.take_along_axis(o, ks, 2)
        want = ds > (t1 + (A & 127))[:, :, None]
        win = np.zeros((N, 8, L), bool)
        for a in range(N):
            for g in range(8):
                win[a, g, np.unique(np.where(want[a, g], c[a, g], W + np.arange(L)), return_index=True)[1]] = True
        win = win & want
        m = cols(cl, c); has = (m >= 0) & win[:, :, None, :]; mm = np.maximum(m, 0)
        s = (((mm * ob) >> 5) + mm) & (W - 1)
        both = np.minimum(cols(x, mm.reshape(N, 8, 16 * L)), cols(x, s.reshape(N, 8, 16 * L))).reshape(N, 8, 16, 16, L)
        e = np.sum(np.abs(both - y[:, :, :, None, :]), axis=2)
        keep = has & (e <= t2[:, :, None, None]); gone = has & ~keep; got = np.any(keep, axis=2)
        best = np.argmin(np.where(keep, e, 2 ** 20), axis=2)[:, :, None, :]
        cp = np.where(got, np.take_along_axis(mm, best, 2)[:, :, 0], 0)
        ynew = np.where(got[:, :, None, :], (y + cols(x, cp)) >> 1, np.abs(y - cols(x, c)))
        for a in range(N):
            for g in range(8):
                k = cl[a, g]; k[:, c[a, g][win[a, g]]] = -1
                ex = m[a, g][gone[a, g]]; k[0, ex] = ex; r[a, g, ex] = ex
                b = np.flatnonzero(got[a, g]); k[:, cp[a, g][b]] = np.where(keep[a, g][:, b], m[a, g][:, b], -1)
                i, b = np.nonzero(keep[a, g]); r[a, g, m[a, g][i, b]] = cp[a, g][b]
        u = np.sum(y, axis=2)[:, :, None, :]
        o = np.where(D > t1[:, :, None, None], (((o * u) >> 5) + o + 37 * row) & (W - 1), o)
        y = ynew; A = A + np.sum(win, axis=2)
        if v < VI - 1: o = np.roll(o, HOP, axis=0); y = np.roll(y, HOP, axis=0)
    yc = np.sum((cl + 1) * (row + 1), axis=2)
    return {"yc": yc.astype(np.float32), "yr": r.astype(np.float32), "yo": o.reshape(N, 128, L).astype(np.float32), "yz": y.reshape(N, 128, L).astype(np.float32)}

@@ -1,0 +1,711 @@
+from concourse.mybir import AluOpType as ALU, AxisListType as AX, ActivationFunctionType as AF
+
+W, L, VI, HOP = 4096, 192, 4, 3
+PAD, SB, NONE = 4288, 4304, 8400
+F32, BF, I32, U16 = "float32", "bfloat16", "int32", "uint16"
+M1, M6 = 1.5 * 2.0 ** 24, 1.5 * 2.0 ** 29
+M8, M16, MZ = 1.5 * 2.0 ** 31, 1.5 * 2.0 ** 39, 2.0 ** 62
+
+_S = {
+    "XX": (SB + 2 * W, BF), "MC": (8416, F32), "MI": (W, I32), "IO": (8608, F32), "P": (W, BF), "F": (PAD, BF),
+    "HN": (L, BF), "CBS": (L, BF), "KN": (2 * L, BF), "ZR": (3 * L, BF), "ZM": (L, F32),
+    "G1B": (3072, BF), "GD": (6144, BF), "AB": (3072, BF), "AM": (3264, F32), "EQ": (1248, BF),
+    "REP": (256, I32), "LA": (256, U16), "CA": (256, I32), "TA": (256, I32), "DA": (1280, BF), "PWA": (256, F32), "DY": (768, BF),
+    "YA": (256, F32), "YT": (256, F32), "CF": (256, F32), "NEG": (256, BF), "XR": (3 * L, BF), "IDM": (128, F32),
+    "FCT": (L, I32), "FH": (2 * L, BF), "TH": (4, I32), "THF": (4, F32), "CO": (32, F32), "AI": (8, I32),
+    "IT": (L, I32), "I2": (L, I32), "DG": (L, F32), "RS": (L, F32), "WS": (L, F32), "TD": (L, F32),
+    "KC": (L, BF), "C37": (L, F32), "EC": (L, F32), "LC": (64, F32), "UL": (12, U16),
+    "ZB": (144, F32), "ZZ": (9 * 144, BF), "ZK": (144, F32), "BF": (128, F32), "BB": (4 * 128, BF), "WF": (3 * 128, F32), "CM": (64, F32),
+    "OL": (4 * L, U16), "OS": (4 * L, U16), "ZL": (8 * L, BF), "ZS": (4 * L, BF),
+    "OF": (L, F32), "PW": (L, F32), "CL": (L, U16), "V1": (L, I32), "V2": (L, I32), "V3": (L, F32),
+    "ID": (L, I32), "IL": (L, U16), "DH": (2 * L, I32), "KY": (768, I32), "UT": (16, F32), "P1": (L, I32), "P2": (L, I32),
+    "P4": (L, F32), "P5": (L, I32), "P6": (L, I32), "SI": (128, I32), "SF": (256, F32), "SU": (128, U16),
+    "IDF": (L, F32), "OG": (L, BF), "ML": (L, U16), "M": (L, F32), "S1": (L, I32), "S2": (L, I32), "S3": (L, I32),
+    "SL": (L, U16), "ZN": (L, BF), "LO": (L, F32), "LS": (L, F32), "Z1": (L, F32), "NIM": (128, F32), "XC": (L, BF), "KP": (L, F32),
+    "KM": (L, F32), "CBV": (L, F32), "FA": (L, F32), "FC": (L, F32), "FT": (L, F32), "FG": (L, BF), "YO": (L, F32), "YZ": (L, F32),
+}
+ALIAS = {"G2B": ("GD", 0, 3072), "YB": ("GD", 0, 3072), "DB": ("GD", 3072, 3072), "EB": ("GD", 3072, 3072), "FL": ("GD", 0, W),
+         "COL": ("IO", SB, W), "FV": ("KY", 0, 256), "FB": ("KY", 256, 256), "FE": ("AM", 256, 256), "FR": ("AM", 512, 256),
+         "FY": ("AM", 768, 256), "FZ": ("AM", 1024, 256), "FX": ("AM", 1280, 256), "FW": ("AM", 1536, 256),
+         "HF": ("YO", 0, L), "ZE": ("YZ", 0, L), "TT": ("FT", 0, L)}
+SCRATCH = {n: ("sbuf", [128, c], d) for n, (c, d) in _S.items()}
+for _n, _c in (("E0", 64), ("E1", 32), ("E2", 16), ("E3", 8), ("E4", 4)):
+    SCRATCH[_n] = ("sbuf", [128, 3, _c], I32)
+for _b in range(8):
+    SCRATCH["B%d" % _b] = ("psum", [128, 512], F32)
+NDMA = 40
+SEMAPHORES = ["cV", "cS", "cP", "cG", "sent"] + ["ar%d" % i for i in range(8)] + ["d%d" % i for i in range(NDMA)]
+SAMEQ = True
+
+
+def rank_program(g, core, T, topo):
+    rank = T.rank_of(core)
+    if rank is None:
+        return
+    n = len(T.cores)
+    dst = T.cores[(rank + HOP) % n]
+    rid, pid, _e = topo.addr(dst)
+    emask, neng = topo.mask(core, dst), len(topo.engines(core, dst))
+    Q = {"V": g.vector, "S": g.scalar, "P": g.tensor, "G": g, "Y": g.sync}
+    ops = []
+
+    def A(nm, lo=0, hi=None, st=1, p=None):
+        if nm in ALIAS:
+            nm, off, n_ = ALIAS[nm]
+            lo, hi = lo + off, off + (n_ if hi is None else hi)
+        if hi is None:
+            hi = SCRATCH[nm][1][1]
+        ps = slice(None) if p is None else slice(p, 128, 16)
+        ap_ = T[nm][ps, lo:hi] if st == 1 else T[nm][ps, lo:hi:st]
+        if st > 1 and p is None and hi - lo > 64:
+            p = ("phase", lo % st)
+        return (ap_, [(nm, lo, hi, p)])
+
+    def C(nm, c):
+        return A(nm, c, c + 1)
+
+    def A3(nm, lo=None, hi=None):
+        return (T[nm][:] if lo is None else T[nm][:, :, lo:hi], [(nm, 0, 1 << 20, None)])
+
+    def IN(w, o):
+        return (w[0].indirect(o[0]), w[1], o[1])
+
+    def rd(*xs):
+        r = []
+        for x in xs:
+            if isinstance(x, tuple):
+                for y in x[1:]:
+                    r += y
+        return r
+
+    def ap(x):
+        return x[0] if isinstance(x, tuple) else x
+
+    def op(q, fn, out, ins, kind="c"):
+        ops.append({"q": q, "fn": fn, "w": list(out[1]) if out else [], "r": rd(*ins) + (list(out[2]) if out and len(out) > 2 else []), "k": kind})
+
+    def cp(o, i):
+        op("V", lambda: g.vector.tensor_copy(o[0], i[0]), o, [i])
+
+    def tt(o, a, b, f):
+        op("V", lambda: g.vector.tensor_tensor(o[0], a[0], b[0], f), o, [a, b])
+
+    def ts(o, a, s1, f1, s2=None, f2=None):
+        if f2 is None:
+            op("V", lambda: g.vector.tensor_scalar(o[0], a[0], ap(s1), None, f1), o, [a, s1])
+        else:
+            op("V", lambda: g.vector.tensor_scalar(o[0], a[0], ap(s1), ap(s2), f1, f2), o, [a, s1, s2])
+
+    def ms(o, v):
+        op("V", lambda: g.vector.memset(o[0], v), o, [])
+
+    def scan(o, a, b, init):
+        op("V", lambda: g.vector.tensor_tensor_scan(o[0], a[0], b[0], init, ALU.mult, ALU.add), o, [a, b])
+
+    def red(o, a):
+        op("V", lambda: g.vector.tensor_reduce(o[0], a[0], AX.X, ALU.add), o, [a])
+
+    def act(o, i, f=AF.Identity, bias=0.0, scale=1.0):
+        op("S", lambda: g.scalar.activation(o[0], i[0], f, bias=ap(bias), scale=ap(scale)), o, [i, bias, scale])
+
+    def gat(q, o, i):
+        if q == "V":
+            cp(o, i)
+        else:
+            act(o, i, AF.Copy)
+
+    def mm(o, w, r, a, b):
+        op("P", lambda: g.tensor.matmul(o[0], w[0], r[0], a, b), o, [w, r])
+
+    def iota(o, pat, base, cm):
+        if SCRATCH[o[1][0][0]][2] == I32:
+            op("G", lambda: g.iota(o[0], pat, base, cm), o, [])
+        else:
+            op("G", lambda: g.iota(o[0], pat, base, cm, allow_small_or_imprecise_dtypes=True), o, [])
+
+    def dma(o, i, q="Y"):
+        op(q, lambda: Q[q].dma_start(o[0], i[0]), o, [i], "d")
+
+    def H(x):
+        return (x, [])
+
+    def send(o, i, k):
+        op("G", lambda: g.remote_dma(o[0], i[0], T.sem["ar%d" % k], T.sem.sent, pid, rid, emask), None, [i], "s")
+
+    def arrive(o, k):
+        ops.append({"q": None, "fn": None, "w": list(o[1]), "r": [], "k": "a", "sem": "ar%d" % k})
+
+    def Z(v, r):
+        return A("ZZ", 144 * v + 15 - r, 144 * v + 143 - r)
+
+    def ZV(v):
+        return A("ZZ", 144 * v, 144 * v + 144)
+    Z1, Z4K, ZPOW, Z01, Z2, Z34, Z23, Z456, ZSL = range(9)
+    BK, BK34, IDN, NID = (A("BB", 128 * i, 128 * i + 128) for i in range(4))
+
+    def deal(o, v, buf, lo, hi, first=True):
+        for r in range(16):
+            mm(o, Z(v, r), A(buf, lo + r, hi, 16), first and r == 0, r == 15)
+
+    RC, T1P, THW, T2K, CAPM, CBB, ACC, WP, MA, MB, C01, C23, C34, C456, K1, X0, X1, X2, X3, NMA, NMB, XA, X4, X5, X6 = (C("CO", i) for i in range(25))
+    AIX, ALT, CAPC, IDXC = (A("LC", 16 * i, 16 * i + 12) for i in range(4))
+    add, sub, mul, mx, mn = ALU.add, ALU.subtract, ALU.mult, ALU.max, ALU.min
+    band, shr = ALU.bitwise_and, ALU.arith_shift_right
+
+    ms(A("TH"), 0)
+    dma(A("REP"), H(T.rep[:])); dma(A("FCT"), H(T.fact[:]))
+    dma(A("ZL", 0, L), H(T.z[:])); dma(A("TH", 0, 2, p=0), H(T.thr[:]))
+    dma(A("MI"), H(T.memb[:]))
+    iota(A("IT"), [[1, L]], 128, -1)
+    iota(A("CA"), [[1, 256]], 0, 256)
+    iota(C("AI", 0), [[0, 1]], 0, 1)
+    iota(A("I2"), [[1, L]], 0, 0)
+    iota(A("COL", 0, 2048), [[1, 128], [256, 16]], 0, 0)
+    iota(A("IO", 0, 1076), [[1, 1076]], 0, 0)
+    ms(A("P", 0, 1024), 0.0)
+    act(A("P", 1024, 2048), A("P", 0, 1024), AF.Copy)
+    act(A("P", 2048, W), A("P", 0, 2048), AF.Copy)
+    ms(A("HF"), 0.5); ms(A("ZE"), 0.0); ms(A("XX", W, SB), -256.0)
+    ms(A("HN", 0, 144), -0.5); ms(A("HN", 144, L), 0.0); ms(A("NEG"), -1.0)
+    ms(A("CM", 0, 16), 2.0); ms(ACC, 0.0); ms(A("WF"), 0.0)
+    scan(A("LS"), A("HF"), A("ZE"), 2.0 ** 96)
+    scan(A("CM", 16, 32), A("CM", 0, 16), A("ZE", 0, 16), 0.5)
+    ts(C("AI", 1), C("AI", 0), 15, band)
+    ts(A("P1"), A("IT"), 15, band)
+    ts(A("CA"), A("CA"), W - 1, band)
+    cp(RC, C("AI", 1))
+    ts(A("DG"), A("P1"), 0.0, ALU.is_equal)
+    ts(A("FH", L, 2 * L), A("FCT"), M6, add, M6, sub)
+    ts(A("DA", 256, 512), A("REP"), M6, add, M6, sub)
+    tt(A("FH", 0, L), A("FCT"), A("FH", L, 2 * L), sub)
+    ts(A("DA", 1024, 1280), A("CA"), M6, add, M6, sub)
+    tt(A("DA", 0, 256), A("REP"), A("DA", 256, 512), sub)
+    ts(A("ZB"), A("IT", 0, 144), RC, add, 143.0, ALU.is_equal)
+    tt(A("DA", 768, 1024), A("CA"), A("DA", 1024, 1280), sub)
+    for row in (1, 0, 4, 3):
+        dma(A("P", p=row), A("DA", 256 * row, 256 * row + 256))
+    dma(A("XX", SB, SB + W), H(T.feat[:]))
+    cp(ZV(Z1), A("ZB"))
+    red(C01, A("DG", 0, 2))
+    for k in range(16):
+        act(A("G1B", L * k, L * k + L), A("FH", L, 2 * L), scale=C("DG", k))
+        ts(A("AB", L * k, L * k + L), A("FH", 0, L), C("DG", k), mul)
+    act(A("COL", 2048, W), A("COL", 0, 2048), bias=128.0)
+    OP, O37 = A("B1", L, 2 * L), A("B0", L, 2 * L)
+    for r in range(16):
+        mm(OP, Z(Z1, r), A("G1B", r, 3072, 16), r == 0, False)
+    deal(OP, Z1, "AB", 0, 3072, first=False)
+    ts(ZV(Z01), A("ZB"), C01, mul)
+    cp(A("LA"), A("REP"))
+    ts(A("TT", 0, 128), A("IT", 0, 128), RC, add, 128.0, ALU.is_ge)
+    ts(A("TD", 0, 128), A("IT", 0, 128), RC, add, 143.0, ALU.is_le)
+    cp(A("THF"), A("TH"))
+    red(C34, A("DG", 3, 5))
+    tt(A("BF"), A("TT", 0, 128), A("TD", 0, 128), mul)
+    ts(A("IDM"), A("IT", 0, 128), 128.0, ALU.is_equal)
+    mm(A("B2", 0, 2), A("BF"), A("THF", 0, 2), True, True)
+    ts(A("V1"), A("I2"), 15, band)
+    cp(IDN, A("IDM"))
+    tt(A("TT"), A("LS"), A("DG"), mul)
+    ts(A("RS"), A("V1"), 0.0, ALU.is_gt)
+    ts(NID, A("IDM"), -1.0, mul)
+    scan(A("WS"), A("RS"), A("TT"), 0.0)
+    ts(ZV(Z4K), A("ZB"), 4096.0, mul)
+    ts(ZV(ZSL), A("ZB"), C("WS", 95), mul)
+    cp(A("OL", 0, L), OP)
+    act(A("OF"), OP, AF.Copy)
+
+    def g1(v, q, k0, k1, lst="OL"):
+        gat(q, A("G1B", L * k0, L * k1), IN(A("P"), A(lst, L * v + 12 * k0, L * v + 12 * k1)))
+
+    def g1pe(bank, off, kind, k0, k1):
+        deal(A(bank, off + 12 * k0, off + 12 * k1), kind, "G1B", L * k0, L * k1)
+
+    for k0, k1 in ((0, 6), (6, 12), (12, 16)):
+        g1(0, "S", k0, k1)
+    iota(A("MC", W, SB), [[0, SB - W]], -1, 0)
+    iota(A("KC"), [[-256, 16], [0, 12]], 3840, 0)
+    iota(A("C37"), [[37, 16], [0, 12]], 0, 0)
+    iota(A("KN", 0, L), [[-32, 16], [0, 12]], 0, 0)
+    iota(A("KN", L, 2 * L), [[-5, 16], [0, 12]], 0, 0)
+    iota(A("EC"), [[1024, 3], [1, 16], [256, 4]], 0, 0)
+    o_, i_ = A("MC", 0, W), A("MI")
+    op("G", lambda: g.affine_select(o_[0], i_[0], [[0, W]], ALU.is_ge, 0.0, 1, 0), o_, [i_])
+    iota(A("F"), [[0, PAD]], 0, 0)
+    dma(A("XX", SB + W, SB + 2 * W), H(T.feat[:]))
+    dma(A("XX", 0, W), H(T.feat[:]))
+    act(A("IO", 1076, 2152), A("IO", 0, 1076), bias=1076.0)
+    for j, c in enumerate((3, 0, 1, 2)):
+        tt(A("FL", 1024 * c, 1024 * c + 1024), IN(A("MI"), A("LA", 64 * c, 64 * c + 64)), A("COL", 1024 * c, 1024 * c + 1024), ALU.is_equal)
+        deal(A("B3", 64 * c, 64 * c + 64), ZSL, "FL", 1024 * c, 1024 * c + 1024)
+        if j < 3:
+            g1pe("B0", 0, Z01, (0, 6, 12)[j], (6, 12, 16)[j])
+    cp(A("IL"), A("B0", 0, L))
+    act(A("ZL", L, 2 * L), A("ZL", 0, L), AF.Copy)
+
+    def slot_row():
+        act(A("PWA"), A("B3", 0, 256), AF.Copy)
+        act(A("DA", 512, 768), A("B3", 0, 256), AF.Copy)
+        dma(A("P", p=2), A("DA", 512, 768))
+
+    def o37():
+        mm(O37, A("IDM"), A("OF"), True, False)
+        mm(O37, A("IDM"), A("C37"), False, True)
+
+    def usum(zo):
+        for r in range(16):
+            mm(A("B7", 0, 12), Z(Z1, r), A("ZL", zo + r, zo + L, 16), r == 0, r == 15)
+
+    def yc_start(i0, i1):
+        for i in range(i0, i1):
+            mm(A("B3", 0, 256), A("ZK", 15 - i, 143 - i), A("MC", 256 * i, 256 * i + 256), i == 0, i == 15)
+    usum(0)
+
+    def late_constants():
+        ts(K1, RC, 1.0, add)
+        cp(A("ID"), A("B0", 0, L))
+        ts(A("ZK"), A("ZB"), K1, mul)
+        ts(AIX, A("I2", 0, L, 16), RC, add)
+        ts(T1P, C("B2", 0), 1.0, add)
+        ts(A("SI", 0, 12), AIX, -5.5, add, 1.0 / 12, mul)
+        ts(THW, C("B2", 0), 1.0, add, 4096.0, mul)
+        ts(A("SF", 0, 12), A("SI", 0, 12), -12.0, mul)
+        ts(CBB, C("B2", 0), -64.0 * 4096, mul, -64.0 * 3968, add)
+        tt(A("SF", 16, 28), A("SF", 0, 12), AIX, add)
+        ts(T2K, C("B2", 1), 4096.0, mul)
+        cp(A("UL"), A("SF", 16, 28))
+        ts(CAPM, C("B2", 1), 1.0, add, 4096.0, mul)
+        ts(IDXC, AIX, 2880.0, add)
+        ts(BK34, A("BF"), C34, mul)
+        act(A("IO", 2152, 3228), A("IO", 0, 1076), bias=2152.0)
+
+    def step3_constants():
+        cp(BK, A("BF"))
+        ts(A("TD"), A("DG"), -9e29, mul, 9e29, add)
+        ts(A("LO"), A("TT"), 2.5, mul)
+        ts(X0, RC, 16.0, mul)
+        tt(A("TD"), A("TD"), A("LO"), add)
+        ts(A("EC"), A("EC"), X0, add)
+        ts(ALT, AIX, 4096.0, add)
+        ts(CAPC, AIX, -1024.0, add)
+        ts(ZV(Z34), A("ZB"), C34, mul)
+        ts(ZV(Z2), A("ZB"), C("DG", 2), mul)
+
+    def f_constants():
+        ts(X1, C("DG", 15), -2.0, mul, 1.0, add)
+        tt(A("CM", 32, 48), A("CM", 16, 32), A("DG", 0, 16), mul)
+        red(X3, A("DG", 1, 6, 2))
+        red(X2, A("CM", 32, 48))
+        ts(X4, C("DG", 6), M16, mul)
+        tt(WP, X2, X1, mul)
+        ts(MA, X3, M8, mul, X4, add)
+        ts(ZV(ZPOW), A("ZB"), WP, mul, 0.5, mul)
+
+    def f_weights():
+        for m, rows, wcol in ((0, (0, 1), WP), (1, (2, 3), 1.0), (2, (4, 5, 6), K1)):
+            for r in rows:
+                ts(A("WF", 128 * m + r, 128 * m + 128, 16), A("BF", r, 128, 16), wcol, mul)
+
+    def f_late():
+        red(X5, A("DG", 0, 5, 2))
+        ts(X6, C("DG", 5), M16, mul)
+        ts(NMA, MA, -1.0, mul)
+        ts(X2, X5, C("DG", 5), add, -1.0, add)
+        ts(X3, X5, M8, mul, X6, add)
+        iota(A("IO", SB, 2 * SB), [[1, SB]], SB, 0)
+        ts(MB, X2, -MZ, mul, X3, add)
+        ts(A("NIM"), A("IDM"), -1.0, mul)
+        ts(NMB, MB, -1.0, mul)
+
+    def end_constants():
+        red(C23, A("DG", 2, 4))
+        red(C456, A("DG", 4, 7))
+        ts(ZV(Z23), A("ZB"), C23, mul)
+        ts(ZV(Z456), A("ZB"), C456, mul)
+
+    def yc_digits():
+        ts(A("DY", 512, 768), A("YA"), M16, add, M16, sub)
+        ts(A("YT"), A("YA"), M8, add, M8, sub)
+        tt(A("DY", 0, 256), A("YA"), A("YT"), sub)
+        tt(A("DY", 256, 512), A("YT"), A("DY", 512, 768), sub)
+        dma(A("F", 0, W, p=0), A("NEG"))
+        for row in (2, 3):
+            dma(A("F", 0, W, p=row), A("DA", 256 * (row + 1), 256 * (row + 2)))
+        for r in range(3):
+            dma(A("F", 0, W, p=4 + r), A("DY", 256 * r, 256 * r + 256))
+
+    KH = A("KY", 744, 768, 2)
+    TGS = (A("SU", 48, 60), A("SU", 80, 92))
+    FP = A("B3", 0, L)
+
+    def f_values():
+        tt(A("CBV"), IN(A("DG", 0, 16), A("SU", 64, 76)), A("M"), mul)
+
+    def f_pe():
+        mm(FP, A("WF", 0, 128), A("KP"), True, False)
+        mm(FP, A("WF", 256, 384), A("KM"), False, False)
+        mm(FP, A("WF", 128, 256), A("CBV"), False, True)
+
+    def EQ(q):
+        o = L * q - 8 * q * (q - 1)
+        return A("EQ", o, o + L - 16 * q)
+
+    for v in range(VI):
+        last = v == VI - 1
+        zo = 2 * L * v
+        TG, TGOLD = TGS[v % 2], TGS[1 - v % 2]
+        z, zz = A("ZL", zo, zo + L), A("ZL", zo, zo + 2 * L)
+        xw = A("XX", SB, SB + W) if v == 0 else A("XX", 0, SB + W)
+        act(A("XR"), IN(xw, A("IL", 156, 192)), AF.Copy)
+        if v == 0:
+            slot_row()
+        for j, o in enumerate((A("B5", 0, L), A("B5", L, 2 * L), A("B6", 0, L))):
+            mm(o, IDN, A("XR", L * j, L * j + L), True, False)
+            mm(o, NID, z, False, True)
+
+        def dpe(k0, k1):
+            mm(A("B4", 12 * k0, 12 * k1), IDN, A("KC", 12 * k0, 12 * k1), True, False)
+            deal(A("B4", 12 * k0, 12 * k1), Z4K, "AB", L * k0, L * k1, first=False)
+        for j, (k0, k1) in enumerate(((0, 1), (1, 3), (3, 5), (5, 7), (7, 9), (9, 11), (11, 13))):
+            tt(A("DB", L * k0, L * k1), IN(xw, A("IL", 12 * k0, 12 * k1)), z if j == 0 else zz, sub)
+            if j == 1:
+                act(A("AB", 13 * L, 15 * L), A("B5", 0, 2 * L), AF.Abs)
+                act(A("AB", 15 * L, 16 * L), A("B6", 0, L), AF.Abs)
+                act(A("UT", 0, 12), A("B7", 0, 12), AF.Copy)
+                dpe(13, 16)
+                o37()
+                act(A("AB", 0, 3 * L), A("DB", 0, 3 * L), AF.Abs)
+            elif j:
+                act(A("AB", L * k0, L * k1), A("DB", L * k0, L * k1), AF.Abs)
+            if j in (2, 4, 6):
+                dpe({2: 0, 4: 5, 6: 9}[j], k1)
+        if v == 0:
+            late_constants()
+            yc_start(0, 3)
+        ts(A("DH", 0, L), A("ID"), 7, shr)
+        tt(A("P1"), IN(A("UT", 0, 12), A("UL")), A("OF"), mul)
+        ts(A("DH", L, 2 * L), A("ID"), 127, band)
+        ts(A("P2"), A("P1"), 5, shr, W - 1, band)
+        if v:
+            act(A("FT"), FP, bias=MA); act(A("LO"), FP, bias=MB)
+            act(A("FA"), A("FT"), bias=NMA); act(A("FC"), A("LO"), bias=NMB)
+            mm(A("B3", L, 2 * L), A("IDM"), A("FA"), True, False); mm(A("B3", L, 2 * L), A("NIM"), A("FC"), False, True)
+        for h in (0, 1):
+            tt(A("B2", h, L, 2), A("B4", 96, L), A("DH", L * h + 96, L * h + L), add)
+            tt(A("KY", h, L, 2), A("B4", 0, 96), A("DH", L * h, L * h + 96), add)
+        act(A("CBS"), A("B4", 0, L), AF.Relu, bias=CBB, scale=64.0)
+        cb = A("B5", L, 2 * L)
+        mm(cb, IDN, A("KN", 0, L), True, False); mm(cb, IDN, A("KN", L, 2 * L), False, False); mm(cb, IDN, A("CBS"), False, True)
+        act(A("ZM"), z, bias=-0.5)
+        if v == 0:
+            yc_start(3, 7)
+            act(A("IO", 3228, SB), A("IO", 0, 1076), bias=3228.0)
+        else:
+            act(A("FG"), A("B3", L, 2 * L), AF.Copy)
+        tt(A("KY", 384, 576), A("B2", 0, L), A("KY", 0, L), mx)
+        tt(A("KY", 576, 672), A("KY", 384, 480), A("KY", 480, 576), mx)
+        tt(A("KY", 672, 720), A("KY", 576, 624), A("KY", 624, 672), mx)
+        tt(A("KY", 744, 768), A("KY", 672, 696), A("KY", 696, 720), mx)
+        ts(A("SI", 0, 24), A("KY", 744, 768), 255, band)
+        ts(A("SF", 0, 12), KH, THW, ALU.is_lt, 16384.0, mul)
+        ts(A("SI", 32, 44), KH, 8, shr, 15, band)
+        ts(A("SF", 16, 28), A("SI", 0, 24, 2), 128.0, mul)
+        tt(A("SF", 32, 44), A("SI", 1, 24, 2), A("SF", 0, 12), add)
+        ts(A("SF", 48, 60), A("SI", 32, 44), -192.0, mul)
+        tt(A("SF", 64, 76), A("SF", 16, 28), A("SF", 32, 44), add)
+        tt(A("SF", 80, 92), A("SF", 48, 60), IDXC, add)
+        ts(A("SU", 0, 12), A("SF", 64, 76), float(PAD if v == 0 else NONE), mn)
+        cp(A("SU", 16, 28), A("SF", 80, 92))
+        mw = A("MC", 0, SB) if v == 0 else A("MC")
+        ts(A("ML"), IN(mw, A("SU", 0, 12)), 16.0, add)
+        act(A("M"), IN(mw, A("SU", 0, 12)), AF.Copy)
+        act(A("OG"), IN(A("G1B"), A("SU", 16, 28)), AF.Copy)
+        mm(A("B6", 0, L), BK34, A("OG"), True, True)
+        act(A("B7", L, 2 * L), A("M"), bias=1.0)
+        if v == 0:
+            yc_start(7, 13)
+        if v < 2:
+            ms(C("IO", NONE if v else PAD), -1.0)
+        xm = A("XX", PAD)
+
+        def gm(c):
+            act(A("AM", 1024 * c, 1024 * c + 1024), IN(xm, A("ML", 64 * c, 64 * c + 64)), AF.Copy)
+        gm(0)
+        act(A("ZN"), IN(A("AB"), A("SU", 16, 28)), AF.Copy)
+        gm(1)
+        tt(A("P4"), cb, A("P2"), mn)
+        tt(A("P5"), O37, A("P4"), add)
+        tt(A("S1"), A("B6", 0, L), A("M"), mul)
+        ts(A("P6"), A("P5"), W - 1, band)
+        ts(A("S2"), A("S1"), 5, shr, W - 1, band)
+        cp(A("OS", L * v, L * v + L), A("P6"))
+        if not last:
+            send(A("OL", L * (v + 1), L * (v + 2)), A("OS", L * v, L * v + L), v + 1)
+            arrive(A("OL", L * (v + 1), L * (v + 2)), v + 1)
+        tt(A("S3"), A("B7", L, 2 * L), A("S2"), add)
+        ts(A("SL"), A("S3"), 15.0, add)
+        n2 = A("B5", L, 2 * L)
+        mm(n2, IDN, A("ZN"), True, False); mm(n2, IDN, A("ZN"), False, False); mm(n2, NID, z, False, True)
+        if v == 0:
+            iota(A("MC", SB, 8416), [[0, 8416 - SB]], -1, 0)
+
+        def gs(c):
+            tt(A("YB", 1024 * c, 1024 * c + 1024), IN(xm, A("SL", 64 * c, 64 * c + 64)), A("AM", 1024 * c, 1024 * c + 1024), mn)
+
+        def psub(c, h):
+            bank = "B%d" % (2 * (c % 2) + h)
+            for k in range(8 * h, 8 * h + 8):
+                o = A(bank, 64 * (k % 8), 64 * (k % 8) + 64)
+                mm(o, IDN, A("YB", 1024 * c + k, 1024 * c + 1024, 16), True, False)
+                mm(o, NID, A("ZL", zo + 64 * c, zo + 64 * c + 64), False, True)
+
+        def sabs(c, h):
+            act(A("EB", 1024 * c + 512 * h, 1024 * c + 512 * h + 512), A("B%d" % (2 * (c % 2) + h)), AF.Abs)
+
+        def e1(c, h):
+            for k in range(8 * h, 8 * h + 8):
+                mm(A("B4", 64 * c, 64 * c + 64), Z(Z4K, k), A("EB", 1024 * c + 64 * k, 1024 * c + 64 * k + 64), k == 0, k == 15)
+
+        def e2(c):
+            deal(A("B5", 64 * c, 64 * c + 64), Z4K, "EB", 1024 * c, 1024 * c + 1024)
+
+        def eq(q0, q1):
+            for q in range(q0, q1):
+                ts(EQ(q), A("IDF", 16 * q, L), C("SF", 64 + q), ALU.is_equal, C("WS", 16 * q + 15), mul)
+
+        def eqpe(q0, q1):
+            for q in range(q0, q1):
+                mm(A("B6", 16 * q, L), BK, EQ(q), q == 0, q == 11)
+
+        gs(0); psub(0, 0); psub(0, 1)
+        if v == 0:
+            yc_start(13, 16)
+        gm(2)
+        gs(1)
+        act(A("IDF"), IN(A("IO", 0, SB) if v == 0 else A("IO"), A("SU", 0, 12)), AF.Copy)
+        if v == 0:
+            act(A("YA"), A("B3", 0, 256), bias=136.0)
+        sabs(0, 0); sabs(0, 1)
+        psub(1, 0); psub(1, 1)
+        act(A("AM", 3072, 3264), n2, AF.Copy)
+        gs(2)
+
+        def e12(c):
+            e1(c, 0); e1(c, 1)
+        ea, eb = (e2, e12) if last else (e12, e2)
+        ea(0)
+        sabs(1, 0); sabs(1, 1)
+        psub(2, 0); psub(2, 1)
+        eq(0, 12)
+        if v == 0:
+            step3_constants()
+        ea(1)
+        sabs(2, 0); sabs(2, 1)
+        eqpe(0, 12)
+        ea(2)
+        for c in range(3):
+            eb(c)
+        if v == 0:
+            cp(A("CF"), A("CA"))
+        if v == 1:
+            yc_digits()
+        if v == 2:
+            end_constants()
+        if not last:
+            g1(v + 1, "V", 0, 4)
+        else:
+            cp(IN(A("F"), TGOLD), A("FG"))
+        tt(A("LO"), A("B6", 0, L), A("TD"), ALU.is_ge)
+        scan(A("LS"), A("RS"), A("LO"), 0.0)
+        if not last:
+            ts(A("KP"), A("B4", 0, L), T2K, ALU.is_le)
+        ts(A("SF", 96, 108), A("LS", 15, L, 16), 16384.0, mul)
+        if not last:
+            tt(A("KM"), A("B7", L, 2 * L), A("KP"), mul)
+        tt(A("SF", 112, 124), A("SF", 96, 108), A("SF", 64, 76), add)
+        if not last:
+            tt(A("SF", 144, 156), A("SF", 112, 124), ALT, mn)
+            ts(A("SF", 128, 140), A("SF", 112, 124), 9000.0, ALU.is_lt, CAPM, mul)
+            cp(TG, A("SF", 144, 156))
+            tt(A("SF", 160, 172), A("SF", 128, 140), CAPC, add)
+            ts(IN(A("MC", 0, PAD), TG), A("KM"), 1.0, mul, -1.0, add)
+            g1(v + 1, "S", 4, 10)
+            g1pe("B0", 0, Z01, 0, 10)
+            g1(v + 1, "S", 10, 16)
+            g1pe("B0", 0, Z01, 10, 16)
+            cp(A("CL"), A("B0", 0, L))
+            g1pe("B1", 0, Z2, 0, 16); g1pe("B1", L, Z34, 0, 16)
+        else:
+            g1(v, "S", 0, 16, "OS")
+        tt(A3("E0"), A("B5", 0, L), A("EC"), add)
+        if last:
+            ts(A("SF", 128, 140), A("SF", 112, 124), 9000.0, ALU.is_lt, CAPM, mul)
+        tt(A3("E1"), A3("E0", 0, 32), A3("E0", 32, 64), mn)
+        if last:
+            tt(A("SF", 160, 172), A("SF", 128, 140), CAPC, add)
+        else:
+            ts(A("SF", 176, 188), A("SF", 112, 124), 9000.0, ALU.is_lt)
+        tt(A3("E2"), A3("E1", 0, 16), A3("E1", 16, 32), mn)
+        if last:
+            tt(A("SF", 144, 156), A("SF", 112, 124), ALT, mn)
+        else:
+            red(XA, A("SF", 176, 188))
+        tt(A3("E3"), A3("E2", 0, 8), A3("E2", 8, 16), mn)
+        if last:
+            cp(TG, A("SF", 144, 156))
+        tt(A3("E4"), A3("E3", 0, 4), A3("E3", 4, 8), mn)
+        if v == 0:
+            f_constants()
+        if last:
+            ts(A("KP"), A("B4", 0, L), T2K, ALU.is_le)
+        tt(A("SI", 48, 60), A3("E4"), A("SF", 160, 172), mn)
+        if last:
+            tt(A("KM"), A("B7", L, 2 * L), A("KP"), mul)
+            mm(FP, A("WF", 0, 128), A("KP"), True, False)
+            mm(FP, A("WF", 256, 384), A("KM"), False, False)
+        ts(A("SI", 80, 92), A("SI", 48, 60), 15, band)
+        ts(A("SI", 64, 76), A("SI", 48, 60), W - 1, band)
+        cp(A("SU", 64, 76), A("SI", 80, 92))
+        cp(A("SU", 32, 44), A("SI", 64, 76))
+        if last:
+            f_values()
+            mm(FP, A("WF", 128, 256), A("CBV"), False, True)
+        zs = A("ZS", L * v, L * v + L)
+        tt(A("Z1"), IN(A("AM"), A("SU", 32, 44)), A("ZM"), add)
+        if last:
+            ts(A("FA"), FP, MA, add, MA, sub)
+            ts(A("B4", L, 2 * L), FP, MB, add, MB, sub)
+            ts(zs, A("Z1"), M1, add, M1, sub)
+            tt(A("FG"), A("FA"), A("B4", L, 2 * L), sub)
+            act(A("YZ"), zs, scale=0.5)
+            dma(H(T.yz[:]), A("YZ"))
+            cp(IN(A("F"), TG), A("FG"))
+            break
+        f_values()
+        ts(zs, A("Z1"), M1, add, M1, sub)
+        send(A("ZR", L * v, L * v + L), zs, 5 + v)
+        if v == 0:
+            dma(A("MC", SB, SB + W, p=0), A("CF"))
+        for j in range(4):
+            o, i = A("G2B", 768 * j, 768 * j + 768), IN(A("MC", 0, PAD), A("CL", 48 * j, 48 * j + 48))
+            if j < 3:
+                act(o, i, AF.Sign, bias=0.5)
+                if j == 1:
+                    act(A("XC"), IN(A("AM"), A("SU", 32, 44)), AF.Copy)
+            else:
+                ts(o, i, 0.0, ALU.is_ge, 2.0, mul)
+                cp(IN(A("XX", 0, PAD), TG), A("XC"))
+                if v:
+                    cp(IN(A("F"), TGOLD), A("FG"))
+                else:
+                    f_weights(); f_late()
+            if j % 2:
+                mm(A("B2", 48 * (j - 1), 48 * (j + 1)), IDN, A("HN", 48 * (j - 1), 48 * (j + 1)), True, False)
+                deal(A("B2", 48 * (j - 1), 48 * (j + 1)), ZPOW, "G2B", 768 * (j - 1), 768 * (j + 1), first=False)
+            if j == 1:
+                mm(C("B6", 0), A("BF"), XA, True, True)
+        f_pe()
+        act(A("PW"), A("B1", 0, L), AF.Copy)
+        act(A("OF"), OP, AF.Copy)
+        act(A("B1", 0, L), A("OF"), bias=float(SB))
+        arrive(A("ZR", L * v, L * v + L), 5 + v)
+        act(A("ZL", zo + 2 * L, zo + 3 * L), A("ZR", L * v, L * v + L), scale=0.5)
+        act(A("ZL", zo + 3 * L, zo + 4 * L), A("ZR", L * v, L * v + L), scale=0.5)
+        usum(zo + 2 * L)
+        tt(ACC, C("B6", 0), ACC, add)
+        tt(A("V1"), A("B2", 0, L), A("PW"), mul)
+        cp(C("AI", 2), ACC)
+        ts(A("V2"), A("V1"), 32768, band)
+        ts(C("AI", 3), C("AI", 2), 127, band)
+        tt(A("V3"), A("B1", 0, L), A("V2"), sub)
+        ts(THW, C("AI", 3), T1P, add, 4096.0, mul)
+        tt(A("ID"), A("B0", 0, L), A("V3"), mx)
+        cp(A("IL"), A("ID"))
+
+    for k in range(16):
+        mm(A("B0", 0, L), Z(Z34, k), A("G1B", L * k, L * k + L), k == 0, k == 15)
+    act(A("YA"), A("CF"), bias=1.0)
+    act(A("B5", 0, 256), A("CF"), AF.Copy)
+    for c in range(4):
+        for h, q in enumerate("VS"):
+            gat(q, A("FL", 1024 * c + 512 * h, 1024 * c + 512 * h + 512), IN(A("F"), A("LA", 64 * c + 32 * h, 64 * c + 32 * h + 32)))
+        deal(A("B1", 64 * c, 64 * c + 64), Z01, "FL", 1024 * c, 1024 * c + 1024)
+        deal(A("B2", 64 * c, 64 * c + 64), Z23, "FL", 1024 * c, 1024 * c + 1024)
+    act(A("YO"), A("B0", 0, L), AF.Copy)
+    dma(H(T.yo[:]), A("YO"))
+    deal(A("B3", 0, 256), Z456, "FL", 0, W)
+    tt(A("FV"), A("B1", 0, 256), A("PWA"), mul)
+    tt(A("B4", 0, 256), A("B2", 0, 256), A("CF"), sub)
+    ts(A("FB"), A("FV"), 15, shr, 1, band)
+    ts(A("B4", 256, 512), A("B4", 0, 256), 0.0, ALU.is_equal)
+    ts(A("B7", 0, 256), A("FB"), -1.0, mul, 1.0, add)
+    tt(A("FE"), A("B4", 0, 256), A("FB"), mul)
+    tt(A("B7", 256, 512), A("B7", 0, 256), A("YA"), mul)
+    tt(A("FW"), A("B4", 256, 512), A("FB"), mul)
+    tt(A("FR"), A("B5", 0, 256), A("FE"), add)
+    dma(H(T.yr[:]), A("FR"))
+    tt(A("FY"), A("B3", 0, 256), A("FW"), mul)
+    tt(A("FZ"), A("B7", 256, 512), A("FY"), add)
+    dma(H(T.yc[:]), A("FZ"), "S")
+
+    hist = {}
+    for i, o in enumerate(ops):
+        deps = set()
+        acc = [(a, False) for a in o["r"]] + [(a, True) for a in o["w"]]
+        for (nm, lo, hi, p1), wr in acc:
+            psum = SCRATCH[nm][0] == "psum"
+            for (j, l2, h2, p2, w2) in hist.get(nm, []):
+                pj = ops[j]
+                same = pj["q"] == o["q"] and pj["k"] == "c" and o["k"] == "c"
+                over = l2 < hi and lo < h2 and (p1 is None or p2 is None or p1 == p2)
+                if pj["k"] == "s":
+                    continue
+                if same:
+                    if o["q"] != "P" and over and ((w2 and not wr) or (SAMEQ and (w2 or wr))):
+                        deps.add(j)
+                elif psum or (over and (wr or w2)):
+                    deps.add(j)
+        best = {}
+        keep = []
+        for j in deps:
+            if ops[j]["k"] == "c":
+                best[ops[j]["q"]] = max(best.get(ops[j]["q"], -1), j)
+            else:
+                keep.append(j)
+        o["deps"] = sorted(keep + list(best.values()))
+        for (nm, lo, hi, p1), wr in acc:
+            hist.setdefault(nm, []).append((i, lo, hi, p1, wr))
+    seen = {q: {} for q in Q}
+    for o in ops:
+        if o["q"] is None:
+            continue
+        need = []
+        for j in o["deps"]:
+            key = ops[j]["q"] if ops[j]["k"] == "c" else j
+            if seen[o["q"]].get(key, -1) < j:
+                seen[o["q"]][key] = j
+                need.append(j)
+                ops[j]["sig"] = True
+        o["deps"] = need
+    cnt = {"V": 0, "S": 0, "P": 0, "G": 0, "d": 0, "s": 0}
+    for o in ops:
+        if o["k"] == "a":
+            o["at"] = (o["sem"], neng)
+            continue
+        for j in o["deps"]:
+            Q[o["q"]].wait_ge(T.sem[ops[j]["at"][0]], ops[j]["at"][1])
+        ins = o["fn"]()
+        if o["k"] == "d":
+            o["at"] = ("d%d" % cnt["d"], 16)
+            cnt["d"] += 1
+            ins.then_inc(T.sem[o["at"][0]], 16)
+        elif o["k"] == "s":
+            cnt["s"] += neng
+        elif o.get("sig"):
+            cnt[o["q"]] += 1
+            o["at"] = ("c" + o["q"], cnt[o["q"]])
+            ins.then_inc(T.sem[o["at"][0]], 1)
+    for o in ops:
+        if o["k"] == "d" and not o.get("sig"):
+            g.sync.wait_ge(T.sem[o["at"][0]], 16)
+    g.wait_ge(T.sem.sent, cnt["s"])

@@ -1,41 +1,136 @@
 from concourse.mybir import AluOpType as ALU, AxisListType as AX, ActivationFunctionType as AF
 
 W, L, VI, HOP = 4096, 192, 4, 3
-PAD, SB, NONE = 4288, 4304, 8400
+PAD, SB = 4288, 4352
 F32, BF, I32, U16 = "float32", "bfloat16", "int32", "uint16"
-M1, M6 = 1.5 * 2.0 ** 24, 1.5 * 2.0 ** 29
-M8, M16, MZ = 1.5 * 2.0 ** 31, 1.5 * 2.0 ** 39, 2.0 ** 62
+M0, M6 = 1.5 * 2.0 ** 23, 1.5 * 2.0 ** 29
+CYC, PECYC, GATHER, SCATTER, WAKE = 0.83e-3, 0.5e-3, 1.56, 3.0, 0.07
+DMA_RATE, DMA_FIX, HOP_TIME = 330e3, 1.8, 3.0
+KS, GV, G0V, GA, GS = 4, 112, 48, 112, 128
 
 _S = {
-    "XX": (SB + 2 * W, BF), "MC": (8416, F32), "MI": (W, I32), "IO": (8608, F32), "P": (W, BF), "F": (PAD, BF),
-    "HN": (L, BF), "CBS": (L, BF), "KN": (2 * L, BF), "ZR": (3 * L, BF), "ZM": (L, F32),
-    "G1B": (3072, BF), "GD": (6144, BF), "AB": (3072, BF), "AM": (3264, F32), "EQ": (1248, BF),
-    "REP": (256, I32), "LA": (256, U16), "CA": (256, I32), "TA": (256, I32), "DA": (1280, BF), "PWA": (256, F32), "DY": (768, BF),
-    "YA": (256, F32), "YT": (256, F32), "CF": (256, F32), "NEG": (256, BF), "XR": (3 * L, BF), "IDM": (128, F32),
-    "FCT": (L, I32), "FH": (2 * L, BF), "TH": (4, I32), "THF": (4, F32), "CO": (32, F32), "AI": (8, I32),
-    "IT": (L, I32), "I2": (L, I32), "DG": (L, F32), "RS": (L, F32), "WS": (L, F32), "TD": (L, F32),
-    "KC": (L, BF), "C37": (L, F32), "EC": (L, F32), "LC": (64, F32), "UL": (12, U16),
-    "ZB": (144, F32), "ZZ": (9 * 144, BF), "ZK": (144, F32), "BF": (128, F32), "BB": (4 * 128, BF), "WF": (3 * 128, F32), "CM": (64, F32),
-    "OL": (4 * L, U16), "OS": (4 * L, U16), "ZL": (8 * L, BF), "ZS": (4 * L, BF),
-    "OF": (L, F32), "PW": (L, F32), "CL": (L, U16), "V1": (L, I32), "V2": (L, I32), "V3": (L, F32),
-    "ID": (L, I32), "IL": (L, U16), "DH": (2 * L, I32), "KY": (768, I32), "UT": (16, F32), "P1": (L, I32), "P2": (L, I32),
-    "P4": (L, F32), "P5": (L, I32), "P6": (L, I32), "SI": (128, I32), "SF": (256, F32), "SU": (128, U16),
-    "IDF": (L, F32), "OG": (L, BF), "ML": (L, U16), "M": (L, F32), "S1": (L, I32), "S2": (L, I32), "S3": (L, I32),
-    "SL": (L, U16), "ZN": (L, BF), "LO": (L, F32), "LS": (L, F32), "Z1": (L, F32), "NIM": (128, F32), "XC": (L, BF), "KP": (L, F32),
-    "KM": (L, F32), "CBV": (L, F32), "FA": (L, F32), "FC": (L, F32), "FT": (L, F32), "FG": (L, BF), "YO": (L, F32), "YZ": (L, F32),
+    "XX": (SB + 2 * W, BF), "MC": (SB + W, F32), "MI": (W, I32), "COL": (W, F32), "P": (SB + W, BF), "F": (PAD, BF),
+    "G1B": (3072, BF), "GD": (W, BF), "AM": (3264, F32), "EQ": (1248, BF), "XR": (KS * L, BF), "DL": (L, F32),
+    "REP": (256, I32), "LA": (256, U16), "DA": (1280, BF), "PWA": (256, F32), "YA": (256, F32), "YT": (256, F32), "CF": (256, F32),
+    "C1": (256, F32), "KB": (4 * 256, BF), "FV": (256, I32), "FB": (256, I32),
+    "FCT": (L, I32), "TH": (4, I32), "THF": (4, F32), "CO": (40, F32), "AI": (8, I32), "IT": (L, I32), "I2": (16, I32), "DG": (16, F32),
+    "RS": (L, F32), "RB": (L, F32), "KC": (L, BF), "KN": (2 * L, BF), "EC": (2 * L, BF), "HN": (L, BF), "LC": (80, F32), "UL": (24, U16),
+    "ZB": (144, F32), "ZZ": (9 * 144, BF), "ZK": (144, F32), "BF": (128, F32), "BB": (7 * 128, BF), "WF": (3 * 128, F32),
+    "FM": (7 * 128, F32), "CM": (64, F32),
+    "OL": (4 * L, U16), "OS": (3 * L, U16), "ZL": (4 * L, BF), "ZS": (3 * L, BF),
+    "OF": (L, F32), "PW": (L, F32), "CL": (L, U16), "V1": (L, I32), "V2": (L, I32), "V3": (L, F32), "ID": (L, I32), "IL": (L, U16),
+    "LO": (L, I32), "HI": (L, I32), "UT": (16, F32), "P1": (L, I32), "P2": (L, I32), "P4": (L, F32), "P5": (L, I32), "P6": (L, I32),
+    "SI": (64, I32), "SF": (96, F32), "SU": (96, U16), "LT": (4 * 16, BF), "CBS": (L, BF),
+    "T2": (48, I32), "D2": (48, F32), "SC": (80, F32), "KS": (L, F32), "K32": (L, BF),
+    "IG": (L, BF), "OG": (L, BF), "XO": (L, BF), "ZN": (L, BF), "WB": (L, BF), "ML": (L, U16), "M": (L, F32),
+    "S1": (L, I32), "S2": (L, I32), "S3": (L, I32), "SL": (L, U16), "KE": (L, F32), "NK": (L, F32), "KM": (L, F32), "XC": (L, F32),
+    "CBV": (L, F32), "FI": (L, I32), "FG": (L, I32), "YO": (L, F32), "YZ": (L, F32),
 }
-ALIAS = {"G2B": ("GD", 0, 3072), "YB": ("GD", 0, 3072), "DB": ("GD", 3072, 3072), "EB": ("GD", 3072, 3072), "FL": ("GD", 0, W),
-         "COL": ("IO", SB, W), "FV": ("KY", 0, 256), "FB": ("KY", 256, 256), "FE": ("AM", 256, 256), "FR": ("AM", 512, 256),
-         "FY": ("AM", 768, 256), "FZ": ("AM", 1024, 256), "FX": ("AM", 1280, 256), "FW": ("AM", 1536, 256),
-         "HF": ("YO", 0, L), "ZE": ("YZ", 0, L), "TT": ("FT", 0, L)}
+ALIAS = {"G2B": ("GD", 0, 3072), "YB": ("GD", 0, 3072), "FL": ("GD", 0, W), "MF": ("COL", 0, W),
+         "FE": ("AM", 0, 256), "FR": ("AM", 256, 256), "FT": ("AM", 512, 256), "FU": ("AM", 768, 256), "FZ": ("AM", 1024, 256),
+         "TA": ("AM", 0, 128), "TB": ("AM", 128, 128), "FF": ("YO", 0, L)}
 SCRATCH = {n: ("sbuf", [128, c], d) for n, (c, d) in _S.items()}
-for _n, _c in (("E0", 64), ("E1", 32), ("E2", 16), ("E3", 8), ("E4", 4)):
-    SCRATCH[_n] = ("sbuf", [128, 3, _c], I32)
+for _n, _sh, _d in (("DB", [L, 16], BF), ("AB", [L, 16], BF), ("EB", [12, 256], BF), ("KY", [L, 2], I32), ("TR", [12, 16], F32)):
+    SCRATCH[_n] = ("sbuf", [128] + _sh, _d)
 for _b in range(8):
-    SCRATCH["B%d" % _b] = ("psum", [128, 512], F32)
+    SCRATCH["B%d" % _b] = ("psum", [128, 32, 16] if _b < 5 else [128, 512], F32)
 NDMA = 40
 SEMAPHORES = ["cV", "cS", "cP", "cG", "sent"] + ["ar%d" % i for i in range(8)] + ["d%d" % i for i in range(NDMA)]
-SAMEQ = True
+
+
+PLAN = []
+SLACK, ROUNDS = 0.05, 8
+
+
+def plan(ops):
+    hist, deps = {}, []
+    for i, o in enumerate(ops):
+        d = {i - 1} if o["k"] == "a" else set()
+        acc = [(a, False) for a in o["r"]] + [(a, True) for a in o["w"]]
+        for (nm, lo, hi, p1, _n), wr in acc:
+            psum = SCRATCH[nm][0] == "psum"
+            for (j, l2, h2, p2, w2) in hist.get(nm, []):
+                over = l2 < hi and lo < h2 and (p1 is None or p2 is None or p1 == p2)
+                if ops[j]["k"] != "s" and ((over and (wr or w2)) or (psum and (ops[j]["q"] != o["q"] or o["q"] == "P"))):
+                    d.add(j)
+        deps.append(d)
+        for (nm, lo, hi, p1, _n), wr in acc:
+            hist.setdefault(nm, []).append((i, lo, hi, p1, wr))
+    waits = [set(d) for d in deps]
+    prev = {}
+    for i, o in enumerate(ops):
+        if o.get("keep") and o["q"] in ("V", "S", "P", "G"):
+            deps[i] |= {prev.get(o["q"], i)} - {i}
+            prev[o["q"]] = i
+    after = [[] for _ in ops]
+    for i, d in enumerate(deps):
+        for j in d:
+            after[j].append(i)
+
+    def lag(j, i):
+        return 0.0 if ops[j]["q"] == ops[i]["q"] == "P" or j not in waits[i] else WAKE + (0.1 if ops[j]["q"] == "P" else 0.0)
+    way = [0.0] * len(ops)
+    left = [len(a) for a in after]
+    todo = [i for i, n_ in enumerate(left) if not n_]
+    while todo:
+        i = todo.pop()
+        way[i] = ops[i]["t"] + (DMA_FIX if ops[i]["k"] == "d" else 0.0) + max([way[k] + lag(i, k) for k in after[i]], default=0.0)
+        for j in deps[i]:
+            left[j] -= 1
+            if not left[j]:
+                todo.append(j)
+
+
+    def run(before, behind, way, back):
+        left, ready = [len(d) for d in before], {i: 0.0 for i, d in enumerate(before) if not d}
+        free, engines, order, ends = {}, 0.0, [], [0.0] * len(ops)
+        loads = [i for i, o in enumerate(ops) if o["q"] == "Y"][::-1 if back else 1]
+        while ready:
+            can = {k: max(t, free.get(ops[k]["q"], 0.0)) for k, t in ready.items() if ops[k]["q"] != "Y" or k == loads[0]}
+            now = min(can.values())
+            q = ops[min(can, key=lambda k: (can[k], -way[k]))]["q"]
+            mine = [k for k in can if ops[k]["q"] == q]
+            i = max((k for k in mine if can[k] <= now + 1e-9), key=lambda k: (way[k], -k))
+            for k in sorted(mine, key=can.get):
+                if q and can[i] < can[k] < can[i] + ops[i]["t"] and \
+                        max(way[k] + can[k], way[i] + can[k] + ops[k]["t"]) < max(way[i] + can[i], way[k] + can[i] + ops[i]["t"]) - SLACK:
+                    i = k
+            o = ops[i]
+            if q == "Y":
+                loads.pop(0)
+            start = can[i]
+            ready.pop(i)
+            end = start + o["t"]
+            if o["k"] == "d":
+                engines = max(engines, start + DMA_FIX / 2) + o["t"]
+                end, free[o["q"]] = engines + DMA_FIX / 2, start + 0.05
+            elif o["q"]:
+                free[o["q"]] = end
+            order.append(i)
+            ends[i] = end
+            for k in behind[i]:
+                left[k] -= 1
+                if not left[k]:
+                    ready[k] = max(ends[j] + (lag(k, j) if back else lag(j, k)) for j in before[k])
+        return order, ends
+    best = None
+    for _ in range(ROUNDS):
+        order, ends = run(deps, after, way, False)
+        if best is None or max(ends) < best[0]:
+            best = (max(ends), order)
+        way = run(after, deps, ends, True)[1]
+    order = best[1]
+    place = {i: n_ for n_, i in enumerate(order)}
+    seen, out = {}, []
+    for i in order:
+        q, need = ops[i]["q"], []
+        for j in sorted(waits[i], key=place.get, reverse=True) if q else []:
+            key = (q, ops[j]["q"] if ops[j]["k"] == "c" else j)
+            if not (q == "P" == ops[j]["q"]) and seen.get(key, -1) < place[j]:
+                seen[key] = place[j]
+                need.append(j)
+        out.append((i, need))
+    return out
 
 
 def rank_program(g, core, T, topo):
@@ -47,25 +142,61 @@ def rank_program(g, core, T, topo):
     rid, pid, _e = topo.addr(dst)
     emask, neng = topo.mask(core, dst), len(topo.engines(core, dst))
     Q = {"V": g.vector, "S": g.scalar, "P": g.tensor, "G": g, "Y": g.sync}
-    ops = []
+    ops, keep = [], [False]
+    ALL = slice(None)
 
     def A(nm, lo=0, hi=None, st=1, p=None):
         if nm in ALIAS:
             nm, off, n_ = ALIAS[nm]
             lo, hi = lo + off, off + (n_ if hi is None else hi)
+        if len(SCRATCH[nm][1]) == 3:
+            if lo % 16 == 0 and hi % 16 == 0:
+                return (T[nm][:, lo // 16:hi // 16, :], [(nm, lo, hi, None, hi - lo)])
+            return (T[nm][:, lo // 16, lo % 16:lo % 16 + hi - lo], [(nm, lo, hi, None, hi - lo)])
         if hi is None:
             hi = SCRATCH[nm][1][1]
-        ps = slice(None) if p is None else slice(p, 128, 16)
+        ps = ALL if p is None else slice(p, 128, 16)
         ap_ = T[nm][ps, lo:hi] if st == 1 else T[nm][ps, lo:hi:st]
-        if st > 1 and p is None and hi - lo > 64:
-            p = ("phase", lo % st)
-        return (ap_, [(nm, lo, hi, p)])
+        return (ap_, [(nm, lo, hi, p, len(range(lo, hi, st)))])
 
     def C(nm, c):
         return A(nm, c, c + 1)
 
-    def A3(nm, lo=None, hi=None):
-        return (T[nm][:] if lo is None else T[nm][:, :, lo:hi], [(nm, 0, 1 << 20, None)])
+    def X(nm, i1, i2, lo=0, hi=1 << 20):
+        cnt_ = 1
+        for i_, d_ in zip((i1, i2), SCRATCH[nm][1][1:]):
+            cnt_ *= len(range(d_)[i_]) if isinstance(i_, slice) else 1
+        return (T[nm][:, i1, i2], [(nm, lo, hi, None, cnt_)])
+
+    def size(x):
+        return x[1][0][4] if len(x) == 2 else 16 * x[2][0][4]
+
+    def wide(x):
+        return {F32: 4, I32: 4, BF: 2, U16: 2}[SCRATCH[x[1][0][0]][2]]
+
+    def cost(q, out, ins, kind):
+        ins = [x for x in ins if isinstance(x, tuple) and x[1]]
+        if kind == "d":
+            x = out if out[1] else ins[0]
+            return size(x) * wide(x) * (128 if x[1][0][3] is None else 8) / DMA_RATE
+        if kind == "s":
+            return 0.3
+        if q == "P":
+            return max(64, size(ins[1])) * (4 if wide(ins[1]) == 4 else 1) * PECYC
+        n_ = max([size(out)] + [size(x) for x in ins[:1]])
+        if q == "G":
+            return 0.15 + 2 * n_ * CYC
+        if len(out) == 3:
+            return 0.05 + SCATTER * n_ * CYC
+        if ins and len(ins[0]) == 3:
+            return 0.06 + GATHER * n_ * CYC
+        if q == "S":
+            return 0.06 + n_ * CYC
+        full = [x for x in ins if size(x) == n_]
+        rate = 2.0 if len(full) == 2 and kind == "tt" and all(SCRATCH[x[1][0][0]][0] == "sbuf" for x in full) else 1.0
+        if kind != "tt" and all(wide(x) == 2 for x in [out] + full):
+            rate = 0.5
+        return 0.03 + max(64, rate * n_) * CYC
 
     def IN(w, o):
         return (w[0].indirect(o[0]), w[1], o[1])
@@ -81,14 +212,22 @@ def rank_program(g, core, T, topo):
     def ap(x):
         return x[0] if isinstance(x, tuple) else x
 
-    def op(q, fn, out, ins, kind="c"):
-        ops.append({"q": q, "fn": fn, "w": list(out[1]) if out else [], "r": rd(*ins) + (list(out[2]) if out and len(out) > 2 else []), "k": kind})
+    def op(q, fn, out, ins, kind="c", more=()):
+        ops.append({"q": q, "fn": fn, "w": (list(out[1]) if out else []) + list(more),
+                    "r": rd(*ins) + (list(out[2]) if out and len(out) > 2 else []), "k": "c" if kind == "tt" else kind,
+                    "t": cost(q, out, ins, kind), "keep": keep[0]})
+        ops[-1]["fn"] = [fn]
+
+    def loose(fn, *args):
+        keep[0] = False
+        fn(*args)
+        keep[0] = True
 
     def cp(o, i):
         op("V", lambda: g.vector.tensor_copy(o[0], i[0]), o, [i])
 
     def tt(o, a, b, f):
-        op("V", lambda: g.vector.tensor_tensor(o[0], a[0], b[0], f), o, [a, b])
+        op("V", lambda: g.vector.tensor_tensor(o[0], a[0], b[0], f), o, [a, b], "tt")
 
     def ts(o, a, s1, f1, s2=None, f2=None):
         if f2 is None:
@@ -99,14 +238,17 @@ def rank_program(g, core, T, topo):
     def ms(o, v):
         op("V", lambda: g.vector.memset(o[0], v), o, [])
 
-    def scan(o, a, b, init):
-        op("V", lambda: g.vector.tensor_tensor_scan(o[0], a[0], b[0], init, ALU.mult, ALU.add), o, [a, b])
+    def scan(o, a, b, init, f0=ALU.mult, f1=ALU.add):
+        op("V", lambda: g.vector.tensor_tensor_scan(o[0], a[0], b[0], init, f0, f1), o, [a, b])
 
     def red(o, a):
         op("V", lambda: g.vector.tensor_reduce(o[0], a[0], AX.X, ALU.add), o, [a])
 
-    def act(o, i, f=AF.Identity, bias=0.0, scale=1.0):
-        op("S", lambda: g.scalar.activation(o[0], i[0], f, bias=ap(bias), scale=ap(scale)), o, [i, bias, scale])
+    def act(o, i, f=AF.Identity, bias=0.0, scale=1.0, acc=None):
+        if acc is None:
+            op("S", lambda: g.scalar.activation(o[0], i[0], f, bias=ap(bias), scale=ap(scale)), o, [i, bias, scale])
+        else:
+            op("S", lambda: g.scalar.activation(o[0], i[0], f, bias=ap(bias), scale=ap(scale), accum_out=acc[0]), o, [i, bias, scale], more=acc[1])
 
     def gat(q, o, i):
         if q == "V":
@@ -114,14 +256,25 @@ def rank_program(g, core, T, topo):
         else:
             act(o, i, AF.Copy)
 
-    def mm(o, w, r, a, b):
+    def mm(o, w, r, a, b, join=None):
         op("P", lambda: g.tensor.matmul(o[0], w[0], r[0], a, b), o, [w, r])
+        new, key = ops[-1], (o[1][0][0], join or r[1][0][0])
+        new["key"] = key
+        if len(ops) > 1 and ops[-2].get("key") == key and ops[-2]["t"] < 0.8:
+            ops.pop()
+            for f_ in ("fn", "w", "r"):
+                ops[-1][f_] += [x for x in new[f_] if x not in ops[-1][f_]]
+            ops[-1]["t"] += new["t"]
 
-    def iota(o, pat, base, cm):
+    def iota(o, pat, base, cm=0):
         if SCRATCH[o[1][0][0]][2] == I32:
             op("G", lambda: g.iota(o[0], pat, base, cm), o, [])
         else:
             op("G", lambda: g.iota(o[0], pat, base, cm, allow_small_or_imprecise_dtypes=True), o, [])
+
+    def gcp(o, i):
+        w = o[1][0][2] - o[1][0][1]
+        op("G", lambda: g.affine_select(o[0], i[0], [[0, w]], ALU.is_ge, 0.0, 1, 0), o, [i])
 
     def dma(o, i, q="Y"):
         op(q, lambda: Q[q].dma_start(o[0], i[0]), o, [i], "d")
@@ -131,570 +284,816 @@ def rank_program(g, core, T, topo):
 
     def send(o, i, k):
         op("G", lambda: g.remote_dma(o[0], i[0], T.sem["ar%d" % k], T.sem.sent, pid, rid, emask), None, [i], "s")
-
-    def arrive(o, k):
-        ops.append({"q": None, "fn": None, "w": list(o[1]), "r": [], "k": "a", "sem": "ar%d" % k})
+        ops.append({"q": None, "fn": None, "w": list(o[1]), "r": [], "k": "a", "sem": "ar%d" % k, "t": HOP_TIME})
 
     def Z(v, r):
         return A("ZZ", 144 * v + 15 - r, 144 * v + 143 - r)
 
     def ZV(v):
         return A("ZZ", 144 * v, 144 * v + 144)
-    Z1, Z4K, ZPOW, Z01, Z2, Z34, Z23, Z456, ZSL = range(9)
-    BK, BK34, IDN, NID = (A("BB", 128 * i, 128 * i + 128) for i in range(4))
+    Z1, Z4K, ZPOW, Z01, Z2, Z345, ZMK, ZSM, ZSL = range(9)
+    BK, BKX, BK345, IDN, NID, I64, IHB = (A("BB", 128 * i, 128 * i + 128) for i in range(7))
+    IDM, NIM, IH, W10, W11, W20, W21 = (A("FM", 128 * i, 128 * i + 128) for i in range(7))
+    KSB, KQ, KNEG, K20 = (A("KB", 256 * i, 256 * i + 256) for i in range(4))
 
-    def deal(o, v, buf, lo, hi, first=True):
+    def deal(o, v, buf, lo, hi, first=True, last=True):
         for r in range(16):
-            mm(o, Z(v, r), A(buf, lo + r, hi, 16), first and r == 0, r == 15)
+            mm(o, Z(v, r), A(buf, lo + r, hi, 16), first and r == 0, last and r == 15)
 
-    RC, T1P, THW, T2K, CAPM, CBB, ACC, WP, MA, MB, C01, C23, C34, C456, K1, X0, X1, X2, X3, NMA, NMB, XA, X4, X5, X6 = (C("CO", i) for i in range(25))
-    AIX, ALT, CAPC, IDXC = (A("LC", 16 * i, 16 * i + 12) for i in range(4))
+    (RC, T1P, THW, T2K, CBB, ACC, WP, WS, WR, THR, C01, C345, CMK, CSM, FBI, K1, RC256, RC16, G0, G1, P2R,
+     X0, X1, X2, X3, X4, X5, X6) = (C("CO", i) for i in range(28))
+    AIX, ALT, CAP = (A("LC", 16 * i, 16 * i + 12) for i in range(3))
+    UJ, UPERM = A("UL", 0, 12), A("UL", 12, 24)
     add, sub, mul, mx, mn = ALU.add, ALU.subtract, ALU.mult, ALU.max, ALU.min
-    band, shr = ALU.bitwise_and, ALU.arith_shift_right
+    band, shr, eq_ = ALU.bitwise_and, ALU.arith_shift_right, ALU.is_equal
+
+    def D(i):
+        return C("DG", i)
+
+    def turn(src, bank):
+        op("V", lambda: g.vector.transpose(T.TR[:], src[0]), X("TR", ALL, ALL), [src])
+        for jp, (w1, w2) in enumerate(((W10, W20), (W11, W21))):
+            o = X(bank, slice(jp, 12, 2), ALL, 0, L)
+            mm(o, w1, X("TR", slice(jp, 12, 2), ALL), True, False)
+            mm(o, w2, X("TR", slice(1 - jp, 12, 2), ALL), False, True)
 
     ms(A("TH"), 0)
     dma(A("REP"), H(T.rep[:])); dma(A("FCT"), H(T.fact[:]))
     dma(A("ZL", 0, L), H(T.z[:])); dma(A("TH", 0, 2, p=0), H(T.thr[:]))
-    dma(A("MI"), H(T.memb[:]))
-    iota(A("IT"), [[1, L]], 128, -1)
-    iota(A("CA"), [[1, 256]], 0, 256)
     iota(C("AI", 0), [[0, 1]], 0, 1)
-    iota(A("I2"), [[1, L]], 0, 0)
-    iota(A("COL", 0, 2048), [[1, 128], [256, 16]], 0, 0)
-    iota(A("IO", 0, 1076), [[1, 1076]], 0, 0)
-    ms(A("P", 0, 1024), 0.0)
-    act(A("P", 1024, 2048), A("P", 0, 1024), AF.Copy)
-    act(A("P", 2048, W), A("P", 0, 2048), AF.Copy)
-    ms(A("HF"), 0.5); ms(A("ZE"), 0.0); ms(A("XX", W, SB), -256.0)
-    ms(A("HN", 0, 144), -0.5); ms(A("HN", 144, L), 0.0); ms(A("NEG"), -1.0)
-    ms(A("CM", 0, 16), 2.0); ms(ACC, 0.0); ms(A("WF"), 0.0)
-    scan(A("LS"), A("HF"), A("ZE"), 2.0 ** 96)
-    scan(A("CM", 16, 32), A("CM", 0, 16), A("ZE", 0, 16), 0.5)
+    iota(A("IT"), [[1, L]], 128, -1)
+    iota(A("DA", 768, 1024), [[256, 256]], 0)
+    iota(A("I2"), [[1, 16]], 0)
+    ms(A("P", 0, 2304), 0.0)
+    act(A("P", 2304, SB), A("P", 0, 2048), AF.Copy)
     ts(C("AI", 1), C("AI", 0), 15, band)
-    ts(A("P1"), A("IT"), 15, band)
-    ts(A("CA"), A("CA"), W - 1, band)
-    cp(RC, C("AI", 1))
-    ts(A("DG"), A("P1"), 0.0, ALU.is_equal)
-    ts(A("FH", L, 2 * L), A("FCT"), M6, add, M6, sub)
+    ts(C("AI", 2), C("AI", 0), 4, shr, 1, band)
+    ts(A("SI", 0, 16), A("IT", 0, 16), 15, band)
+    cp(RC, C("AI", 1)); cp(G1, C("AI", 2))
+    ts(A("DG"), A("SI", 0, 16), 0.0, eq_)
+    ts(RC256, RC, 256.0, mul)
+    ts(G0, G1, -1.0, mul, 1.0, add)
+    ts(A("ZB"), A("IT", 0, 144), RC, add, 143.0, eq_)
+    ts(A("DA", 1024, 1280), A("DA", 768, 1024), 0.0, mul, RC256, add)
+    for w_, d_, m_ in ((W10, 128.0, G0), (W20, 144.0, G0), (W11, 128.0, G1), (W21, 112.0, G1)):
+        ts(w_, A("IT", 0, 128), d_, eq_, m_, mul)
     ts(A("DA", 256, 512), A("REP"), M6, add, M6, sub)
-    tt(A("FH", 0, L), A("FCT"), A("FH", L, 2 * L), sub)
-    ts(A("DA", 1024, 1280), A("CA"), M6, add, M6, sub)
+    cp(A("FF"), A("FCT"))
     tt(A("DA", 0, 256), A("REP"), A("DA", 256, 512), sub)
-    ts(A("ZB"), A("IT", 0, 144), RC, add, 143.0, ALU.is_equal)
-    tt(A("DA", 768, 1024), A("CA"), A("DA", 1024, 1280), sub)
-    for row in (1, 0, 4, 3):
-        dma(A("P", p=row), A("DA", 256 * row, 256 * row + 256))
+    for row in (1, 0):
+        dma(A("P", 0, W, p=row), A("DA", 256 * row, 256 * row + 256))
     dma(A("XX", SB, SB + W), H(T.feat[:]))
-    cp(ZV(Z1), A("ZB"))
-    red(C01, A("DG", 0, 2))
-    for k in range(16):
-        act(A("G1B", L * k, L * k + L), A("FH", L, 2 * L), scale=C("DG", k))
-        ts(A("AB", L * k, L * k + L), A("FH", 0, L), C("DG", k), mul)
-    act(A("COL", 2048, W), A("COL", 0, 2048), bias=128.0)
-    OP, O37 = A("B1", L, 2 * L), A("B0", L, 2 * L)
-    for r in range(16):
-        mm(OP, Z(Z1, r), A("G1B", r, 3072, 16), r == 0, False)
-    deal(OP, Z1, "AB", 0, 3072, first=False)
-    ts(ZV(Z01), A("ZB"), C01, mul)
-    cp(A("LA"), A("REP"))
-    ts(A("TT", 0, 128), A("IT", 0, 128), RC, add, 128.0, ALU.is_ge)
-    ts(A("TD", 0, 128), A("IT", 0, 128), RC, add, 143.0, ALU.is_le)
+    dma(A("MI"), H(T.memb[:]))
+    for row in (3, 4):
+        dma(A("P", 0, W, p=row), A("DA", 256 * row, 256 * row + 256), "S")
+    turn(A("FF"), "B1")
+    ts(C01, D(0), D(1), add)
+    ts(IDM, A("IT", 0, 128), 128.0, eq_)
+    act(ZV(Z01), A("ZB"), scale=C01)
+    act(ZV(Z4K), A("ZB"), scale=4096.0)
+    act(ZV(Z1), A("ZB"), AF.Copy)
+    cp(A("OL", 0, L), A("B1", 0, L))
+    act(A("OF"), A("B1", 0, L), AF.Copy)
+    act(IDN, IDM, AF.Copy); act(NID, IDM, scale=-1.0); act(NIM, IDM, scale=-1.0)
+    iota(A("KC"), [[0, 12], [-256, 16]], 3840)
+    iota(A("RS"), [[0, L]], 1)
+    iota(A("RB"), [[0, L]], 0)
+    for b_, fill in (("RS", 0.0), ("RB", 2.0 ** 30)):
+        op("G", lambda b_=b_, fill=fill: g.affine_select(T[b_][:], T[b_][:], [[0, 12], [1, 16]], ALU.is_gt, fill, 0, 0), A(b_), [A(b_)])
+    gcp(A("LA"), A("REP"))
+    iota(A("KN", 0, L), [[0, 12], [-32, 16]], 0)
+    iota(A("KN", L, 2 * L), [[0, 12], [-5, 16]], 0)
+    iota(A("EC", 0, L), [[16, L]], 0)
+    for c in range(4):
+        iota(A("COL", 1024 * c, 1024 * c + 1024), [[1, 64], [256, 16]], 64 * c)
+    ts(AIX, A("I2", 0, 12), 16.0, mul, RC, add)
+    cp(UJ, A("I2", 0, 12))
+    ts(A("SI", 16, 28), AIX, -5.5, add, 1.0 / 12, mul)
+    ts(A("SF", 0, 12), AIX, 16.0, mul)
+    ts(A("SF", 16, 28), A("SI", 16, 28), -191.0, mul)
     cp(A("THF"), A("TH"))
-    red(C34, A("DG", 3, 5))
-    tt(A("BF"), A("TT", 0, 128), A("TD", 0, 128), mul)
-    ts(A("IDM"), A("IT", 0, 128), 128.0, ALU.is_equal)
+    tt(A("SF", 32, 44), A("SF", 0, 12), A("SF", 16, 28), add)
+    ts(A("TA"), A("IT", 0, 128), RC, add, 128.0, ALU.is_ge)
+    cp(UPERM, A("SF", 32, 44))
+    ts(A("TB"), A("IT", 0, 128), RC, add, 143.0, ALU.is_le)
+    ms(A("XX", W, SB), -256.0)
+    tt(A("BF"), A("TA"), A("TB"), mul)
     mm(A("B2", 0, 2), A("BF"), A("THF", 0, 2), True, True)
-    ts(A("V1"), A("I2"), 15, band)
-    cp(IDN, A("IDM"))
-    tt(A("TT"), A("LS"), A("DG"), mul)
-    ts(A("RS"), A("V1"), 0.0, ALU.is_gt)
-    ts(NID, A("IDM"), -1.0, mul)
-    scan(A("WS"), A("RS"), A("TT"), 0.0)
-    ts(ZV(Z4K), A("ZB"), 4096.0, mul)
-    ts(ZV(ZSL), A("ZB"), C("WS", 95), mul)
-    cp(A("OL", 0, L), OP)
-    act(A("OF"), OP, AF.Copy)
+    ms(A("D2", 0, 48, 2), 0.0)
 
-    def g1(v, q, k0, k1, lst="OL"):
-        gat(q, A("G1B", L * k0, L * k1), IN(A("P"), A(lst, L * v + 12 * k0, L * v + 12 * k1)))
+    def g1(v, q, c0, c1):
+        gat(q, A("G1B", 16 * c0, 16 * c1), IN(A("P", 0, W), A("OL", L * v + c0, L * v + c1)))
 
-    def g1pe(bank, off, kind, k0, k1):
-        deal(A(bank, off + 12 * k0, off + 12 * k1), kind, "G1B", L * k0, L * k1)
+    def g1pe(bank, kind, c0, c1):
+        deal(A(bank, c0, c1), kind, "G1B", 16 * c0, 16 * c1)
 
-    for k0, k1 in ((0, 6), (6, 12), (12, 16)):
-        g1(0, "S", k0, k1)
-    iota(A("MC", W, SB), [[0, SB - W]], -1, 0)
-    iota(A("KC"), [[-256, 16], [0, 12]], 3840, 0)
-    iota(A("C37"), [[37, 16], [0, 12]], 0, 0)
-    iota(A("KN", 0, L), [[-32, 16], [0, 12]], 0, 0)
-    iota(A("KN", L, 2 * L), [[-5, 16], [0, 12]], 0, 0)
-    iota(A("EC"), [[1024, 3], [1, 16], [256, 4]], 0, 0)
-    o_, i_ = A("MC", 0, W), A("MI")
-    op("G", lambda: g.affine_select(o_[0], i_[0], [[0, W]], ALU.is_ge, 0.0, 1, 0), o_, [i_])
-    iota(A("F"), [[0, PAD]], 0, 0)
+    def usum(v):
+        deal(A("B7", 0, 12), Z1, "ZL", L * v, L * v + L)
+
+    for q, c0, c1 in (("V", 0, 64), ("S", 96, 160), ("V", 64, 96), ("S", 160, 192)):
+        g1(0, q, c0, c1)
+        g1pe("B0", Z01, c0, c1)
+    ms(A("D2", 1, 24, 2), 64.0); ms(A("D2", 25, 48, 2), -1.0)
+    ts(X0, RC, 240.0, add)
+    red(X1, A("DG", 4, 6))
+    ts(A("T2", 25, 48, 2), A("I2", 0, 12), 256.0, mul, X0, add)
+    ts(C345, D(3), 1.0 / 256, mul, X1, add)
+    act(BK, A("BF"), AF.Copy); act(BKX, A("BF"), scale=2.0 ** 17)
+    act(A("EC", L, 2 * L), A("EC", 0, L), bias=RC, scale=0.0)
+    act(BK345, A("BF"), scale=C345)
+    cp(A("ID"), A("B0", 0, L))
     dma(A("XX", SB + W, SB + 2 * W), H(T.feat[:]))
     dma(A("XX", 0, W), H(T.feat[:]))
-    act(A("IO", 1076, 2152), A("IO", 0, 1076), bias=1076.0)
-    for j, c in enumerate((3, 0, 1, 2)):
-        tt(A("FL", 1024 * c, 1024 * c + 1024), IN(A("MI"), A("LA", 64 * c, 64 * c + 64)), A("COL", 1024 * c, 1024 * c + 1024), ALU.is_equal)
-        deal(A("B3", 64 * c, 64 * c + 64), ZSL, "FL", 1024 * c, 1024 * c + 1024)
-        if j < 3:
-            g1pe("B0", 0, Z01, (0, 6, 12)[j], (6, 12, 16)[j])
-    cp(A("IL"), A("B0", 0, L))
-    act(A("ZL", L, 2 * L), A("ZL", 0, L), AF.Copy)
+
+    def step1_constants():
+        ts(T1P, C("B2", 0), 1.0, add)
+        ts(THW, C("B2", 0), 1.0, add, 4096.0, mul)
+        ts(CBB, C("B2", 0), -64.0 * 4096, mul, -64.0 * 4000, add)
+        ts(T2K, C("B2", 1), 4096.0, mul, 4095.0, add)
+
+    def powers():
+        ms(A("CM", 0, 16), 2.0); ms(A("CM", 16, 32), 0.5); ms(A("CM", 32, 48), 0.0)
+        scan(A("CM", 48, 64), A("CM", 16, 32), A("CM", 32, 48), 2.0 ** 16)
+        scan(A("CM", 16, 32), A("CM", 0, 16), A("CM", 32, 48), 0.5)
+        tt(A("CM", 48, 64), A("CM", 48, 64), A("DG"), mul)
+        tt(A("CM", 16, 32), A("CM", 16, 32), A("DG"), mul)
+        red(WS, A("CM", 48, 64)); red(P2R, A("CM", 16, 32))
+        act(ZV(ZSL), A("ZB"), scale=WS)
+        ts(WR, WS, 2.0 ** -15, mul); ts(THR, WS, 40.0 * 2.0 ** -15, mul)
+        ts(X2, D(15), -1.0, mul, 0.5, add)
+        ts(X3, T2K, -1023.0, add)
+        ts(WP, P2R, X2, mul)
+        ts(ALT, AIX, 4096.0, add); ts(CAP, AIX, X3, add)
+        ms(KQ, -0.25); ms(KSB, float(SB))
+        act(IH, IDM, scale=0.5); act(IHB, IDM, scale=0.5)
+
+    def slots(c0, c1):
+        for c in range(c0, c1):
+            tt(A("FL", 1024 * c, 1024 * c + 1024), IN(A("MI"), A("LA", 64 * c, 64 * c + 64)), A("COL", 1024 * c, 1024 * c + 1024), eq_)
+            deal(A("B3", 64 * c, 64 * c + 64), ZSL, "FL", 1024 * c, 1024 * c + 1024)
 
     def slot_row():
-        act(A("PWA"), A("B3", 0, 256), AF.Copy)
         act(A("DA", 512, 768), A("B3", 0, 256), AF.Copy)
-        dma(A("P", p=2), A("DA", 512, 768))
-
-    def o37():
-        mm(O37, A("IDM"), A("OF"), True, False)
-        mm(O37, A("IDM"), A("C37"), False, True)
-
-    def usum(zo):
-        for r in range(16):
-            mm(A("B7", 0, 12), Z(Z1, r), A("ZL", zo + r, zo + L, 16), r == 0, r == 15)
-
-    def yc_start(i0, i1):
-        for i in range(i0, i1):
-            mm(A("B3", 0, 256), A("ZK", 15 - i, 143 - i), A("MC", 256 * i, 256 * i + 256), i == 0, i == 15)
-    usum(0)
-
-    def late_constants():
-        ts(K1, RC, 1.0, add)
-        cp(A("ID"), A("B0", 0, L))
-        ts(A("ZK"), A("ZB"), K1, mul)
-        ts(AIX, A("I2", 0, L, 16), RC, add)
-        ts(T1P, C("B2", 0), 1.0, add)
-        ts(A("SI", 0, 12), AIX, -5.5, add, 1.0 / 12, mul)
-        ts(THW, C("B2", 0), 1.0, add, 4096.0, mul)
-        ts(A("SF", 0, 12), A("SI", 0, 12), -12.0, mul)
-        ts(CBB, C("B2", 0), -64.0 * 4096, mul, -64.0 * 3968, add)
-        tt(A("SF", 16, 28), A("SF", 0, 12), AIX, add)
-        ts(T2K, C("B2", 1), 4096.0, mul)
-        cp(A("UL"), A("SF", 16, 28))
-        ts(CAPM, C("B2", 1), 1.0, add, 4096.0, mul)
-        ts(IDXC, AIX, 2880.0, add)
-        ts(BK34, A("BF"), C34, mul)
-        act(A("IO", 2152, 3228), A("IO", 0, 1076), bias=2152.0)
-
-    def step3_constants():
-        cp(BK, A("BF"))
-        ts(A("TD"), A("DG"), -9e29, mul, 9e29, add)
-        ts(A("LO"), A("TT"), 2.5, mul)
-        ts(X0, RC, 16.0, mul)
-        tt(A("TD"), A("TD"), A("LO"), add)
-        ts(A("EC"), A("EC"), X0, add)
-        ts(ALT, AIX, 4096.0, add)
-        ts(CAPC, AIX, -1024.0, add)
-        ts(ZV(Z34), A("ZB"), C34, mul)
-        ts(ZV(Z2), A("ZB"), C("DG", 2), mul)
+        dma(A("P", 0, W, p=2), A("DA", 512, 768))
+        act(A("PWA"), A("B3", 0, 256), AF.Copy)
 
     def f_constants():
-        ts(X1, C("DG", 15), -2.0, mul, 1.0, add)
-        tt(A("CM", 32, 48), A("CM", 16, 32), A("DG", 0, 16), mul)
-        red(X3, A("DG", 1, 6, 2))
-        red(X2, A("CM", 32, 48))
-        ts(X4, C("DG", 6), M16, mul)
-        tt(WP, X2, X1, mul)
-        ts(MA, X3, M8, mul, X4, add)
-        ts(ZV(ZPOW), A("ZB"), WP, mul, 0.5, mul)
-
-    def f_weights():
-        for m, rows, wcol in ((0, (0, 1), WP), (1, (2, 3), 1.0), (2, (4, 5, 6), K1)):
-            for r in rows:
-                ts(A("WF", 128 * m + r, 128 * m + 128, 16), A("BF", r, 128, 16), wcol, mul)
-
-    def f_late():
-        red(X5, A("DG", 0, 5, 2))
-        ts(X6, C("DG", 5), M16, mul)
-        ts(NMA, MA, -1.0, mul)
-        ts(X2, X5, C("DG", 5), add, -1.0, add)
-        ts(X3, X5, M8, mul, X6, add)
-        iota(A("IO", SB, 2 * SB), [[1, SB]], SB, 0)
-        ts(MB, X2, -MZ, mul, X3, add)
-        ts(A("NIM"), A("IDM"), -1.0, mul)
-        ts(NMB, MB, -1.0, mul)
+        act(ZV(ZPOW), A("ZB"), scale=WP); act(ZV(Z2), A("ZB"), scale=D(2))
+        ms(A("WF"), 0.0)
+        ms(A("HN", 0, GS), -0.5); ms(A("HN", GS, L), 0.0)
+        ts(K1, RC, 1.0, add)
+        act(A("ZK"), A("ZB"), scale=K1)
+        ts(X4, D(9), 2.0 ** 28, mul)
+        for m, col, rows in ((0, P2R, ((7, -1.0 / 32), (8, -1.0 / 8192))), (1, 1.0, ((3, 256.0), (4, 1.0))),
+                             (2, K1, ((9, -256.0), (10, -1.0), (11, -1.0 / 256)))):
+            for r, w_ in rows:
+                ts(A("WF", 128 * m + r, 128 * m + 128, 16), A("BF", r, 128, 16), col, mul, w_, mul)
+        ts(X5, D(10), 2.0 ** 20, mul, X4, add)
+        ts(A("CF"), A("DA", 768, 1024), 1.0 / 256, mul, RC256, add)
+        ts(FBI, D(11), 4096.0 - 255.0 / 512, mul, X5, add)
 
     def end_constants():
-        red(C23, A("DG", 2, 4))
-        red(C456, A("DG", 4, 7))
-        ts(ZV(Z23), A("ZB"), C23, mul)
-        ts(ZV(Z456), A("ZB"), C456, mul)
+        ts(CMK, D(7), -1.0 / 256, mul, D(8), sub)
+        ts(X6, D(9), -1.0 / 256, mul, D(10), sub)
+        ms(KNEG, -1.0); ms(K20, 2.0 ** 20)
+        ts(CSM, D(11), -256.0, mul, X6, add)
+        act(ZV(ZMK), A("ZB"), scale=CMK); act(ZV(Z345), A("ZB"), scale=C345); act(ZV(ZSM), A("ZB"), scale=CSM)
+        act(A("C1"), A("CF"), bias=1.0)
 
-    def yc_digits():
-        ts(A("DY", 512, 768), A("YA"), M16, add, M16, sub)
-        ts(A("YT"), A("YA"), M8, add, M8, sub)
-        tt(A("DY", 0, 256), A("YA"), A("YT"), sub)
-        tt(A("DY", 256, 512), A("YT"), A("DY", 512, 768), sub)
-        dma(A("F", 0, W, p=0), A("NEG"))
-        for row in (2, 3):
-            dma(A("F", 0, W, p=row), A("DA", 256 * (row + 1), 256 * (row + 2)))
-        for r in range(3):
-            dma(A("F", 0, W, p=4 + r), A("DY", 256 * r, 256 * r + 256))
+    def yc_sums(v, n0, n1):
+        steps = [[], [0, 1, 2, 3, 4, 5], [6, 7, 8, 9, 10, None], [11, 12, 13, 14, 15, None]][v]
+        for n_ in range(n0, min(n1, len(steps))):
+            i = steps[n_]
+            if i is None:
+                mm(A("B2", 256, 512), IDM, A("YT"), False, True)
+            else:
+                mm(A("B2", 256, 512), A("ZK", 15 - i, 143 - i), A("MF", 256 * i, 256 * i + 256), n_ == 0, i == 5, "yc%d" % i)
+        if n1 == 6 and v:
+            act(A("YT"), A("B2", 256, 512), bias=136.0 if v == 1 else 0.0)
 
-    KH = A("KY", 744, 768, 2)
-    TGS = (A("SU", 48, 60), A("SU", 80, 92))
-    FP = A("B3", 0, L)
+    def yc_finish():
+        act(A("DA", 0, 256), A("YT"), AF.Relu, bias=2.0 ** 21, scale=-2.0 ** 21)
+        o = A("B3", 256, 512)
+        mm(o, IDM, A("YT"), True, False); mm(o, NIM, A("C1"), False, False); mm(o, IDN, A("DA", 0, 256), False, True)
+        act(A("YT"), o, AF.Copy)
 
-    def f_values():
-        tt(A("CBV"), IN(A("DG", 0, 16), A("SU", 64, 76)), A("M"), mul)
+    TG, IDX, SLOT = A("SU", 32, 44), A("SU", 48, 60), A("SU", 60, 72)
+    KA, KBK, OWN, O37 = A("B4", 0, L), A("B5", 0, L), A("B1", L, 2 * L), A("B0", L, 2 * L)
+    FP, ZP = A("B1", 0, L), A("B2", L, 2 * L)
+
+    def f_scatter():
+        ts(A("FI"), FP, FBI, add)
+        ts(A("FG"), A("FI"), 0xFF00, band)
+        cp(IN(A("F"), TG), A("FG"))
+
+    def EQ(q, lo=0):
+        o = L * q - 8 * q * (q - 1)
+        return A("EQ", o + lo, o + L - 16 * q)
 
     def f_pe():
-        mm(FP, A("WF", 0, 128), A("KP"), True, False)
-        mm(FP, A("WF", 256, 384), A("KM"), False, False)
-        mm(FP, A("WF", 128, 256), A("CBV"), False, True)
+        mm(FP, A("WF", 0, 128), A("NK"), True, False)
+        mm(FP, A("WF", 128, 256), A("CBV"), False, False)
+        mm(FP, A("WF", 256, 384), A("KM"), False, True)
 
-    def EQ(q):
-        o = L * q - 8 * q * (q - 1)
-        return A("EQ", o, o + L - 16 * q)
+    def f_put(tg):
+        ts(A("FG"), A("FI"), 0xFF00, band)
+        cp(IN(A("F"), tg), A("FG"))
 
+    def facts_out():
+        turn(A("FF"), "B3")
+        act(A("YO"), A("B3", 0, L), AF.Copy)
+        dma(H(T.yo[:]), A("YO"))
+
+    def late_loads():
+        dma(A("F"), A("P", 0, PAD))
+        dma(A("P", SB, SB + W), A("P", 0, W))
+        dma(A("P", SB, SB + W, p=5), KSB)
+
+    keep[0] = True
     for v in range(VI):
         last = v == VI - 1
-        zo = 2 * L * v
-        TG, TGOLD = TGS[v % 2], TGS[1 - v % 2]
-        z, zz = A("ZL", zo, zo + L), A("ZL", zo, zo + 2 * L)
+        TG, TGOLD = (A("SU", 32 + 48 * (u % 2), 44 + 48 * (u % 2)) for u in (v, v + 1))
+        z = A("ZL", L * v, L * v + L)
         xw = A("XX", SB, SB + W) if v == 0 else A("XX", 0, SB + W)
-        act(A("XR"), IN(xw, A("IL", 156, 192)), AF.Copy)
-        if v == 0:
-            slot_row()
-        for j, o in enumerate((A("B5", 0, L), A("B5", L, 2 * L), A("B6", 0, L))):
-            mm(o, IDN, A("XR", L * j, L * j + L), True, False)
-            mm(o, NID, z, False, True)
-
-        def dpe(k0, k1):
-            mm(A("B4", 12 * k0, 12 * k1), IDN, A("KC", 12 * k0, 12 * k1), True, False)
-            deal(A("B4", 12 * k0, 12 * k1), Z4K, "AB", L * k0, L * k1, first=False)
-        for j, (k0, k1) in enumerate(((0, 1), (1, 3), (3, 5), (5, 7), (7, 9), (9, 11), (11, 13))):
-            tt(A("DB", L * k0, L * k1), IN(xw, A("IL", 12 * k0, 12 * k1)), z if j == 0 else zz, sub)
-            if j == 1:
-                act(A("AB", 13 * L, 15 * L), A("B5", 0, 2 * L), AF.Abs)
-                act(A("AB", 15 * L, 16 * L), A("B6", 0, L), AF.Abs)
-                act(A("UT", 0, 12), A("B7", 0, 12), AF.Copy)
-                dpe(13, 16)
-                o37()
-                act(A("AB", 0, 3 * L), A("DB", 0, 3 * L), AF.Abs)
-            elif j:
-                act(A("AB", L * k0, L * k1), A("DB", L * k0, L * k1), AF.Abs)
-            if j in (2, 4, 6):
-                dpe({2: 0, 4: 5, 6: 9}[j], k1)
-        if v == 0:
-            late_constants()
-            yc_start(0, 3)
-        ts(A("DH", 0, L), A("ID"), 7, shr)
-        tt(A("P1"), IN(A("UT", 0, 12), A("UL")), A("OF"), mul)
-        ts(A("DH", L, 2 * L), A("ID"), 127, band)
-        ts(A("P2"), A("P1"), 5, shr, W - 1, band)
-        if v:
-            act(A("FT"), FP, bias=MA); act(A("LO"), FP, bias=MB)
-            act(A("FA"), A("FT"), bias=NMA); act(A("FC"), A("LO"), bias=NMB)
-            mm(A("B3", L, 2 * L), A("IDM"), A("FA"), True, False); mm(A("B3", L, 2 * L), A("NIM"), A("FC"), False, True)
-        for h in (0, 1):
-            tt(A("B2", h, L, 2), A("B4", 96, L), A("DH", L * h + 96, L * h + L), add)
-            tt(A("KY", h, L, 2), A("B4", 0, 96), A("DH", L * h, L * h + 96), add)
-        act(A("CBS"), A("B4", 0, L), AF.Relu, bias=CBB, scale=64.0)
-        cb = A("B5", L, 2 * L)
-        mm(cb, IDN, A("KN", 0, L), True, False); mm(cb, IDN, A("KN", L, 2 * L), False, False); mm(cb, IDN, A("CBS"), False, True)
-        act(A("ZM"), z, bias=-0.5)
-        if v == 0:
-            yc_start(3, 7)
-            act(A("IO", 3228, SB), A("IO", 0, 1076), bias=3228.0)
-        else:
-            act(A("FG"), A("B3", L, 2 * L), AF.Copy)
-        tt(A("KY", 384, 576), A("B2", 0, L), A("KY", 0, L), mx)
-        tt(A("KY", 576, 672), A("KY", 384, 480), A("KY", 480, 576), mx)
-        tt(A("KY", 672, 720), A("KY", 576, 624), A("KY", 624, 672), mx)
-        tt(A("KY", 744, 768), A("KY", 672, 696), A("KY", 696, 720), mx)
-        ts(A("SI", 0, 24), A("KY", 744, 768), 255, band)
-        ts(A("SF", 0, 12), KH, THW, ALU.is_lt, 16384.0, mul)
-        ts(A("SI", 32, 44), KH, 8, shr, 15, band)
-        ts(A("SF", 16, 28), A("SI", 0, 24, 2), 128.0, mul)
-        tt(A("SF", 32, 44), A("SI", 1, 24, 2), A("SF", 0, 12), add)
-        ts(A("SF", 48, 60), A("SI", 32, 44), -192.0, mul)
-        tt(A("SF", 64, 76), A("SF", 16, 28), A("SF", 32, 44), add)
-        tt(A("SF", 80, 92), A("SF", 48, 60), IDXC, add)
-        ts(A("SU", 0, 12), A("SF", 64, 76), float(PAD if v == 0 else NONE), mn)
-        cp(A("SU", 16, 28), A("SF", 80, 92))
-        mw = A("MC", 0, SB) if v == 0 else A("MC")
-        ts(A("ML"), IN(mw, A("SU", 0, 12)), 16.0, add)
-        act(A("M"), IN(mw, A("SU", 0, 12)), AF.Copy)
-        act(A("OG"), IN(A("G1B"), A("SU", 16, 28)), AF.Copy)
-        mm(A("B6", 0, L), BK34, A("OG"), True, True)
-        act(A("B7", L, 2 * L), A("M"), bias=1.0)
-        if v == 0:
-            yc_start(7, 13)
-        if v < 2:
-            ms(C("IO", NONE if v else PAD), -1.0)
         xm = A("XX", PAD)
+        xo = [A("B6", 0, L), A("B6", L, 2 * L), A("B7", L, 2 * L), A("B5", 0, L), A("B5", L, 2 * L)]
+        IDL, KL = A("SU", 0, 12), A("SU", 12, 24)
+        cb, n2, lt = A("B5", L, 2 * L), A("B6", L, 2 * L), A("LT", 16 * v, 16 * v + 12)
+
+        def dv(k0, k1):
+            for k in range(k0, k1):
+                tt(X("DB", ALL, k, k, k + 1), IN(xw, A("IL", 12 * k, 12 * k + 12)), z, sub)
+
+        def dabs(k0, k1):
+            act(X("AB", ALL, slice(k0, k1), k0, k1), X("DB", ALL, slice(k0, k1), k0, k1), AF.Abs)
+
+        def dpe(k0, k1, end=False):
+            for r in range(16):
+                mm(X("B4", slice(0, 12), slice(k0, k1), 0, L), Z(Z4K, r), X("AB", slice(r, L, 16), slice(k0, k1), k0, k1), False, end and r == 15)
 
         def gm(c):
             act(A("AM", 1024 * c, 1024 * c + 1024), IN(xm, A("ML", 64 * c, 64 * c + 64)), AF.Copy)
-        gm(0)
-        act(A("ZN"), IN(A("AB"), A("SU", 16, 28)), AF.Copy)
-        gm(1)
-        tt(A("P4"), cb, A("P2"), mn)
-        tt(A("P5"), O37, A("P4"), add)
-        tt(A("S1"), A("B6", 0, L), A("M"), mul)
-        ts(A("P6"), A("P5"), W - 1, band)
-        ts(A("S2"), A("S1"), 5, shr, W - 1, band)
-        cp(A("OS", L * v, L * v + L), A("P6"))
-        if not last:
-            send(A("OL", L * (v + 1), L * (v + 2)), A("OS", L * v, L * v + L), v + 1)
-            arrive(A("OL", L * (v + 1), L * (v + 2)), v + 1)
-        tt(A("S3"), A("B7", L, 2 * L), A("S2"), add)
-        ts(A("SL"), A("S3"), 15.0, add)
-        n2 = A("B5", L, 2 * L)
-        mm(n2, IDN, A("ZN"), True, False); mm(n2, IDN, A("ZN"), False, False); mm(n2, NID, z, False, True)
-        if v == 0:
-            iota(A("MC", SB, 8416), [[0, 8416 - SB]], -1, 0)
 
         def gs(c):
             tt(A("YB", 1024 * c, 1024 * c + 1024), IN(xm, A("SL", 64 * c, 64 * c + 64)), A("AM", 1024 * c, 1024 * c + 1024), mn)
 
-        def psub(c, h):
-            bank = "B%d" % (2 * (c % 2) + h)
-            for k in range(8 * h, 8 * h + 8):
-                o = A(bank, 64 * (k % 8), 64 * (k % 8) + 64)
-                mm(o, IDN, A("YB", 1024 * c + k, 1024 * c + 1024, 16), True, False)
-                mm(o, NID, A("ZL", zo + 64 * c, zo + 64 * c + 64), False, True)
+        def pz(i):
+            for k in range(8):
+                mm(X("B%d" % (i % 3), slice(k, 32, 8), ALL), NID, A("ZL", L * v + 64 * (i // 2), L * v + 64 * (i // 2) + 64), k == 0, False)
 
-        def sabs(c, h):
-            act(A("EB", 1024 * c + 512 * h, 1024 * c + 512 * h + 512), A("B%d" % (2 * (c % 2) + h)), AF.Abs)
+        def py(i):
+            for k in range(8):
+                mm(X("B%d" % (i % 3), slice(k, 32, 8), ALL), IDN, A("YB", 1024 * (i // 2) + 8 * (i % 2) + k, 1024 * (i // 2) + 1024, 16), False, k == 7)
 
-        def e1(c, h):
-            for k in range(8 * h, 8 * h + 8):
-                mm(A("B4", 64 * c, 64 * c + 64), Z(Z4K, k), A("EB", 1024 * c + 64 * k, 1024 * c + 64 * k + 64), k == 0, k == 15)
+        def sabs(i):
+            act(X("EB", slice(4 * (i // 2), 4 * (i // 2) + 4), slice(128 * (i % 2), 128 * (i % 2) + 128), i, i + 1), A("B%d" % (i % 3), 0, 512), AF.Abs)
 
-        def e2(c):
-            deal(A("B5", 64 * c, 64 * c + 64), Z4K, "EB", 1024 * c, 1024 * c + 1024)
+        def e1(i):
+            c = i // 2
+            for k in range(8 * (i % 2), 8 * (i % 2) + 8):
+                mm(A("B4", 64 * c, 64 * c + 64), Z(Z4K, k), X("EB", slice(4 * c, 4 * c + 4), slice(16 * k, 16 * k + 16), i, i + 1),
+                   False, i == 5 and k == 15, "e%d" % i)
 
         def eq(q0, q1):
             for q in range(q0, q1):
-                ts(EQ(q), A("IDF", 16 * q, L), C("SF", 64 + q), ALU.is_equal, C("WS", 16 * q + 15), mul)
+                ts(EQ(q), A("B7", 16 * q, L), C("SC", 64 + q), eq_, WR, mul)
 
-        def eqpe(q0, q1):
-            for q in range(q0, q1):
-                mm(A("B6", 16 * q, L), BK, EQ(q), q == 0, q == 11)
+        def eqpe():
+            mm(A("B6", 0, L), BK, EQ(0), True, False)
+            for q in range(12):
+                if q:
+                    mm(A("B6", 16 * q, 16 * q + 16), BK, A("EQ", EQ(q)[1][0][1], EQ(q)[1][0][1] + 16), False, q == 11)
+                if q < 11:
+                    mm(A("B6", 16 * q + 16, L), BKX, EQ(q, 16), False, False)
 
-        gs(0); psub(0, 0); psub(0, 1)
-        if v == 0:
-            yc_start(13, 16)
-        gm(2)
-        gs(1)
-        act(A("IDF"), IN(A("IO", 0, SB) if v == 0 else A("IO"), A("SU", 0, 12)), AF.Copy)
-        if v == 0:
-            act(A("YA"), A("B3", 0, 256), bias=136.0)
-        sabs(0, 0); sabs(0, 1)
-        psub(1, 0); psub(1, 1)
-        act(A("AM", 3072, 3264), n2, AF.Copy)
-        gs(2)
-
-        def e12(c):
-            e1(c, 0); e1(c, 1)
-        ea, eb = (e2, e12) if last else (e12, e2)
-        ea(0)
-        sabs(1, 0); sabs(1, 1)
-        psub(2, 0); psub(2, 1)
-        eq(0, 12)
-        if v == 0:
-            step3_constants()
-        ea(1)
-        sabs(2, 0); sabs(2, 1)
-        eqpe(0, 12)
-        ea(2)
-        for c in range(3):
-            eb(c)
-        if v == 0:
-            cp(A("CF"), A("CA"))
-        if v == 1:
-            yc_digits()
-        if v == 2:
-            end_constants()
-        if not last:
-            g1(v + 1, "V", 0, 4)
-        else:
-            cp(IN(A("F"), TGOLD), A("FG"))
-        tt(A("LO"), A("B6", 0, L), A("TD"), ALU.is_ge)
-        scan(A("LS"), A("RS"), A("LO"), 0.0)
-        if not last:
-            ts(A("KP"), A("B4", 0, L), T2K, ALU.is_le)
-        ts(A("SF", 96, 108), A("LS", 15, L, 16), 16384.0, mul)
-        if not last:
-            tt(A("KM"), A("B7", L, 2 * L), A("KP"), mul)
-        tt(A("SF", 112, 124), A("SF", 96, 108), A("SF", 64, 76), add)
-        if not last:
-            tt(A("SF", 144, 156), A("SF", 112, 124), ALT, mn)
-            ts(A("SF", 128, 140), A("SF", 112, 124), 9000.0, ALU.is_lt, CAPM, mul)
-            cp(TG, A("SF", 144, 156))
-            tt(A("SF", 160, 172), A("SF", 128, 140), CAPC, add)
-            ts(IN(A("MC", 0, PAD), TG), A("KM"), 1.0, mul, -1.0, add)
-            g1(v + 1, "S", 4, 10)
-            g1pe("B0", 0, Z01, 0, 10)
-            g1(v + 1, "S", 10, 16)
-            g1pe("B0", 0, Z01, 10, 16)
-            cp(A("CL"), A("B0", 0, L))
-            g1pe("B1", 0, Z2, 0, 16); g1pe("B1", L, Z34, 0, 16)
-        else:
-            g1(v, "S", 0, 16, "OS")
-        tt(A3("E0"), A("B5", 0, L), A("EC"), add)
-        if last:
-            ts(A("SF", 128, 140), A("SF", 112, 124), 9000.0, ALU.is_lt, CAPM, mul)
-        tt(A3("E1"), A3("E0", 0, 32), A3("E0", 32, 64), mn)
-        if last:
-            tt(A("SF", 160, 172), A("SF", 128, 140), CAPC, add)
-        else:
-            ts(A("SF", 176, 188), A("SF", 112, 124), 9000.0, ALU.is_lt)
-        tt(A3("E2"), A3("E1", 0, 16), A3("E1", 16, 32), mn)
-        if last:
-            tt(A("SF", 144, 156), A("SF", 112, 124), ALT, mn)
-        else:
-            red(XA, A("SF", 176, 188))
-        tt(A3("E3"), A3("E2", 0, 8), A3("E2", 8, 16), mn)
-        if last:
-            cp(TG, A("SF", 144, 156))
-        tt(A3("E4"), A3("E3", 0, 4), A3("E3", 4, 8), mn)
-        if v == 0:
-            f_constants()
-        if last:
-            ts(A("KP"), A("B4", 0, L), T2K, ALU.is_le)
-        tt(A("SI", 48, 60), A3("E4"), A("SF", 160, 172), mn)
-        if last:
-            tt(A("KM"), A("B7", L, 2 * L), A("KP"), mul)
-            mm(FP, A("WF", 0, 128), A("KP"), True, False)
-            mm(FP, A("WF", 256, 384), A("KM"), False, False)
-        ts(A("SI", 80, 92), A("SI", 48, 60), 15, band)
-        ts(A("SI", 64, 76), A("SI", 48, 60), W - 1, band)
-        cp(A("SU", 64, 76), A("SI", 80, 92))
-        cp(A("SU", 32, 44), A("SI", 64, 76))
-        if last:
-            f_values()
-            mm(FP, A("WF", 128, 256), A("CBV"), False, True)
-        zs = A("ZS", L * v, L * v + L)
-        tt(A("Z1"), IN(A("AM"), A("SU", 32, 44)), A("ZM"), add)
-        if last:
-            ts(A("FA"), FP, MA, add, MA, sub)
-            ts(A("B4", L, 2 * L), FP, MB, add, MB, sub)
-            ts(zs, A("Z1"), M1, add, M1, sub)
-            tt(A("FG"), A("FA"), A("B4", L, 2 * L), sub)
-            act(A("YZ"), zs, scale=0.5)
-            dma(H(T.yz[:]), A("YZ"))
-            cp(IN(A("F"), TG), A("FG"))
-            break
-        f_values()
-        ts(zs, A("Z1"), M1, add, M1, sub)
-        send(A("ZR", L * v, L * v + L), zs, 5 + v)
-        if v == 0:
-            dma(A("MC", SB, SB + W, p=0), A("CF"))
-        for j in range(4):
-            o, i = A("G2B", 768 * j, 768 * j + 768), IN(A("MC", 0, PAD), A("CL", 48 * j, 48 * j + 48))
-            if j < 3:
+        def g2(q, c0, c1):
+            o, i = A("G2B", 16 * c0, 16 * c1), IN(A("MC", 0, PAD), A("CL", c0, c1))
+            if q == "S":
                 act(o, i, AF.Sign, bias=0.5)
-                if j == 1:
-                    act(A("XC"), IN(A("AM"), A("SU", 32, 44)), AF.Copy)
             else:
                 ts(o, i, 0.0, ALU.is_ge, 2.0, mul)
-                cp(IN(A("XX", 0, PAD), TG), A("XC"))
-                if v:
-                    cp(IN(A("F"), TGOLD), A("FG"))
-                else:
-                    f_weights(); f_late()
-            if j % 2:
-                mm(A("B2", 48 * (j - 1), 48 * (j + 1)), IDN, A("HN", 48 * (j - 1), 48 * (j + 1)), True, False)
-                deal(A("B2", 48 * (j - 1), 48 * (j + 1)), ZPOW, "G2B", 768 * (j - 1), 768 * (j + 1), first=False)
-            if j == 1:
-                mm(C("B6", 0), A("BF"), XA, True, True)
-        f_pe()
-        act(A("PW"), A("B1", 0, L), AF.Copy)
-        act(A("OF"), OP, AF.Copy)
-        act(A("B1", 0, L), A("OF"), bias=float(SB))
-        arrive(A("ZR", L * v, L * v + L), 5 + v)
-        act(A("ZL", zo + 2 * L, zo + 3 * L), A("ZR", L * v, L * v + L), scale=0.5)
-        act(A("ZL", zo + 3 * L, zo + 4 * L), A("ZR", L * v, L * v + L), scale=0.5)
-        usum(zo + 2 * L)
-        tt(ACC, C("B6", 0), ACC, add)
-        tt(A("V1"), A("B2", 0, L), A("PW"), mul)
-        cp(C("AI", 2), ACC)
-        ts(A("V2"), A("V1"), 32768, band)
-        ts(C("AI", 3), C("AI", 2), 127, band)
-        tt(A("V3"), A("B1", 0, L), A("V2"), sub)
-        ts(THW, C("AI", 3), T1P, add, 4096.0, mul)
-        tt(A("ID"), A("B0", 0, L), A("V3"), mx)
-        cp(A("IL"), A("ID"))
 
-    for k in range(16):
-        mm(A("B0", 0, L), Z(Z34, k), A("G1B", L * k, L * k + L), k == 0, k == 15)
-    act(A("YA"), A("CF"), bias=1.0)
-    act(A("B5", 0, 256), A("CF"), AF.Copy)
+        def g2pe(c0, c1):
+            mm(A("B2", c0, c1), IDN, A("HN", c0, c1), True, False)
+            deal(A("B2", c0, c1), ZPOW, "G2B", 16 * c0, 16 * c1, first=False)
+
+        cp(A("IL"), IN(A("ID"), UPERM))
+        act(A("XR"), IN(xw, A("IL", 0, 12 * KS)), AF.Copy)
+        mm(KA, IDN, A("KC", 0, L), True, False)
+        mm(O37, IDM, A("OF"), True, False); mm(O37, NID, A("KN", 0, L), False, False); mm(O37, NID, A("KN", L, 2 * L), False, True)
+        usum(v)
+        act(A("UT", 0, 12), A("B7", 0, 12), AF.Copy)
+        if v:
+            f_pe()
+        for j in range(KS):
+            mm(xo[j], IDN, A("XR", L * j, L * j + L), True, False)
+            mm(xo[j], NID, z, False, True)
+        yc_sums(v, 0, 1)
+        dv(KS, 7)
+        dabs(KS, 7)
+        for j in range(KS):
+            act(X("AB", ALL, j, j, j + 1), xo[j], AF.Abs)
+        dv(7, 11)
+        dpe(0, 7)
+        dabs(7, 11)
+        mm(cb, IDN, A("KN", 0, L), True, False); mm(cb, IDN, A("KN", L, 2 * L), False, False)
+        dv(11, 14)
+        dpe(7, 11)
+        dabs(11, 14)
+        dv(14, 16)
+        dabs(14, 16)
+        dpe(11, 16, True)
+        ts(A("HI"), A("ID"), 6, shr); ts(A("LO"), A("ID"), 63, band)
+        tt(A("P1"), IN(A("UT", 0, 12), UJ), A("OF"), mul)
+        if v:
+            ts(A("FI"), FP, FBI, add)
+        else:
+            loose(step1_constants)
+        ts(A("P2"), A("P1"), 5, shr, W - 1, band)
+        tt(A("KE"), KA, A("HI"), add)
+        tt(A("KS"), KA, A("LO"), add)
+        scan(X("KY", ALL, 0, 0, 1), A("RS"), A("KE"), 0.0, mul, mx)
+        scan(X("KY", ALL, 1, 1, 2), A("RS"), A("KS"), 0.0, mul, mx)
+        act(A("CBS"), A("KE"), AF.Relu, bias=CBB, scale=64.0)
+        yc_sums(v, 1, 2)
+        mm(cb, IDN, A("CBS"), False, True)
+        yc_sums(v, 2, 4)
+        top = X("KY", slice(15, L, 16), 0, 0, 1)
+        ts(A("T2", 24, 48, 2), top, 4, shr, 0xF0, band)
+        ts(A("T2", 0, 24), X("KY", slice(15, L, 16), ALL), 255, band)
+        ts(A("SC", 48, 60), top, THW, ALU.is_lt, 2.0 ** 24, mul)
+        scan(A("SC", 0, 48), A("D2"), A("T2"), 0.0)
+        cp(A("SU", 0, 24), A("SC", 1, 48, 2))
+        tt(A("SC", 64, 76), A("SC", 1, 24, 2), A("SC", 48, 60), add)
+        act(A("OG"), IN(A("G1B"), KL), AF.Copy)
+        if v == 0:
+            ts(A("ML"), IN(A("MI"), IDL), float(SB - PAD), add)
+            cp(A("M"), IN(A("MI"), IDL))
+        else:
+            act(A("M"), IN(A("MC"), IDL), AF.Copy)
+            ts(A("ML"), IN(A("MC"), IDL), float(SB - PAD), add)
+        tt(A("P4"), cb, A("P2"), mn)
+        mm(KA, IDN, A("EC", 0, L), True, False); mm(KA, IDN, A("EC", L, 2 * L), False, False)
+        mm(A("B6", L, 2 * L), BK345, A("OG"), True, True)
+        mm(A("B7", L, 2 * L), IDM, A("M"), True, True)
+        gm(0)
+        tt(A("P5"), O37, A("P4"), add)
+        tt(A("S1"), A("B6", L, 2 * L), A("M"), mul)
+        ts(A("P6"), A("P5"), W - 1, band)
+        ts(A("S2"), A("S1"), 5, shr, W - 1, band)
+        tt(A("S3"), A("B7", L, 2 * L), A("S2"), add)
+        ts(A("SL"), A("S3"), float(SB - PAD), add)
+        if v == 0:
+            gcp(A("MC", 0, 1024), A("MI", 0, 1024))
+        if not last:
+            gcp(A("OS", L * v, L * v + L), A("P6"))
+            send(A("OL", L * (v + 1), L * (v + 2)), A("OS", L * v, L * v + L), v + 1)
+        else:
+            gcp(A("FF"), A("P6"))
+        if v == 0:
+            for c in range(1, 4):
+                gcp(A("MC", 1024 * c, 1024 * c + 1024), A("MI", 1024 * c, 1024 * c + 1024))
+            iota(A("MC", W, SB), [[0, SB - W]], -1)
+        act(A("IG"), IN(A("P", 0, W) if v == 0 else A("P"), IDL), AF.Copy)
+        yc_sums(v, 4, 6)
+        pz(0)
+        mm(A("B7", 0, L), BK345, A("IG"), True, True)
+        pz(1); pz(2)
+        gm(1)
+        if v == 0:
+            gm(2)
+            loose(powers)
+            slots(0, 4)
+            slot_row()
+        gs(0); py(0); py(1)
+        sabs(0); sabs(1)
+        eq(0, 12)
+        pz(3); pz(4)
+        eqpe()
+        e1(0); e1(1)
+        gv, gw = (GV, GV) if v else (G0V, GA)
+        if v:
+            gm(2)
+        else:
+            g1(v + 1, "S", gv, gw)
+        act(A("WB"), A("B6", 0, L), AF.Copy)
+        gs(1)
+        py(2); py(3)
+        act(A("XO"), IN(xw, IDL), AF.Copy)
+        deal(A("B7", 0, 12), Z1, "WB", 0, L)
+        sabs(2); sabs(3)
+        mm(n2, IDN, A("XO"), True, False); mm(n2, NID, z, False, True)
+        act(A("ZN"), n2, AF.Abs, scale=2.0)
+        gs(2)
+        pz(5); py(4); py(5)
+        e1(2); e1(3)
+        sabs(4); sabs(5)
+        mm(n2, IDN, A("ZN"), True, False); mm(n2, NID, z, False, True)
+        e1(4); e1(5)
+        if v == 0:
+            loose(f_constants)
+            late_loads()
+        if v == 1:
+            loose(end_constants)
+        if not last:
+            gcp(A("OF"), A("OL", L * (v + 1), L * (v + 2)))
+            if v == 0:
+                iota(A("MC", SB, SB + W), [[0, W]], -1)
+                dma(A("MC", SB, SB + W, p=0), A("CF"))
+            g1(v + 1, "V", 0, gv // 2)
+            g1(v + 1, "S", gw, (gw + L) // 2)
+        else:
+            f_put(TGOLD)
+            loose(yc_finish)
+            loose(facts_out)
+        ts(A("SF", 0, 12), A("B7", 0, 12), THR, ALU.is_ge, 2.0 ** 24, mul)
+        if not last:
+            g1(v + 1, "V", gv // 2, gv)
+            g1(v + 1, "S", (gw + L) // 2, L)
+        act(A("AM", 3072, 3264), n2, AF.Copy)
+        tt(A("SF", 16, 28), A("SF", 0, 12), A("SC", 64, 76), add)
+        op("V", lambda: g.vector.transpose(T.KS[:], T.B4[:, 0:12, :]), A("KS"), [A("B4", 0, L)])
+        tt(A("SF", 32, 44), A("SF", 16, 28), ALT, mn)
+        scan(A("KE"), A("RB"), A("KS"), 0.0, mx, mn)
+        cp(TG, A("SF", 32, 44))
+        ts(A("NK"), A("B4", 0, L), T2K, ALU.is_gt, -8192.0, mul)
+        ts(lt, A("SF", 16, 28), 9000.0, ALU.is_ge, 2.0 ** 24, mul)
+        if last:
+            tt(A("XC"), A("B7", L, 2 * L), A("NK"), add)
+            act(A("KM"), A("XC"), AF.Relu, bias=1.0)
+        else:
+            g1pe("B3", Z01, 0, gw)
+            tt(IN(A("MC", 0, PAD), TG), A("M"), A("NK"), add)
+        for jp, (w1, w2) in enumerate(((W10, W20), (W11, W21))):
+            mm(A("B5", jp, 12, 2), w1, A("KE", 16 * jp + 15, L, 32), True, False)
+            mm(A("B5", jp, 12, 2), w2, A("KE", 31 - 16 * jp, L, 32), False, True)
+        if not last:
+            g1pe("B3", Z01, gw, L)
+            for u in range(v + 1):
+                mm(A("B6", 0, 12), BK, A("LT", 16 * u, 16 * u + 12), u == 0, u == v)
+            act(OWN, A("OF"), bias=float(SB))
+        else:
+            mm(FP, A("WF", 0, 128), A("NK"), True, False)
+            mm(FP, A("WF", 256, 384), A("KM"), False, False)
+        mm(ZP, IHB, z, True, False); mm(ZP, IDN, A("KB", 256, 256 + L), False, False)
+        tt(A("SF", 48, 60), A("B5", 0, 12), lt, add)
+        tt(A("SI", 0, 12), A("SF", 48, 60), CAP, mn)
+        ts(A("SI", 16, 28), A("SI", 0, 12), W - 1, band)
+        ts(A("SI", 28, 40), A("SI", 0, 12), 15, band)
+        cp(A("SU", 48, 72), A("SI", 16, 40))
+        if not last:
+            cp(A("CL"), A("B3", 0, L))
+        if last:
+            tt(A("CBV"), IN(A("DG"), SLOT), A("M"), mul)
+            act(A("XC"), IN(A("AM"), IDX), AF.Copy)
+            mm(FP, A("WF", 128, 256), A("CBV"), False, True)
+            mm(ZP, IH, A("XC"), False, True)
+            ts(A("FI"), FP, FBI, add)
+            f_put(TG)
+            ts(A("YZ"), ZP, M0, add, M0, sub)
+            dma(H(T.yz[:]), A("YZ"))
+            break
+        act(A("XC"), IN(A("AM"), IDX), AF.Copy)
+        g1pe("B0", Z2, 0, 64)
+        mm(ZP, IH, A("XC"), False, True)
+        g2("S", 0, GS // 2)
+        g2("V", GS, (GS + L) // 2)
+        zs = A("ZS", L * v, L * v + L)
+        ts(zs, ZP, M0, add, M0, sub)
+        send(A("ZL", L * (v + 1), L * (v + 2)), zs, 5 + v)
+        if v == 0:
+            for c in range(0, W, 512):
+                gcp(A("MF", c, c + 512), A("MI", c, c + 512))
+        g1pe("B0", Z2, 64, L)
+        g2("V", (GS + L) // 2, L)
+        g2("S", GS // 2, GS)
+        g2pe(0, GS // 2)
+        g2pe(GS, L)
+        g2pe(GS // 2, GS)
+        act(A("PW"), A("B0", 0, L), AF.Copy)
+        act(A("SF", 64, 76), A("B6", 0, 12), scale=-2.0 ** -24, bias=16.0 * (v + 1), acc=ACC)
+        act(A("KM"), IN(A("MC", 0, PAD), TG), AF.Relu, bias=1.0)
+        tt(A("CBV"), IN(A("DG"), SLOT), A("M"), mul)
+        cp(IN(A("XX", 0, PAD), TG), A("XC"))
+        if v:
+            f_put(TGOLD)
+        tt(A("V1"), A("B2", 0, L), A("PW"), mul)
+        cp(C("AI", 3), ACC)
+        ts(A("V2"), A("V1"), 32768, band)
+        ts(C("AI", 4), C("AI", 3), 127, band)
+        tt(A("V3"), OWN, A("V2"), sub)
+        ts(THW, C("AI", 4), T1P, add, 4096.0, mul)
+        tt(A("ID"), A("B3", 0, L), A("V3"), mx)
+
+    for v in ():
+        last = v == VI - 1
+        z = A("ZL", L * v, L * v + L)
+        xw = A("XX", SB, SB + W) if v == 0 else A("XX", 0, SB + W)
+        cp(A("IL"), IN(A("ID"), UPERM))
+        act(A("XR"), IN(xw, A("IL", 0, 12 * KS)), AF.Copy)
+        mm(KA, IDN, A("KC", 0, L), True, False)
+        xo = [A("B6", 0, L), A("B6", L, 2 * L), A("B7", L, 2 * L), A("B5", 0, L), A("B5", L, 2 * L)]
+        for j in range(KS):
+            mm(xo[j], IDN, A("XR", L * j, L * j + L), True, False)
+            mm(xo[j], NID, z, False, True)
+
+        def dv(k0, k1):
+            for k in range(k0, k1):
+                tt(X("DB", ALL, k, k, k + 1), IN(xw, A("IL", 12 * k, 12 * k + 12)), z, sub)
+
+        def dabs(k0, k1):
+            act(X("AB", ALL, slice(k0, k1), k0, k1), X("DB", ALL, slice(k0, k1), k0, k1), AF.Abs)
+
+        def dpe(k0, k1, end=False):
+            for r in range(16):
+                mm(X("B4", slice(0, 12), slice(k0, k1), 0, L), Z(Z4K, r), X("AB", slice(r, L, 16), slice(k0, k1), k0, k1), False, end and r == 15)
+        dv(KS, 6)
+        for j in range(KS):
+            act(X("AB", ALL, j, j, j + 1), xo[j], AF.Abs)
+        dv(6, 9)
+        dabs(KS, 6)
+        usum(v)
+        dpe(0, 6)
+        dv(9, 11)
+        dabs(6, 9)
+        mm(O37, IDM, A("OF"), True, False); mm(O37, NID, A("KN", 0, L), False, False); mm(O37, NID, A("KN", L, 2 * L), False, True)
+        dv(11, 14)
+        dabs(9, 11)
+        dpe(6, 11)
+        act(A("UT", 0, 12), A("B7", 0, 12), AF.Copy)
+        dv(14, 16)
+        dabs(11, 14)
+        dabs(14, 16)
+        dpe(11, 16, True)
+        ts(A("HI"), A("ID"), 6, shr); ts(A("LO"), A("ID"), 63, band)
+        if v == 0:
+            step1_constants()
+        else:
+            f_scatter()
+        tt(A("P1"), IN(A("UT", 0, 12), UJ), A("OF"), mul)
+        tt(A("KE"), KA, A("HI"), add)
+        tt(A("KS"), KA, A("LO"), add)
+        scan(X("KY", ALL, 0, 0, 1), A("RS"), A("KE"), 0.0, mul, mx)
+        scan(X("KY", ALL, 1, 1, 2), A("RS"), A("KS"), 0.0, mul, mx)
+        act(A("CBS"), A("KS"), AF.Relu, bias=CBB, scale=64.0)
+        top = X("KY", slice(15, L, 16), 0, 0, 1)
+        ts(A("T2", 24, 48, 2), top, 4, shr, 0xF0, band)
+        ts(A("SC", 48, 60), top, THW, ALU.is_lt, 2.0 ** 24, mul)
+        ts(A("T2", 0, 24), X("KY", slice(15, L, 16), ALL), 255, band)
+        scan(A("SC", 0, 48), A("D2"), A("T2"), 0.0)
+        cp(A("SU", 0, 24), A("SC", 1, 48, 2))
+        tt(A("SC", 64, 76), A("SC", 1, 24, 2), A("SC", 48, 60), add)
+        IDL, KL = A("SU", 0, 12), A("SU", 12, 24)
+        cb = A("B5", L, 2 * L)
+        mm(cb, IDN, A("KN", 0, L), True, False); mm(cb, IDN, A("KN", L, 2 * L), False, False); mm(cb, IDN, A("CBS"), False, True)
+        act(A("OG"), IN(A("G1B"), KL), AF.Copy)
+        mm(A("B6", L, 2 * L), BK345, A("OG"), True, True)
+        if v == 0:
+            ts(A("ML"), IN(A("MI"), IDL), float(SB - PAD), add)
+            cp(A("M"), IN(A("MI"), IDL))
+        else:
+            act(A("M"), IN(A("MC"), IDL), AF.Copy)
+            ts(A("ML"), IN(A("MC"), IDL), float(SB - PAD), add)
+        mm(A("B7", L, 2 * L), IDM, A("M"), True, True)
+        xm = A("XX", PAD)
+
+        def gm(c):
+            act(A("AM", 1024 * c, 1024 * c + 1024), IN(xm, A("ML", 64 * c, 64 * c + 64)), AF.Copy)
+            name("members%d" % c, v)
+        gm(0)
+        ts(A("P2"), A("P1"), 5, shr, W - 1, band)
+        tt(A("S1"), A("B6", L, 2 * L), A("M"), mul)
+        tt(A("P4"), cb, A("P2"), mn)
+        ts(A("S2"), A("S1"), 5, shr, W - 1, band)
+        tt(A("P5"), O37, A("P4"), add)
+        tt(A("S3"), A("B7", L, 2 * L), A("S2"), add)
+        ts(A("P6"), A("P5"), W - 1, band)
+        ts(A("SL"), A("S3"), float(SB - PAD), add)
+        if v in (1, 2):
+            yc_start(8 * v - 8, 8 * v)
+            act(A("YT" if v == 1 else "YA"), A("B2", 256, 512), bias=68.0)
+        if last:
+            yc_finish()
+        if v == 0:
+            gcp(A("MC", 0, 1024), A("MI", 0, 1024))
+        if not last:
+            gcp(A("OS", L * v, L * v + L), A("P6"))
+            send(A("OL", L * (v + 1), L * (v + 2)), A("OS", L * v, L * v + L), v + 1)
+        else:
+            gcp(A("FF"), A("P6"))
+        if v == 0:
+            for c in range(1, 4):
+                gcp(A("MC", 1024 * c, 1024 * c + 1024), A("MI", 1024 * c, 1024 * c + 1024))
+            iota(A("MC", W, SB), [[0, SB - W]], -1)
+        act(A("IG"), IN(A("P", 0, W) if v == 0 else A("P"), IDL), AF.Copy)
+        name("ids", v)
+        mm(A("B7", 0, L), BK345, A("IG"), True, True)
+        gm(1)
+
+        def gs(c):
+            tt(A("YB", 1024 * c, 1024 * c + 1024), IN(xm, A("SL", 64 * c, 64 * c + 64)), A("AM", 1024 * c, 1024 * c + 1024), mn)
+            name("supports%d" % c, v)
+
+        def psub(c, h):
+            bank = "B%d" % ((2 * c + h) % 3)
+            for k in range(8):
+                o = X(bank, slice(k, 32, 8), ALL)
+                mm(o, IDN, A("YB", 1024 * c + 8 * h + k, 1024 * c + 1024, 16), True, False, "psub")
+                mm(o, NID, A("ZL", L * v + 64 * c, L * v + 64 * c + 64), False, True, "psub")
+
+        def sabs(c, h):
+            act(X("EB", slice(4 * c, 4 * c + 4), slice(128 * h, 128 * h + 128), 2 * c + h, 2 * c + h + 1), A("B%d" % ((2 * c + h) % 3), 0, 512), AF.Abs)
+            name("abs%d" % (2 * c + h), v)
+
+        def e1(c):
+            if c == 0:
+                mm(KA, IDN, A("EC", 0, L), True, False); mm(KA, IDN, A("EC", L, 2 * L), False, False)
+            for h in range(2):
+                for k in range(8 * h, 8 * h + 8):
+                    mm(A("B4", 64 * c, 64 * c + 64), Z(Z4K, k), X("EB", slice(4 * c, 4 * c + 4), slice(16 * k, 16 * k + 16), 2 * c + h, 2 * c + h + 1),
+                       False, c == 2 and k == 15, "e%d" % h)
+
+        def eq(q0, q1):
+            for q in range(q0, q1):
+                ts(EQ(q), A("B7", 16 * q, L), C("SC", 64 + q), eq_, WR, mul)
+                name("equal", v)
+
+        def eqpe():
+            mm(A("B6", 0, L), BK, EQ(0), True, False)
+            for q in range(12):
+                if q:
+                    mm(A("B6", 16 * q, 16 * q + 16), BK, A("EQ", EQ(q)[1][0][1], EQ(q)[1][0][1] + 16), False, q == 11)
+                if q < 11:
+                    mm(A("B6", 16 * q + 16, L), BKX, EQ(q, 16), False, False)
+
+        if v == 0:
+            powers()
+            slots(0, 4)
+            slot_row()
+        gs(0); psub(0, 0); psub(0, 1)
+        gm(2)
+        eq(0, 12)
+        gs(1)
+        eqpe()
+        sabs(0, 0); sabs(0, 1)
+        psub(1, 0); psub(1, 1)
+        act(A("WB"), A("B6", 0, L), AF.Copy)
+        gs(2)
+        e1(0)
+        deal(A("B7", 0, 12), Z1, "WB", 0, L)
+        sabs(1, 0); sabs(1, 1)
+        psub(2, 0); psub(2, 1)
+        act(A("XO"), IN(xw, IDL), AF.Copy)
+        e1(1)
+        sabs(2, 0); sabs(2, 1)
+        n2 = A("B6", L, 2 * L)
+        mm(n2, IDN, A("XO"), True, False); mm(n2, NID, z, False, True)
+        e1(2)
+        act(A("ZN"), n2, AF.Abs, scale=2.0)
+        mm(n2, IDN, A("ZN"), True, False); mm(n2, NID, z, False, True)
+        act(A("AM", 3072, 3264), n2, AF.Copy)
+        if v == 0:
+            f_constants()
+            dma(A("F"), A("P", 0, PAD))
+            dma(A("P", SB, SB + W), A("P", 0, W))
+            dma(A("P", SB, SB + W, p=5), KSB)
+        if v == 1:
+            end_constants()
+        ts(A("SF", 0, 12), A("B7", 0, 12), THR, ALU.is_ge, 2.0 ** 24, mul)
+        if not last:
+            gcp(A("OF"), A("OL", L * (v + 1), L * (v + 2)))
+            g1(v + 1, "V", 0, GV // 2)
+        else:
+            turn(A("FF"), "B3")
+            act(A("YO"), A("B3", 0, L), AF.Copy)
+            dma(H(T.yo[:]), A("YO"))
+        tt(A("SF", 16, 28), A("SF", 0, 12), A("SC", 64, 76), add)
+        if not last:
+            g1(v + 1, "V", GV // 2, GV)
+            g1(v + 1, "S", GV, (GV + L) // 2)
+            g1pe("B3", Z01, 0, GV)
+            g1(v + 1, "S", (GV + L) // 2, L)
+            g1pe("B3", Z01, GV, L)
+        lt = A("LT", 16 * v, 16 * v + 12)
+        tt(A("SF", 32, 44), A("SF", 16, 28), ALT, mn)
+        ts(lt, A("SF", 16, 28), 9000.0, ALU.is_ge, 2.0 ** 24, mul)
+        cp(TG, A("SF", 32, 44))
+        op("V", lambda: g.vector.transpose(T.KS[:], T.B4[:, 0:12, :]), A("KS"), [A("B4", 0, L)])
+        ts(A("NK"), A("B4", 0, L), T2K, ALU.is_gt, -8192.0, mul)
+        scan(A("KE"), A("RB"), A("KS"), 0.0, mx, mn)
+        for jp, (w1, w2) in enumerate(((W10, W20), (W11, W21))):
+            mm(A("B5", jp, 12, 2), w1, A("KE", 16 * jp + 15, L, 32), True, False)
+            mm(A("B5", jp, 12, 2), w2, A("KE", 31 - 16 * jp, L, 32), False, True)
+        if last:
+            tt(A("XC"), A("B7", L, 2 * L), A("NK"), add)
+            mm(FP, A("WF", 0, 128), A("NK"), True, False)
+            act(A("KM"), A("XC"), AF.Relu, bias=1.0)
+            mm(FP, A("WF", 256, 384), A("KM"), False, False)
+        else:
+            tt(IN(A("MC", 0, PAD), TG), A("M"), A("NK"), add)
+        tt(A("SF", 48, 60), A("B5", 0, 12), lt, add)
+        mm(ZP, IHB, z, True, False); mm(ZP, IDN, A("KB", 256, 256 + L), False, False)
+        if not last:
+            cp(A("CL"), A("B3", 0, L))
+        tt(A("SI", 0, 12), A("SF", 48, 60), CAP, mn)
+        ts(A("SI", 16, 28), A("SI", 0, 12), W - 1, band)
+        ts(A("SI", 28, 40), A("SI", 0, 12), 15, band)
+        cp(A("SU", 48, 72), A("SI", 16, 40))
+
+        def g2(q, c0, c1):
+            o, i = A("G2B", 16 * c0, 16 * c1), IN(A("MC", 0, PAD), A("CL", c0, c1))
+            if q == "S":
+                act(o, i, AF.Sign, bias=0.5)
+            else:
+                ts(o, i, 0.0, ALU.is_ge, 2.0, mul)
+
+        def g2pe(c0, c1):
+            mm(A("B2", c0, c1), IDN, A("HN", c0, c1), True, False)
+            deal(A("B2", c0, c1), ZPOW, "G2B", 16 * c0, 16 * c1, first=False)
+        if last:
+            tt(A("CBV"), IN(A("DG"), SLOT), A("M"), mul)
+            act(A("XC"), IN(A("AM"), IDX), AF.Copy)
+            mm(FP, A("WF", 128, 256), A("CBV"), False, True)
+            mm(ZP, IH, A("XC"), False, True)
+            f_scatter()
+            ts(A("YZ"), ZP, M0, add, M0, sub)
+            dma(H(T.yz[:]), A("YZ"))
+            break
+        act(A("XC"), IN(A("AM"), IDX), AF.Copy)
+        mm(ZP, IH, A("XC"), False, True)
+        g2("S", 0, GS // 2)
+        tt(A("CBV"), IN(A("DG"), SLOT), A("M"), mul)
+        zs = A("ZS", L * v, L * v + L)
+        ts(zs, ZP, M0, add, M0, sub)
+        send(A("ZL", L * (v + 1), L * (v + 2)), zs, 5 + v)
+        if v == 0:
+            for c in range(0, W, 512):
+                iota(A("MC", SB + c, SB + c + 512), [[0, 512]], -1)
+            dma(A("MC", SB, SB + W, p=0), A("CF"))
+            for c in range(0, W, 512):
+                gcp(A("MF", c, c + 512), A("MI", c, c + 512))
+        g1pe("B0", Z2, 0, GV); g1pe("B0", Z2, GV, L)
+        g2("V", GS, L)
+        g2("S", GS // 2, GS)
+        g2pe(0, GS // 2)
+        g2pe(GS, L)
+        act(OWN, A("OF"), bias=float(SB))
+        for u in range(v + 1):
+            mm(A("B6", 0, 12), BK, A("LT", 16 * u, 16 * u + 12), u == 0, u == v)
+        g2pe(GS // 2, GS)
+        cp(IN(A("XX", 0, PAD), TG), A("XC"))
+        act(A("PW"), A("B0", 0, L), AF.Copy)
+        act(A("SF", 64, 76), A("B6", 0, 12), scale=-2.0 ** -24, bias=16.0 * (v + 1), acc=ACC)
+        act(A("KM"), IN(A("MC", 0, PAD), TG), AF.Relu, bias=1.0)
+        mm(FP, A("WF", 0, 128), A("NK"), True, False)
+        mm(FP, A("WF", 128, 256), A("CBV"), False, False)
+        mm(FP, A("WF", 256, 384), A("KM"), False, True)
+        tt(A("V1"), A("B2", 0, L), A("PW"), mul)
+        cp(C("AI", 3), ACC)
+        ts(A("V2"), A("V1"), 32768, band)
+        ts(C("AI", 4), C("AI", 3), 127, band)
+        tt(A("V3"), OWN, A("V2"), sub)
+        ts(THW, C("AI", 4), T1P, add, 4096.0, mul)
+        tt(A("ID"), A("B3", 0, L), A("V3"), mx)
+
+    act(A("B0", 0, 256), A("CF"), AF.Copy)
+    act(A("B0", 256, 512), A("C1"), AF.Copy)
+    mm(A("B4", 0, 256), IDN, KNEG, True, False)
+    mm(A("B5", 0, 256), NIM, A("CF"), True, False)
+    mm(A("B6", 0, 256), NIM, A("C1"), True, False); mm(A("B6", 0, 256), IDN, K20, False, False)
     for c in range(4):
         for h, q in enumerate("VS"):
             gat(q, A("FL", 1024 * c + 512 * h, 1024 * c + 512 * h + 512), IN(A("F"), A("LA", 64 * c + 32 * h, 64 * c + 32 * h + 32)))
-        deal(A("B1", 64 * c, 64 * c + 64), Z01, "FL", 1024 * c, 1024 * c + 1024)
-        deal(A("B2", 64 * c, 64 * c + 64), Z23, "FL", 1024 * c, 1024 * c + 1024)
-    act(A("YO"), A("B0", 0, L), AF.Copy)
-    dma(H(T.yo[:]), A("YO"))
-    deal(A("B3", 0, 256), Z456, "FL", 0, W)
-    tt(A("FV"), A("B1", 0, 256), A("PWA"), mul)
-    tt(A("B4", 0, 256), A("B2", 0, 256), A("CF"), sub)
+        for bank, kind in (("B4", ZMK), ("B5", Z345)):
+            deal(A(bank, 64 * c, 64 * c + 64), kind, "FL", 1024 * c, 1024 * c + 1024, False, c == 3)
+    deal(A("B6", 0, 256), ZSM, "FL", 0, W, False)
+    tt(A("FV"), A("B4", 0, 256), A("PWA"), mul)
     ts(A("FB"), A("FV"), 15, shr, 1, band)
-    ts(A("B4", 256, 512), A("B4", 0, 256), 0.0, ALU.is_equal)
-    ts(A("B7", 0, 256), A("FB"), -1.0, mul, 1.0, add)
-    tt(A("FE"), A("B4", 0, 256), A("FB"), mul)
-    tt(A("B7", 256, 512), A("B7", 0, 256), A("YA"), mul)
-    tt(A("FW"), A("B4", 256, 512), A("FB"), mul)
-    tt(A("FR"), A("B5", 0, 256), A("FE"), add)
+    tt(A("FE"), A("B5", 0, 256), A("FB"), mul)
+    tt(A("FR"), A("B0", 0, 256), A("FE"), add)
     dma(H(T.yr[:]), A("FR"))
-    tt(A("FY"), A("B3", 0, 256), A("FW"), mul)
-    tt(A("FZ"), A("B7", 256, 512), A("FY"), add)
+    ts(A("B7", 0, 256), A("FE"), 0.0, eq_)
+    tt(A("B3", 256, 512), A("B6", 0, 256), A("YT"), mn)
+    tt(A("FT"), A("B3", 256, 512), A("FB"), mul)
+    tt(A("FU"), A("B0", 256, 512), A("FT"), add)
+    tt(A("FZ"), A("B7", 0, 256), A("FU"), mul)
     dma(H(T.yc[:]), A("FZ"), "S")
 
-    hist = {}
-    for i, o in enumerate(ops):
-        deps = set()
-        acc = [(a, False) for a in o["r"]] + [(a, True) for a in o["w"]]
-        for (nm, lo, hi, p1), wr in acc:
-            psum = SCRATCH[nm][0] == "psum"
-            for (j, l2, h2, p2, w2) in hist.get(nm, []):
-                pj = ops[j]
-                same = pj["q"] == o["q"] and pj["k"] == "c" and o["k"] == "c"
-                over = l2 < hi and lo < h2 and (p1 is None or p2 is None or p1 == p2)
-                if pj["k"] == "s":
-                    continue
-                if same:
-                    if o["q"] != "P" and over and ((w2 and not wr) or (SAMEQ and (w2 or wr))):
-                        deps.add(j)
-                elif psum or (over and (wr or w2)):
-                    deps.add(j)
-        best = {}
-        keep = []
-        for j in deps:
-            if ops[j]["k"] == "c":
-                best[ops[j]["q"]] = max(best.get(ops[j]["q"], -1), j)
-            else:
-                keep.append(j)
-        o["deps"] = sorted(keep + list(best.values()))
-        for (nm, lo, hi, p1), wr in acc:
-            hist.setdefault(nm, []).append((i, lo, hi, p1, wr))
-    seen = {q: {} for q in Q}
-    for o in ops:
-        if o["q"] is None:
-            continue
-        need = []
-        for j in o["deps"]:
-            key = ops[j]["q"] if ops[j]["k"] == "c" else j
-            if seen[o["q"]].get(key, -1) < j:
-                seen[o["q"]][key] = j
-                need.append(j)
-                ops[j]["sig"] = True
-        o["deps"] = need
+    if not PLAN:
+        PLAN.extend(plan(ops))
     cnt = {"V": 0, "S": 0, "P": 0, "G": 0, "d": 0, "s": 0}
-    for o in ops:
+    for i, need in PLAN:
+        for j in need:
+            ops[j]["sig"] = True
+    for i, need in PLAN:
+        o = ops[i]
         if o["k"] == "a":
             o["at"] = (o["sem"], neng)
             continue
-        for j in o["deps"]:
+        for j in need:
             Q[o["q"]].wait_ge(T.sem[ops[j]["at"][0]], ops[j]["at"][1])
-        ins = o["fn"]()
+        for fn in o["fn"]:
+            ins = fn()
         if o["k"] == "d":
             o["at"] = ("d%d" % cnt["d"], 16)
             cnt["d"] += 1

from concourse.mybir import AluOpType as ALU, AxisListType as AX, ActivationFunctionType as AF

W, L, VI, HOP = 4096, 192, 4, 3
PAD, SB = 4288, 4352
F32, BF, I32, U16 = "float32", "bfloat16", "int32", "uint16"
M0, M6 = 1.5 * 2.0 ** 23, 1.5 * 2.0 ** 29
CYC, PECYC, GATHER, SCATTER, WAKE = 0.83e-3, 0.5e-3, 1.56, 3.0, 0.07
DMA_RATE, DMA_FIX, HOP_TIME = 330e3, 1.8, 3.0
KS, GV, G0V, GA, GS = 4, 112, 48, 112, 128

_S = {
    "XX": (SB + 2 * W, BF), "MC": (SB + W, F32), "MI": (W, I32), "COL": (W, F32), "P": (SB + W, BF), "F": (PAD, BF),
    "G1B": (3072, BF), "GD": (W, BF), "AM": (3264, F32), "EQ": (1248, BF), "XR": (KS * L, BF), "DL": (L, F32),
    "REP": (256, I32), "LA": (256, U16), "DA": (1280, BF), "PWA": (256, F32), "YA": (256, F32), "YT": (256, F32), "CF": (256, F32),
    "C1": (256, F32), "KB": (4 * 256, BF), "FV": (256, I32), "FB": (256, I32),
    "FCT": (L, I32), "TH": (4, I32), "THF": (4, F32), "CO": (40, F32), "AI": (8, I32), "IT": (L, I32), "I2": (16, I32), "DG": (16, F32),
    "RS": (L, F32), "RB": (L, F32), "KC": (L, BF), "KN": (2 * L, BF), "EC": (2 * L, BF), "HN": (L, BF), "LC": (80, F32), "UL": (24, U16),
    "ZB": (144, F32), "ZZ": (9 * 144, BF), "ZK": (144, F32), "BF": (128, F32), "BB": (7 * 128, BF), "WF": (3 * 128, F32),
    "FM": (7 * 128, F32), "CM": (64, F32),
    "OL": (4 * L, U16), "OS": (3 * L, U16), "ZL": (4 * L, BF), "ZS": (3 * L, BF),
    "OF": (L, F32), "PW": (L, F32), "CL": (L, U16), "V1": (L, I32), "V2": (L, I32), "V3": (L, F32), "ID": (L, I32), "IL": (L, U16),
    "LO": (L, I32), "HI": (L, I32), "UT": (16, F32), "P1": (L, I32), "P2": (L, I32), "P4": (L, F32), "P5": (L, I32), "P6": (L, I32),
    "SI": (64, I32), "SF": (96, F32), "SU": (96, U16), "LT": (4 * 16, BF), "CBS": (L, BF),
    "T2": (48, I32), "D2": (48, F32), "SC": (80, F32), "KS": (L, F32), "K32": (L, BF),
    "IG": (L, BF), "OG": (L, BF), "XO": (L, BF), "ZN": (L, BF), "WB": (L, BF), "ML": (L, U16), "M": (L, F32),
    "S1": (L, I32), "S2": (L, I32), "S3": (L, I32), "SL": (L, U16), "KE": (L, F32), "NK": (L, F32), "KM": (L, F32), "XC": (L, F32),
    "CBV": (L, F32), "FI": (L, I32), "FG": (L, I32), "YO": (L, F32), "YZ": (L, F32),
}
ALIAS = {"G2B": ("GD", 0, 3072), "YB": ("GD", 0, 3072), "FL": ("GD", 0, W), "MF": ("COL", 0, W),
         "FE": ("AM", 0, 256), "FR": ("AM", 256, 256), "FT": ("AM", 512, 256), "FU": ("AM", 768, 256), "FZ": ("AM", 1024, 256),
         "TA": ("AM", 0, 128), "TB": ("AM", 128, 128), "FF": ("YO", 0, L)}
SCRATCH = {n: ("sbuf", [128, c], d) for n, (c, d) in _S.items()}
for _n, _sh, _d in (("DB", [L, 16], BF), ("AB", [L, 16], BF), ("EB", [12, 256], BF), ("KY", [L, 2], I32), ("TR", [12, 16], F32)):
    SCRATCH[_n] = ("sbuf", [128] + _sh, _d)
for _b in range(8):
    SCRATCH["B%d" % _b] = ("psum", [128, 32, 16] if _b < 5 else [128, 512], F32)
NDMA = 40
SEMAPHORES = ["cV", "cS", "cP", "cG", "sent"] + ["ar%d" % i for i in range(8)] + ["d%d" % i for i in range(NDMA)]


PLAN = []
SLACK, ROUNDS = 0.05, 8


def plan(ops):
    hist, deps = {}, []
    for i, o in enumerate(ops):
        d = {i - 1} if o["k"] == "a" else set()
        acc = [(a, False) for a in o["r"]] + [(a, True) for a in o["w"]]
        for (nm, lo, hi, p1, _n), wr in acc:
            psum = SCRATCH[nm][0] == "psum"
            for (j, l2, h2, p2, w2) in hist.get(nm, []):
                over = l2 < hi and lo < h2 and (p1 is None or p2 is None or p1 == p2)
                if ops[j]["k"] != "s" and ((over and (wr or w2)) or (psum and (ops[j]["q"] != o["q"] or o["q"] == "P"))):
                    d.add(j)
        deps.append(d)
        for (nm, lo, hi, p1, _n), wr in acc:
            hist.setdefault(nm, []).append((i, lo, hi, p1, wr))
    waits = [set(d) for d in deps]
    prev = {}
    for i, o in enumerate(ops):
        if o.get("keep") and o["q"] in ("V", "S", "P", "G"):
            deps[i] |= {prev.get(o["q"], i)} - {i}
            prev[o["q"]] = i
    after = [[] for _ in ops]
    for i, d in enumerate(deps):
        for j in d:
            after[j].append(i)

    def lag(j, i):
        return 0.0 if ops[j]["q"] == ops[i]["q"] == "P" or j not in waits[i] else WAKE + (0.1 if ops[j]["q"] == "P" else 0.0)
    way = [0.0] * len(ops)
    left = [len(a) for a in after]
    todo = [i for i, n_ in enumerate(left) if not n_]
    while todo:
        i = todo.pop()
        way[i] = ops[i]["t"] + (DMA_FIX if ops[i]["k"] == "d" else 0.0) + max([way[k] + lag(i, k) for k in after[i]], default=0.0)
        for j in deps[i]:
            left[j] -= 1
            if not left[j]:
                todo.append(j)


    def run(before, behind, way, back):
        left, ready = [len(d) for d in before], {i: 0.0 for i, d in enumerate(before) if not d}
        free, engines, order, ends = {}, 0.0, [], [0.0] * len(ops)
        loads = [i for i, o in enumerate(ops) if o["q"] == "Y"][::-1 if back else 1]
        while ready:
            can = {k: max(t, free.get(ops[k]["q"], 0.0)) for k, t in ready.items() if ops[k]["q"] != "Y" or k == loads[0]}
            now = min(can.values())
            q = ops[min(can, key=lambda k: (can[k], -way[k]))]["q"]
            mine = [k for k in can if ops[k]["q"] == q]
            i = max((k for k in mine if can[k] <= now + 1e-9), key=lambda k: (way[k], -k))
            for k in sorted(mine, key=can.get):
                if q and can[i] < can[k] < can[i] + ops[i]["t"] and \
                        max(way[k] + can[k], way[i] + can[k] + ops[k]["t"]) < max(way[i] + can[i], way[k] + can[i] + ops[i]["t"]) - SLACK:
                    i = k
            o = ops[i]
            if q == "Y":
                loads.pop(0)
            start = can[i]
            ready.pop(i)
            end = start + o["t"]
            if o["k"] == "d":
                engines = max(engines, start + DMA_FIX / 2) + o["t"]
                end, free[o["q"]] = engines + DMA_FIX / 2, start + 0.05
            elif o["q"]:
                free[o["q"]] = end
            order.append(i)
            ends[i] = end
            for k in behind[i]:
                left[k] -= 1
                if not left[k]:
                    ready[k] = max(ends[j] + (lag(k, j) if back else lag(j, k)) for j in before[k])
        return order, ends
    best = None
    for _ in range(ROUNDS):
        order, ends = run(deps, after, way, False)
        if best is None or max(ends) < best[0]:
            best = (max(ends), order)
        way = run(after, deps, ends, True)[1]
    order = best[1]
    place = {i: n_ for n_, i in enumerate(order)}
    seen, out = {}, []
    for i in order:
        q, need = ops[i]["q"], []
        for j in sorted(waits[i], key=place.get, reverse=True) if q else []:
            key = (q, ops[j]["q"] if ops[j]["k"] == "c" else j)
            if not (q == "P" == ops[j]["q"]) and seen.get(key, -1) < place[j]:
                seen[key] = place[j]
                need.append(j)
        out.append((i, need))
    return out


def rank_program(g, core, T, topo):
    rank = T.rank_of(core)
    if rank is None:
        return
    n = len(T.cores)
    dst = T.cores[(rank + HOP) % n]
    rid, pid, _e = topo.addr(dst)
    emask, neng = topo.mask(core, dst), len(topo.engines(core, dst))
    Q = {"V": g.vector, "S": g.scalar, "P": g.tensor, "G": g, "Y": g.sync}
    ops, keep = [], [False]
    ALL = slice(None)

    def A(nm, lo=0, hi=None, st=1, p=None):
        if nm in ALIAS:
            nm, off, n_ = ALIAS[nm]
            lo, hi = lo + off, off + (n_ if hi is None else hi)
        if len(SCRATCH[nm][1]) == 3:
            if lo % 16 == 0 and hi % 16 == 0:
                return (T[nm][:, lo // 16:hi // 16, :], [(nm, lo, hi, None, hi - lo)])
            return (T[nm][:, lo // 16, lo % 16:lo % 16 + hi - lo], [(nm, lo, hi, None, hi - lo)])
        if hi is None:
            hi = SCRATCH[nm][1][1]
        ps = ALL if p is None else slice(p, 128, 16)
        ap_ = T[nm][ps, lo:hi] if st == 1 else T[nm][ps, lo:hi:st]
        return (ap_, [(nm, lo, hi, p, len(range(lo, hi, st)))])

    def C(nm, c):
        return A(nm, c, c + 1)

    def X(nm, i1, i2, lo=0, hi=1 << 20):
        cnt_ = 1
        for i_, d_ in zip((i1, i2), SCRATCH[nm][1][1:]):
            cnt_ *= len(range(d_)[i_]) if isinstance(i_, slice) else 1
        return (T[nm][:, i1, i2], [(nm, lo, hi, None, cnt_)])

    def size(x):
        return x[1][0][4] if len(x) == 2 else 16 * x[2][0][4]

    def wide(x):
        return {F32: 4, I32: 4, BF: 2, U16: 2}[SCRATCH[x[1][0][0]][2]]

    def cost(q, out, ins, kind):
        ins = [x for x in ins if isinstance(x, tuple) and x[1]]
        if kind == "d":
            x = out if out[1] else ins[0]
            return size(x) * wide(x) * (128 if x[1][0][3] is None else 8) / DMA_RATE
        if kind == "s":
            return 0.3
        if q == "P":
            return max(64, size(ins[1])) * (4 if wide(ins[1]) == 4 else 1) * PECYC
        n_ = max([size(out)] + [size(x) for x in ins[:1]])
        if q == "G":
            return 0.15 + 2 * n_ * CYC
        if len(out) == 3:
            return 0.05 + SCATTER * n_ * CYC
        if ins and len(ins[0]) == 3:
            return 0.06 + GATHER * n_ * CYC
        if q == "S":
            return 0.06 + n_ * CYC
        full = [x for x in ins if size(x) == n_]
        rate = 2.0 if len(full) == 2 and kind == "tt" and all(SCRATCH[x[1][0][0]][0] == "sbuf" for x in full) else 1.0
        if kind != "tt" and all(wide(x) == 2 for x in [out] + full):
            rate = 0.5
        return 0.03 + max(64, rate * n_) * CYC

    def IN(w, o):
        return (w[0].indirect(o[0]), w[1], o[1])

    def rd(*xs):
        r = []
        for x in xs:
            if isinstance(x, tuple):
                for y in x[1:]:
                    r += y
        return r

    def ap(x):
        return x[0] if isinstance(x, tuple) else x

    def op(q, fn, out, ins, kind="c", more=()):
        ops.append({"q": q, "fn": fn, "w": (list(out[1]) if out else []) + list(more),
                    "r": rd(*ins) + (list(out[2]) if out and len(out) > 2 else []), "k": "c" if kind == "tt" else kind,
                    "t": cost(q, out, ins, kind), "keep": keep[0]})
        ops[-1]["fn"] = [fn]

    def loose(fn, *args):
        keep[0] = False
        fn(*args)
        keep[0] = True

    def cp(o, i):
        op("V", lambda: g.vector.tensor_copy(o[0], i[0]), o, [i])

    def tt(o, a, b, f):
        op("V", lambda: g.vector.tensor_tensor(o[0], a[0], b[0], f), o, [a, b], "tt")

    def ts(o, a, s1, f1, s2=None, f2=None):
        if f2 is None:
            op("V", lambda: g.vector.tensor_scalar(o[0], a[0], ap(s1), None, f1), o, [a, s1])
        else:
            op("V", lambda: g.vector.tensor_scalar(o[0], a[0], ap(s1), ap(s2), f1, f2), o, [a, s1, s2])

    def ms(o, v):
        op("V", lambda: g.vector.memset(o[0], v), o, [])

    def scan(o, a, b, init, f0=ALU.mult, f1=ALU.add):
        op("V", lambda: g.vector.tensor_tensor_scan(o[0], a[0], b[0], init, f0, f1), o, [a, b])

    def red(o, a):
        op("V", lambda: g.vector.tensor_reduce(o[0], a[0], AX.X, ALU.add), o, [a])

    def act(o, i, f=AF.Identity, bias=0.0, scale=1.0, acc=None):
        if acc is None:
            op("S", lambda: g.scalar.activation(o[0], i[0], f, bias=ap(bias), scale=ap(scale)), o, [i, bias, scale])
        else:
            op("S", lambda: g.scalar.activation(o[0], i[0], f, bias=ap(bias), scale=ap(scale), accum_out=acc[0]), o, [i, bias, scale], more=acc[1])

    def gat(q, o, i):
        if q == "V":
            cp(o, i)
        else:
            act(o, i, AF.Copy)

    def mm(o, w, r, a, b, join=None):
        op("P", lambda: g.tensor.matmul(o[0], w[0], r[0], a, b), o, [w, r])
        new, key = ops[-1], (o[1][0][0], join or r[1][0][0])
        new["key"] = key
        if len(ops) > 1 and ops[-2].get("key") == key and ops[-2]["t"] < 0.8:
            ops.pop()
            for f_ in ("fn", "w", "r"):
                ops[-1][f_] += [x for x in new[f_] if x not in ops[-1][f_]]
            ops[-1]["t"] += new["t"]

    def iota(o, pat, base, cm=0):
        if SCRATCH[o[1][0][0]][2] == I32:
            op("G", lambda: g.iota(o[0], pat, base, cm), o, [])
        else:
            op("G", lambda: g.iota(o[0], pat, base, cm, allow_small_or_imprecise_dtypes=True), o, [])

    def gcp(o, i):
        w = o[1][0][2] - o[1][0][1]
        op("G", lambda: g.affine_select(o[0], i[0], [[0, w]], ALU.is_ge, 0.0, 1, 0), o, [i])

    def dma(o, i, q="Y"):
        op(q, lambda: Q[q].dma_start(o[0], i[0]), o, [i], "d")

    def H(x):
        return (x, [])

    def send(o, i, k):
        op("G", lambda: g.remote_dma(o[0], i[0], T.sem["ar%d" % k], T.sem.sent, pid, rid, emask), None, [i], "s")
        ops.append({"q": None, "fn": None, "w": list(o[1]), "r": [], "k": "a", "sem": "ar%d" % k, "t": HOP_TIME})

    def Z(v, r):
        return A("ZZ", 144 * v + 15 - r, 144 * v + 143 - r)

    def ZV(v):
        return A("ZZ", 144 * v, 144 * v + 144)
    Z1, Z4K, ZPOW, Z01, Z2, Z345, ZMK, ZSM, ZSL = range(9)
    BK, BKX, BK345, IDN, NID, I64, IHB = (A("BB", 128 * i, 128 * i + 128) for i in range(7))
    IDM, NIM, IH, W10, W11, W20, W21 = (A("FM", 128 * i, 128 * i + 128) for i in range(7))
    KSB, KQ, KNEG, K20 = (A("KB", 256 * i, 256 * i + 256) for i in range(4))

    def deal(o, v, buf, lo, hi, first=True, last=True):
        for r in range(16):
            mm(o, Z(v, r), A(buf, lo + r, hi, 16), first and r == 0, last and r == 15)

    (RC, T1P, THW, T2K, CBB, ACC, WP, WS, WR, THR, C01, C345, CMK, CSM, FBI, K1, RC256, RC16, G0, G1, P2R,
     X0, X1, X2, X3, X4, X5, X6) = (C("CO", i) for i in range(28))
    AIX, ALT, CAP = (A("LC", 16 * i, 16 * i + 12) for i in range(3))
    UJ, UPERM = A("UL", 0, 12), A("UL", 12, 24)
    add, sub, mul, mx, mn = ALU.add, ALU.subtract, ALU.mult, ALU.max, ALU.min
    band, shr, eq_ = ALU.bitwise_and, ALU.arith_shift_right, ALU.is_equal

    def D(i):
        return C("DG", i)

    def turn(src, bank):
        op("V", lambda: g.vector.transpose(T.TR[:], src[0]), X("TR", ALL, ALL), [src])
        for jp, (w1, w2) in enumerate(((W10, W20), (W11, W21))):
            o = X(bank, slice(jp, 12, 2), ALL, 0, L)
            mm(o, w1, X("TR", slice(jp, 12, 2), ALL), True, False)
            mm(o, w2, X("TR", slice(1 - jp, 12, 2), ALL), False, True)

    ms(A("TH"), 0)
    dma(A("REP"), H(T.rep[:])); dma(A("FCT"), H(T.fact[:]))
    dma(A("ZL", 0, L), H(T.z[:])); dma(A("TH", 0, 2, p=0), H(T.thr[:]))
    iota(C("AI", 0), [[0, 1]], 0, 1)
    iota(A("IT"), [[1, L]], 128, -1)
    iota(A("DA", 768, 1024), [[256, 256]], 0)
    iota(A("I2"), [[1, 16]], 0)
    ms(A("P", 0, 2304), 0.0)
    act(A("P", 2304, SB), A("P", 0, 2048), AF.Copy)
    ts(C("AI", 1), C("AI", 0), 15, band)
    ts(C("AI", 2), C("AI", 0), 4, shr, 1, band)
    ts(A("SI", 0, 16), A("IT", 0, 16), 15, band)
    cp(RC, C("AI", 1)); cp(G1, C("AI", 2))
    ts(A("DG"), A("SI", 0, 16), 0.0, eq_)
    ts(RC256, RC, 256.0, mul)
    ts(G0, G1, -1.0, mul, 1.0, add)
    ts(A("ZB"), A("IT", 0, 144), RC, add, 143.0, eq_)
    ts(A("DA", 1024, 1280), A("DA", 768, 1024), 0.0, mul, RC256, add)
    for w_, d_, m_ in ((W10, 128.0, G0), (W20, 144.0, G0), (W11, 128.0, G1), (W21, 112.0, G1)):
        ts(w_, A("IT", 0, 128), d_, eq_, m_, mul)
    ts(A("DA", 256, 512), A("REP"), M6, add, M6, sub)
    cp(A("FF"), A("FCT"))
    tt(A("DA", 0, 256), A("REP"), A("DA", 256, 512), sub)
    for row in (1, 0):
        dma(A("P", 0, W, p=row), A("DA", 256 * row, 256 * row + 256))
    dma(A("XX", SB, SB + W), H(T.feat[:]))
    dma(A("MI"), H(T.memb[:]))
    for row in (3, 4):
        dma(A("P", 0, W, p=row), A("DA", 256 * row, 256 * row + 256), "S")
    turn(A("FF"), "B1")
    ts(C01, D(0), D(1), add)
    ts(IDM, A("IT", 0, 128), 128.0, eq_)
    act(ZV(Z01), A("ZB"), scale=C01)
    act(ZV(Z4K), A("ZB"), scale=4096.0)
    act(ZV(Z1), A("ZB"), AF.Copy)
    cp(A("OL", 0, L), A("B1", 0, L))
    act(A("OF"), A("B1", 0, L), AF.Copy)
    act(IDN, IDM, AF.Copy); act(NID, IDM, scale=-1.0); act(NIM, IDM, scale=-1.0)
    iota(A("KC"), [[0, 12], [-256, 16]], 3840)
    iota(A("RS"), [[0, L]], 1)
    iota(A("RB"), [[0, L]], 0)
    for b_, fill in (("RS", 0.0), ("RB", 2.0 ** 30)):
        op("G", lambda b_=b_, fill=fill: g.affine_select(T[b_][:], T[b_][:], [[0, 12], [1, 16]], ALU.is_gt, fill, 0, 0), A(b_), [A(b_)])
    gcp(A("LA"), A("REP"))
    iota(A("KN", 0, L), [[0, 12], [-32, 16]], 0)
    iota(A("KN", L, 2 * L), [[0, 12], [-5, 16]], 0)
    iota(A("EC", 0, L), [[16, L]], 0)
    for c in range(4):
        iota(A("COL", 1024 * c, 1024 * c + 1024), [[1, 64], [256, 16]], 64 * c)
    ts(AIX, A("I2", 0, 12), 16.0, mul, RC, add)
    cp(UJ, A("I2", 0, 12))
    ts(A("SI", 16, 28), AIX, -5.5, add, 1.0 / 12, mul)
    ts(A("SF", 0, 12), AIX, 16.0, mul)
    ts(A("SF", 16, 28), A("SI", 16, 28), -191.0, mul)
    cp(A("THF"), A("TH"))
    tt(A("SF", 32, 44), A("SF", 0, 12), A("SF", 16, 28), add)
    ts(A("TA"), A("IT", 0, 128), RC, add, 128.0, ALU.is_ge)
    cp(UPERM, A("SF", 32, 44))
    ts(A("TB"), A("IT", 0, 128), RC, add, 143.0, ALU.is_le)
    ms(A("XX", W, SB), -256.0)
    tt(A("BF"), A("TA"), A("TB"), mul)
    mm(A("B2", 0, 2), A("BF"), A("THF", 0, 2), True, True)
    ms(A("D2", 0, 48, 2), 0.0)

    def g1(v, q, c0, c1):
        gat(q, A("G1B", 16 * c0, 16 * c1), IN(A("P", 0, W), A("OL", L * v + c0, L * v + c1)))

    def g1pe(bank, kind, c0, c1):
        deal(A(bank, c0, c1), kind, "G1B", 16 * c0, 16 * c1)

    def usum(v):
        deal(A("B7", 0, 12), Z1, "ZL", L * v, L * v + L)

    for q, c0, c1 in (("V", 0, 64), ("S", 96, 160), ("V", 64, 96), ("S", 160, 192)):
        g1(0, q, c0, c1)
        g1pe("B0", Z01, c0, c1)
    ms(A("D2", 1, 24, 2), 64.0); ms(A("D2", 25, 48, 2), -1.0)
    ts(X0, RC, 240.0, add)
    red(X1, A("DG", 4, 6))
    ts(A("T2", 25, 48, 2), A("I2", 0, 12), 256.0, mul, X0, add)
    ts(C345, D(3), 1.0 / 256, mul, X1, add)
    act(BK, A("BF"), AF.Copy); act(BKX, A("BF"), scale=2.0 ** 17)
    act(A("EC", L, 2 * L), A("EC", 0, L), bias=RC, scale=0.0)
    act(BK345, A("BF"), scale=C345)
    cp(A("ID"), A("B0", 0, L))
    dma(A("XX", SB + W, SB + 2 * W), H(T.feat[:]))
    dma(A("XX", 0, W), H(T.feat[:]))

    def step1_constants():
        ts(T1P, C("B2", 0), 1.0, add)
        ts(THW, C("B2", 0), 1.0, add, 4096.0, mul)
        ts(CBB, C("B2", 0), -64.0 * 4096, mul, -64.0 * 4000, add)
        ts(T2K, C("B2", 1), 4096.0, mul, 4095.0, add)

    def powers():
        ms(A("CM", 0, 16), 2.0); ms(A("CM", 16, 32), 0.5); ms(A("CM", 32, 48), 0.0)
        scan(A("CM", 48, 64), A("CM", 16, 32), A("CM", 32, 48), 2.0 ** 16)
        scan(A("CM", 16, 32), A("CM", 0, 16), A("CM", 32, 48), 0.5)
        tt(A("CM", 48, 64), A("CM", 48, 64), A("DG"), mul)
        tt(A("CM", 16, 32), A("CM", 16, 32), A("DG"), mul)
        red(WS, A("CM", 48, 64)); red(P2R, A("CM", 16, 32))
        act(ZV(ZSL), A("ZB"), scale=WS)
        ts(WR, WS, 2.0 ** -15, mul); ts(THR, WS, 40.0 * 2.0 ** -15, mul)
        ts(X2, D(15), -1.0, mul, 0.5, add)
        ts(X3, T2K, -1023.0, add)
        ts(WP, P2R, X2, mul)
        ts(ALT, AIX, 4096.0, add); ts(CAP, AIX, X3, add)
        ms(KQ, -0.25); ms(KSB, float(SB))
        act(IH, IDM, scale=0.5); act(IHB, IDM, scale=0.5)

    def slots(c0, c1):
        for c in range(c0, c1):
            tt(A("FL", 1024 * c, 1024 * c + 1024), IN(A("MI"), A("LA", 64 * c, 64 * c + 64)), A("COL", 1024 * c, 1024 * c + 1024), eq_)
            deal(A("B3", 64 * c, 64 * c + 64), ZSL, "FL", 1024 * c, 1024 * c + 1024)

    def slot_row():
        act(A("DA", 512, 768), A("B3", 0, 256), AF.Copy)
        dma(A("P", 0, W, p=2), A("DA", 512, 768))
        act(A("PWA"), A("B3", 0, 256), AF.Copy)

    def f_constants():
        act(ZV(ZPOW), A("ZB"), scale=WP); act(ZV(Z2), A("ZB"), scale=D(2))
        ms(A("WF"), 0.0)
        ms(A("HN", 0, GS), -0.5); ms(A("HN", GS, L), 0.0)
        ts(K1, RC, 1.0, add)
        act(A("ZK"), A("ZB"), scale=K1)
        ts(X4, D(9), 2.0 ** 28, mul)
        for m, col, rows in ((0, P2R, ((7, -1.0 / 32), (8, -1.0 / 8192))), (1, 1.0, ((3, 256.0), (4, 1.0))),
                             (2, K1, ((9, -256.0), (10, -1.0), (11, -1.0 / 256)))):
            for r, w_ in rows:
                ts(A("WF", 128 * m + r, 128 * m + 128, 16), A("BF", r, 128, 16), col, mul, w_, mul)
        ts(X5, D(10), 2.0 ** 20, mul, X4, add)
        ts(A("CF"), A("DA", 768, 1024), 1.0 / 256, mul, RC256, add)
        ts(FBI, D(11), 4096.0 - 255.0 / 512, mul, X5, add)

    def end_constants():
        ts(CMK, D(7), -1.0 / 256, mul, D(8), sub)
        ts(X6, D(9), -1.0 / 256, mul, D(10), sub)
        ms(KNEG, -1.0); ms(K20, 2.0 ** 20)
        ts(CSM, D(11), -256.0, mul, X6, add)
        act(ZV(ZMK), A("ZB"), scale=CMK); act(ZV(Z345), A("ZB"), scale=C345); act(ZV(ZSM), A("ZB"), scale=CSM)
        act(A("C1"), A("CF"), bias=1.0)

    def yc_sums(v, n0, n1):
        steps = [[], [0, 1, 2, 3, 4, 5], [6, 7, 8, 9, 10, None], [11, 12, 13, 14, 15, None]][v]
        for n_ in range(n0, min(n1, len(steps))):
            i = steps[n_]
            if i is None:
                mm(A("B2", 256, 512), IDM, A("YT"), False, True)
            else:
                mm(A("B2", 256, 512), A("ZK", 15 - i, 143 - i), A("MF", 256 * i, 256 * i + 256), n_ == 0, i == 5, "yc%d" % i)
        if n1 == 6 and v:
            act(A("YT"), A("B2", 256, 512), bias=136.0 if v == 1 else 0.0)

    def yc_finish():
        act(A("DA", 0, 256), A("YT"), AF.Relu, bias=2.0 ** 21, scale=-2.0 ** 21)
        o = A("B3", 256, 512)
        mm(o, IDM, A("YT"), True, False); mm(o, NIM, A("C1"), False, False); mm(o, IDN, A("DA", 0, 256), False, True)
        act(A("YT"), o, AF.Copy)

    TG, IDX, SLOT = A("SU", 32, 44), A("SU", 48, 60), A("SU", 60, 72)
    KA, KBK, OWN, O37 = A("B4", 0, L), A("B5", 0, L), A("B1", L, 2 * L), A("B0", L, 2 * L)
    FP, ZP = A("B1", 0, L), A("B2", L, 2 * L)

    def f_scatter():
        ts(A("FI"), FP, FBI, add)
        ts(A("FG"), A("FI"), 0xFF00, band)
        cp(IN(A("F"), TG), A("FG"))

    def EQ(q, lo=0):
        o = L * q - 8 * q * (q - 1)
        return A("EQ", o + lo, o + L - 16 * q)

    def f_pe():
        mm(FP, A("WF", 0, 128), A("NK"), True, False)
        mm(FP, A("WF", 128, 256), A("CBV"), False, False)
        mm(FP, A("WF", 256, 384), A("KM"), False, True)

    def f_put(tg):
        ts(A("FG"), A("FI"), 0xFF00, band)
        cp(IN(A("F"), tg), A("FG"))

    def facts_out():
        turn(A("FF"), "B3")
        act(A("YO"), A("B3", 0, L), AF.Copy)
        dma(H(T.yo[:]), A("YO"))

    def late_loads():
        dma(A("F"), A("P", 0, PAD))
        dma(A("P", SB, SB + W), A("P", 0, W))
        dma(A("P", SB, SB + W, p=5), KSB)

    keep[0] = True
    for v in range(VI):
        last = v == VI - 1
        TG, TGOLD = (A("SU", 32 + 48 * (u % 2), 44 + 48 * (u % 2)) for u in (v, v + 1))
        z = A("ZL", L * v, L * v + L)
        xw = A("XX", SB, SB + W) if v == 0 else A("XX", 0, SB + W)
        xm = A("XX", PAD)
        xo = [A("B6", 0, L), A("B6", L, 2 * L), A("B7", L, 2 * L), A("B5", 0, L), A("B5", L, 2 * L)]
        IDL, KL = A("SU", 0, 12), A("SU", 12, 24)
        cb, n2, lt = A("B5", L, 2 * L), A("B6", L, 2 * L), A("LT", 16 * v, 16 * v + 12)

        def dv(k0, k1):
            for k in range(k0, k1):
                tt(X("DB", ALL, k, k, k + 1), IN(xw, A("IL", 12 * k, 12 * k + 12)), z, sub)

        def dabs(k0, k1):
            act(X("AB", ALL, slice(k0, k1), k0, k1), X("DB", ALL, slice(k0, k1), k0, k1), AF.Abs)

        def dpe(k0, k1, end=False):
            for r in range(16):
                mm(X("B4", slice(0, 12), slice(k0, k1), 0, L), Z(Z4K, r), X("AB", slice(r, L, 16), slice(k0, k1), k0, k1), False, end and r == 15)

        def gm(c):
            act(A("AM", 1024 * c, 1024 * c + 1024), IN(xm, A("ML", 64 * c, 64 * c + 64)), AF.Copy)

        def gs(c):
            tt(A("YB", 1024 * c, 1024 * c + 1024), IN(xm, A("SL", 64 * c, 64 * c + 64)), A("AM", 1024 * c, 1024 * c + 1024), mn)

        def pz(i):
            for k in range(8):
                mm(X("B%d" % (i % 3), slice(k, 32, 8), ALL), NID, A("ZL", L * v + 64 * (i // 2), L * v + 64 * (i // 2) + 64), k == 0, False)

        def py(i):
            for k in range(8):
                mm(X("B%d" % (i % 3), slice(k, 32, 8), ALL), IDN, A("YB", 1024 * (i // 2) + 8 * (i % 2) + k, 1024 * (i // 2) + 1024, 16), False, k == 7)

        def sabs(i):
            act(X("EB", slice(4 * (i // 2), 4 * (i // 2) + 4), slice(128 * (i % 2), 128 * (i % 2) + 128), i, i + 1), A("B%d" % (i % 3), 0, 512), AF.Abs)

        def e1(i):
            c = i // 2
            for k in range(8 * (i % 2), 8 * (i % 2) + 8):
                mm(A("B4", 64 * c, 64 * c + 64), Z(Z4K, k), X("EB", slice(4 * c, 4 * c + 4), slice(16 * k, 16 * k + 16), i, i + 1),
                   False, i == 5 and k == 15, "e%d" % i)

        def eq(q0, q1):
            for q in range(q0, q1):
                ts(EQ(q), A("B7", 16 * q, L), C("SC", 64 + q), eq_, WR, mul)

        def eqpe():
            mm(A("B6", 0, L), BK, EQ(0), True, False)
            for q in range(12):
                if q:
                    mm(A("B6", 16 * q, 16 * q + 16), BK, A("EQ", EQ(q)[1][0][1], EQ(q)[1][0][1] + 16), False, q == 11)
                if q < 11:
                    mm(A("B6", 16 * q + 16, L), BKX, EQ(q, 16), False, False)

        def g2(q, c0, c1):
            o, i = A("G2B", 16 * c0, 16 * c1), IN(A("MC", 0, PAD), A("CL", c0, c1))
            if q == "S":
                act(o, i, AF.Sign, bias=0.5)
            else:
                ts(o, i, 0.0, ALU.is_ge, 2.0, mul)

        def g2pe(c0, c1):
            mm(A("B2", c0, c1), IDN, A("HN", c0, c1), True, False)
            deal(A("B2", c0, c1), ZPOW, "G2B", 16 * c0, 16 * c1, first=False)

        cp(A("IL"), IN(A("ID"), UPERM))
        act(A("XR"), IN(xw, A("IL", 0, 12 * KS)), AF.Copy)
        mm(KA, IDN, A("KC", 0, L), True, False)
        mm(O37, IDM, A("OF"), True, False); mm(O37, NID, A("KN", 0, L), False, False); mm(O37, NID, A("KN", L, 2 * L), False, True)
        usum(v)
        act(A("UT", 0, 12), A("B7", 0, 12), AF.Copy)
        if v:
            f_pe()
        for j in range(KS):
            mm(xo[j], IDN, A("XR", L * j, L * j + L), True, False)
            mm(xo[j], NID, z, False, True)
        yc_sums(v, 0, 1)
        dv(KS, 7)
        dabs(KS, 7)
        for j in range(KS):
            act(X("AB", ALL, j, j, j + 1), xo[j], AF.Abs)
        dv(7, 11)
        dpe(0, 7)
        dabs(7, 11)
        mm(cb, IDN, A("KN", 0, L), True, False); mm(cb, IDN, A("KN", L, 2 * L), False, False)
        dv(11, 14)
        dpe(7, 11)
        dabs(11, 14)
        dv(14, 16)
        dabs(14, 16)
        dpe(11, 16, True)
        ts(A("HI"), A("ID"), 6, shr); ts(A("LO"), A("ID"), 63, band)
        tt(A("P1"), IN(A("UT", 0, 12), UJ), A("OF"), mul)
        if v:
            ts(A("FI"), FP, FBI, add)
        else:
            loose(step1_constants)
        ts(A("P2"), A("P1"), 5, shr, W - 1, band)
        tt(A("KE"), KA, A("HI"), add)
        tt(A("KS"), KA, A("LO"), add)
        scan(X("KY", ALL, 0, 0, 1), A("RS"), A("KE"), 0.0, mul, mx)
        scan(X("KY", ALL, 1, 1, 2), A("RS"), A("KS"), 0.0, mul, mx)
        act(A("CBS"), A("KE"), AF.Relu, bias=CBB, scale=64.0)
        yc_sums(v, 1, 2)
        mm(cb, IDN, A("CBS"), False, True)
        yc_sums(v, 2, 4)
        top = X("KY", slice(15, L, 16), 0, 0, 1)
        ts(A("T2", 24, 48, 2), top, 4, shr, 0xF0, band)
        ts(A("T2", 0, 24), X("KY", slice(15, L, 16), ALL), 255, band)
        ts(A("SC", 48, 60), top, THW, ALU.is_lt, 2.0 ** 24, mul)
        scan(A("SC", 0, 48), A("D2"), A("T2"), 0.0)
        cp(A("SU", 0, 24), A("SC", 1, 48, 2))
        tt(A("SC", 64, 76), A("SC", 1, 24, 2), A("SC", 48, 60), add)
        act(A("OG"), IN(A("G1B"), KL), AF.Copy)
        if v == 0:
            ts(A("ML"), IN(A("MI"), IDL), float(SB - PAD), add)
            cp(A("M"), IN(A("MI"), IDL))
        else:
            act(A("M"), IN(A("MC"), IDL), AF.Copy)
            ts(A("ML"), IN(A("MC"), IDL), float(SB - PAD), add)
        tt(A("P4"), cb, A("P2"), mn)
        mm(KA, IDN, A("EC", 0, L), True, False); mm(KA, IDN, A("EC", L, 2 * L), False, False)
        mm(A("B6", L, 2 * L), BK345, A("OG"), True, True)
        mm(A("B7", L, 2 * L), IDM, A("M"), True, True)
        gm(0)
        tt(A("P5"), O37, A("P4"), add)
        tt(A("S1"), A("B6", L, 2 * L), A("M"), mul)
        ts(A("P6"), A("P5"), W - 1, band)
        ts(A("S2"), A("S1"), 5, shr, W - 1, band)
        tt(A("S3"), A("B7", L, 2 * L), A("S2"), add)
        ts(A("SL"), A("S3"), float(SB - PAD), add)
        if v == 0:
            gcp(A("MC", 0, 1024), A("MI", 0, 1024))
        if not last:
            gcp(A("OS", L * v, L * v + L), A("P6"))
            send(A("OL", L * (v + 1), L * (v + 2)), A("OS", L * v, L * v + L), v + 1)
        else:
            gcp(A("FF"), A("P6"))
        if v == 0:
            for c in range(1, 4):
                gcp(A("MC", 1024 * c, 1024 * c + 1024), A("MI", 1024 * c, 1024 * c + 1024))
            iota(A("MC", W, SB), [[0, SB - W]], -1)
        act(A("IG"), IN(A("P", 0, W) if v == 0 else A("P"), IDL), AF.Copy)
        yc_sums(v, 4, 6)
        pz(0)
        mm(A("B7", 0, L), BK345, A("IG"), True, True)
        pz(1); pz(2)
        gm(1)
        if v == 0:
            gm(2)
            loose(powers)
            slots(0, 4)
            slot_row()
        gs(0); py(0); py(1)
        sabs(0); sabs(1)
        eq(0, 12)
        pz(3); pz(4)
        eqpe()
        e1(0); e1(1)
        gv, gw = (GV, GV) if v else (G0V, GA)
        if v:
            gm(2)
        else:
            g1(v + 1, "S", gv, gw)
        act(A("WB"), A("B6", 0, L), AF.Copy)
        gs(1)
        py(2); py(3)
        act(A("XO"), IN(xw, IDL), AF.Copy)
        deal(A("B7", 0, 12), Z1, "WB", 0, L)
        sabs(2); sabs(3)
        mm(n2, IDN, A("XO"), True, False); mm(n2, NID, z, False, True)
        act(A("ZN"), n2, AF.Abs, scale=2.0)
        gs(2)
        pz(5); py(4); py(5)
        e1(2); e1(3)
        sabs(4); sabs(5)
        mm(n2, IDN, A("ZN"), True, False); mm(n2, NID, z, False, True)
        e1(4); e1(5)
        if v == 0:
            loose(f_constants)
            late_loads()
        if v == 1:
            loose(end_constants)
        if not last:
            gcp(A("OF"), A("OL", L * (v + 1), L * (v + 2)))
            if v == 0:
                iota(A("MC", SB, SB + W), [[0, W]], -1)
                dma(A("MC", SB, SB + W, p=0), A("CF"))
            g1(v + 1, "V", 0, gv // 2)
            g1(v + 1, "S", gw, (gw + L) // 2)
        else:
            f_put(TGOLD)
            loose(yc_finish)
            loose(facts_out)
        ts(A("SF", 0, 12), A("B7", 0, 12), THR, ALU.is_ge, 2.0 ** 24, mul)
        if not last:
            g1(v + 1, "V", gv // 2, gv)
            g1(v + 1, "S", (gw + L) // 2, L)
        act(A("AM", 3072, 3264), n2, AF.Copy)
        tt(A("SF", 16, 28), A("SF", 0, 12), A("SC", 64, 76), add)
        op("V", lambda: g.vector.transpose(T.KS[:], T.B4[:, 0:12, :]), A("KS"), [A("B4", 0, L)])
        tt(A("SF", 32, 44), A("SF", 16, 28), ALT, mn)
        scan(A("KE"), A("RB"), A("KS"), 0.0, mx, mn)
        cp(TG, A("SF", 32, 44))
        ts(A("NK"), A("B4", 0, L), T2K, ALU.is_gt, -8192.0, mul)
        ts(lt, A("SF", 16, 28), 9000.0, ALU.is_ge, 2.0 ** 24, mul)
        if last:
            tt(A("XC"), A("B7", L, 2 * L), A("NK"), add)
            act(A("KM"), A("XC"), AF.Relu, bias=1.0)
        else:
            g1pe("B3", Z01, 0, gw)
            tt(IN(A("MC", 0, PAD), TG), A("M"), A("NK"), add)
        for jp, (w1, w2) in enumerate(((W10, W20), (W11, W21))):
            mm(A("B5", jp, 12, 2), w1, A("KE", 16 * jp + 15, L, 32), True, False)
            mm(A("B5", jp, 12, 2), w2, A("KE", 31 - 16 * jp, L, 32), False, True)
        if not last:
            g1pe("B3", Z01, gw, L)
            for u in range(v + 1):
                mm(A("B6", 0, 12), BK, A("LT", 16 * u, 16 * u + 12), u == 0, u == v)
            act(OWN, A("OF"), bias=float(SB))
        else:
            mm(FP, A("WF", 0, 128), A("NK"), True, False)
            mm(FP, A("WF", 256, 384), A("KM"), False, False)
        mm(ZP, IHB, z, True, False); mm(ZP, IDN, A("KB", 256, 256 + L), False, False)
        tt(A("SF", 48, 60), A("B5", 0, 12), lt, add)
        tt(A("SI", 0, 12), A("SF", 48, 60), CAP, mn)
        ts(A("SI", 16, 28), A("SI", 0, 12), W - 1, band)
        ts(A("SI", 28, 40), A("SI", 0, 12), 15, band)
        cp(A("SU", 48, 72), A("SI", 16, 40))
        if not last:
            cp(A("CL"), A("B3", 0, L))
        if last:
            tt(A("CBV"), IN(A("DG"), SLOT), A("M"), mul)
            act(A("XC"), IN(A("AM"), IDX), AF.Copy)
            mm(FP, A("WF", 128, 256), A("CBV"), False, True)
            mm(ZP, IH, A("XC"), False, True)
            ts(A("FI"), FP, FBI, add)
            f_put(TG)
            ts(A("YZ"), ZP, M0, add, M0, sub)
            dma(H(T.yz[:]), A("YZ"))
            break
        act(A("XC"), IN(A("AM"), IDX), AF.Copy)
        g1pe("B0", Z2, 0, 64)
        mm(ZP, IH, A("XC"), False, True)
        g2("S", 0, GS // 2)
        g2("V", GS, (GS + L) // 2)
        zs = A("ZS", L * v, L * v + L)
        ts(zs, ZP, M0, add, M0, sub)
        send(A("ZL", L * (v + 1), L * (v + 2)), zs, 5 + v)
        if v == 0:
            for c in range(0, W, 512):
                gcp(A("MF", c, c + 512), A("MI", c, c + 512))
        g1pe("B0", Z2, 64, L)
        g2("V", (GS + L) // 2, L)
        g2("S", GS // 2, GS)
        g2pe(0, GS // 2)
        g2pe(GS, L)
        g2pe(GS // 2, GS)
        act(A("PW"), A("B0", 0, L), AF.Copy)
        act(A("SF", 64, 76), A("B6", 0, 12), scale=-2.0 ** -24, bias=16.0 * (v + 1), acc=ACC)
        act(A("KM"), IN(A("MC", 0, PAD), TG), AF.Relu, bias=1.0)
        tt(A("CBV"), IN(A("DG"), SLOT), A("M"), mul)
        cp(IN(A("XX", 0, PAD), TG), A("XC"))
        if v:
            f_put(TGOLD)
        tt(A("V1"), A("B2", 0, L), A("PW"), mul)
        cp(C("AI", 3), ACC)
        ts(A("V2"), A("V1"), 32768, band)
        ts(C("AI", 4), C("AI", 3), 127, band)
        tt(A("V3"), OWN, A("V2"), sub)
        ts(THW, C("AI", 4), T1P, add, 4096.0, mul)
        tt(A("ID"), A("B3", 0, L), A("V3"), mx)

    for v in ():
        last = v == VI - 1
        z = A("ZL", L * v, L * v + L)
        xw = A("XX", SB, SB + W) if v == 0 else A("XX", 0, SB + W)
        cp(A("IL"), IN(A("ID"), UPERM))
        act(A("XR"), IN(xw, A("IL", 0, 12 * KS)), AF.Copy)
        mm(KA, IDN, A("KC", 0, L), True, False)
        xo = [A("B6", 0, L), A("B6", L, 2 * L), A("B7", L, 2 * L), A("B5", 0, L), A("B5", L, 2 * L)]
        for j in range(KS):
            mm(xo[j], IDN, A("XR", L * j, L * j + L), True, False)
            mm(xo[j], NID, z, False, True)

        def dv(k0, k1):
            for k in range(k0, k1):
                tt(X("DB", ALL, k, k, k + 1), IN(xw, A("IL", 12 * k, 12 * k + 12)), z, sub)

        def dabs(k0, k1):
            act(X("AB", ALL, slice(k0, k1), k0, k1), X("DB", ALL, slice(k0, k1), k0, k1), AF.Abs)

        def dpe(k0, k1, end=False):
            for r in range(16):
                mm(X("B4", slice(0, 12), slice(k0, k1), 0, L), Z(Z4K, r), X("AB", slice(r, L, 16), slice(k0, k1), k0, k1), False, end and r == 15)
        dv(KS, 6)
        for j in range(KS):
            act(X("AB", ALL, j, j, j + 1), xo[j], AF.Abs)
        dv(6, 9)
        dabs(KS, 6)
        usum(v)
        dpe(0, 6)
        dv(9, 11)
        dabs(6, 9)
        mm(O37, IDM, A("OF"), True, False); mm(O37, NID, A("KN", 0, L), False, False); mm(O37, NID, A("KN", L, 2 * L), False, True)
        dv(11, 14)
        dabs(9, 11)
        dpe(6, 11)
        act(A("UT", 0, 12), A("B7", 0, 12), AF.Copy)
        dv(14, 16)
        dabs(11, 14)
        dabs(14, 16)
        dpe(11, 16, True)
        ts(A("HI"), A("ID"), 6, shr); ts(A("LO"), A("ID"), 63, band)
        if v == 0:
            step1_constants()
        else:
            f_scatter()
        tt(A("P1"), IN(A("UT", 0, 12), UJ), A("OF"), mul)
        tt(A("KE"), KA, A("HI"), add)
        tt(A("KS"), KA, A("LO"), add)
        scan(X("KY", ALL, 0, 0, 1), A("RS"), A("KE"), 0.0, mul, mx)
        scan(X("KY", ALL, 1, 1, 2), A("RS"), A("KS"), 0.0, mul, mx)
        act(A("CBS"), A("KS"), AF.Relu, bias=CBB, scale=64.0)
        top = X("KY", slice(15, L, 16), 0, 0, 1)
        ts(A("T2", 24, 48, 2), top, 4, shr, 0xF0, band)
        ts(A("SC", 48, 60), top, THW, ALU.is_lt, 2.0 ** 24, mul)
        ts(A("T2", 0, 24), X("KY", slice(15, L, 16), ALL), 255, band)
        scan(A("SC", 0, 48), A("D2"), A("T2"), 0.0)
        cp(A("SU", 0, 24), A("SC", 1, 48, 2))
        tt(A("SC", 64, 76), A("SC", 1, 24, 2), A("SC", 48, 60), add)
        IDL, KL = A("SU", 0, 12), A("SU", 12, 24)
        cb = A("B5", L, 2 * L)
        mm(cb, IDN, A("KN", 0, L), True, False); mm(cb, IDN, A("KN", L, 2 * L), False, False); mm(cb, IDN, A("CBS"), False, True)
        act(A("OG"), IN(A("G1B"), KL), AF.Copy)
        mm(A("B6", L, 2 * L), BK345, A("OG"), True, True)
        if v == 0:
            ts(A("ML"), IN(A("MI"), IDL), float(SB - PAD), add)
            cp(A("M"), IN(A("MI"), IDL))
        else:
            act(A("M"), IN(A("MC"), IDL), AF.Copy)
            ts(A("ML"), IN(A("MC"), IDL), float(SB - PAD), add)
        mm(A("B7", L, 2 * L), IDM, A("M"), True, True)
        xm = A("XX", PAD)

        def gm(c):
            act(A("AM", 1024 * c, 1024 * c + 1024), IN(xm, A("ML", 64 * c, 64 * c + 64)), AF.Copy)
            name("members%d" % c, v)
        gm(0)
        ts(A("P2"), A("P1"), 5, shr, W - 1, band)
        tt(A("S1"), A("B6", L, 2 * L), A("M"), mul)
        tt(A("P4"), cb, A("P2"), mn)
        ts(A("S2"), A("S1"), 5, shr, W - 1, band)
        tt(A("P5"), O37, A("P4"), add)
        tt(A("S3"), A("B7", L, 2 * L), A("S2"), add)
        ts(A("P6"), A("P5"), W - 1, band)
        ts(A("SL"), A("S3"), float(SB - PAD), add)
        if v in (1, 2):
            yc_start(8 * v - 8, 8 * v)
            act(A("YT" if v == 1 else "YA"), A("B2", 256, 512), bias=68.0)
        if last:
            yc_finish()
        if v == 0:
            gcp(A("MC", 0, 1024), A("MI", 0, 1024))
        if not last:
            gcp(A("OS", L * v, L * v + L), A("P6"))
            send(A("OL", L * (v + 1), L * (v + 2)), A("OS", L * v, L * v + L), v + 1)
        else:
            gcp(A("FF"), A("P6"))
        if v == 0:
            for c in range(1, 4):
                gcp(A("MC", 1024 * c, 1024 * c + 1024), A("MI", 1024 * c, 1024 * c + 1024))
            iota(A("MC", W, SB), [[0, SB - W]], -1)
        act(A("IG"), IN(A("P", 0, W) if v == 0 else A("P"), IDL), AF.Copy)
        name("ids", v)
        mm(A("B7", 0, L), BK345, A("IG"), True, True)
        gm(1)

        def gs(c):
            tt(A("YB", 1024 * c, 1024 * c + 1024), IN(xm, A("SL", 64 * c, 64 * c + 64)), A("AM", 1024 * c, 1024 * c + 1024), mn)
            name("supports%d" % c, v)

        def psub(c, h):
            bank = "B%d" % ((2 * c + h) % 3)
            for k in range(8):
                o = X(bank, slice(k, 32, 8), ALL)
                mm(o, IDN, A("YB", 1024 * c + 8 * h + k, 1024 * c + 1024, 16), True, False, "psub")
                mm(o, NID, A("ZL", L * v + 64 * c, L * v + 64 * c + 64), False, True, "psub")

        def sabs(c, h):
            act(X("EB", slice(4 * c, 4 * c + 4), slice(128 * h, 128 * h + 128), 2 * c + h, 2 * c + h + 1), A("B%d" % ((2 * c + h) % 3), 0, 512), AF.Abs)
            name("abs%d" % (2 * c + h), v)

        def e1(c):
            if c == 0:
                mm(KA, IDN, A("EC", 0, L), True, False); mm(KA, IDN, A("EC", L, 2 * L), False, False)
            for h in range(2):
                for k in range(8 * h, 8 * h + 8):
                    mm(A("B4", 64 * c, 64 * c + 64), Z(Z4K, k), X("EB", slice(4 * c, 4 * c + 4), slice(16 * k, 16 * k + 16), 2 * c + h, 2 * c + h + 1),
                       False, c == 2 and k == 15, "e%d" % h)

        def eq(q0, q1):
            for q in range(q0, q1):
                ts(EQ(q), A("B7", 16 * q, L), C("SC", 64 + q), eq_, WR, mul)
                name("equal", v)

        def eqpe():
            mm(A("B6", 0, L), BK, EQ(0), True, False)
            for q in range(12):
                if q:
                    mm(A("B6", 16 * q, 16 * q + 16), BK, A("EQ", EQ(q)[1][0][1], EQ(q)[1][0][1] + 16), False, q == 11)
                if q < 11:
                    mm(A("B6", 16 * q + 16, L), BKX, EQ(q, 16), False, False)

        if v == 0:
            powers()
            slots(0, 4)
            slot_row()
        gs(0); psub(0, 0); psub(0, 1)
        gm(2)
        eq(0, 12)
        gs(1)
        eqpe()
        sabs(0, 0); sabs(0, 1)
        psub(1, 0); psub(1, 1)
        act(A("WB"), A("B6", 0, L), AF.Copy)
        gs(2)
        e1(0)
        deal(A("B7", 0, 12), Z1, "WB", 0, L)
        sabs(1, 0); sabs(1, 1)
        psub(2, 0); psub(2, 1)
        act(A("XO"), IN(xw, IDL), AF.Copy)
        e1(1)
        sabs(2, 0); sabs(2, 1)
        n2 = A("B6", L, 2 * L)
        mm(n2, IDN, A("XO"), True, False); mm(n2, NID, z, False, True)
        e1(2)
        act(A("ZN"), n2, AF.Abs, scale=2.0)
        mm(n2, IDN, A("ZN"), True, False); mm(n2, NID, z, False, True)
        act(A("AM", 3072, 3264), n2, AF.Copy)
        if v == 0:
            f_constants()
            dma(A("F"), A("P", 0, PAD))
            dma(A("P", SB, SB + W), A("P", 0, W))
            dma(A("P", SB, SB + W, p=5), KSB)
        if v == 1:
            end_constants()
        ts(A("SF", 0, 12), A("B7", 0, 12), THR, ALU.is_ge, 2.0 ** 24, mul)
        if not last:
            gcp(A("OF"), A("OL", L * (v + 1), L * (v + 2)))
            g1(v + 1, "V", 0, GV // 2)
        else:
            turn(A("FF"), "B3")
            act(A("YO"), A("B3", 0, L), AF.Copy)
            dma(H(T.yo[:]), A("YO"))
        tt(A("SF", 16, 28), A("SF", 0, 12), A("SC", 64, 76), add)
        if not last:
            g1(v + 1, "V", GV // 2, GV)
            g1(v + 1, "S", GV, (GV + L) // 2)
            g1pe("B3", Z01, 0, GV)
            g1(v + 1, "S", (GV + L) // 2, L)
            g1pe("B3", Z01, GV, L)
        lt = A("LT", 16 * v, 16 * v + 12)
        tt(A("SF", 32, 44), A("SF", 16, 28), ALT, mn)
        ts(lt, A("SF", 16, 28), 9000.0, ALU.is_ge, 2.0 ** 24, mul)
        cp(TG, A("SF", 32, 44))
        op("V", lambda: g.vector.transpose(T.KS[:], T.B4[:, 0:12, :]), A("KS"), [A("B4", 0, L)])
        ts(A("NK"), A("B4", 0, L), T2K, ALU.is_gt, -8192.0, mul)
        scan(A("KE"), A("RB"), A("KS"), 0.0, mx, mn)
        for jp, (w1, w2) in enumerate(((W10, W20), (W11, W21))):
            mm(A("B5", jp, 12, 2), w1, A("KE", 16 * jp + 15, L, 32), True, False)
            mm(A("B5", jp, 12, 2), w2, A("KE", 31 - 16 * jp, L, 32), False, True)
        if last:
            tt(A("XC"), A("B7", L, 2 * L), A("NK"), add)
            mm(FP, A("WF", 0, 128), A("NK"), True, False)
            act(A("KM"), A("XC"), AF.Relu, bias=1.0)
            mm(FP, A("WF", 256, 384), A("KM"), False, False)
        else:
            tt(IN(A("MC", 0, PAD), TG), A("M"), A("NK"), add)
        tt(A("SF", 48, 60), A("B5", 0, 12), lt, add)
        mm(ZP, IHB, z, True, False); mm(ZP, IDN, A("KB", 256, 256 + L), False, False)
        if not last:
            cp(A("CL"), A("B3", 0, L))
        tt(A("SI", 0, 12), A("SF", 48, 60), CAP, mn)
        ts(A("SI", 16, 28), A("SI", 0, 12), W - 1, band)
        ts(A("SI", 28, 40), A("SI", 0, 12), 15, band)
        cp(A("SU", 48, 72), A("SI", 16, 40))

        def g2(q, c0, c1):
            o, i = A("G2B", 16 * c0, 16 * c1), IN(A("MC", 0, PAD), A("CL", c0, c1))
            if q == "S":
                act(o, i, AF.Sign, bias=0.5)
            else:
                ts(o, i, 0.0, ALU.is_ge, 2.0, mul)

        def g2pe(c0, c1):
            mm(A("B2", c0, c1), IDN, A("HN", c0, c1), True, False)
            deal(A("B2", c0, c1), ZPOW, "G2B", 16 * c0, 16 * c1, first=False)
        if last:
            tt(A("CBV"), IN(A("DG"), SLOT), A("M"), mul)
            act(A("XC"), IN(A("AM"), IDX), AF.Copy)
            mm(FP, A("WF", 128, 256), A("CBV"), False, True)
            mm(ZP, IH, A("XC"), False, True)
            f_scatter()
            ts(A("YZ"), ZP, M0, add, M0, sub)
            dma(H(T.yz[:]), A("YZ"))
            break
        act(A("XC"), IN(A("AM"), IDX), AF.Copy)
        mm(ZP, IH, A("XC"), False, True)
        g2("S", 0, GS // 2)
        tt(A("CBV"), IN(A("DG"), SLOT), A("M"), mul)
        zs = A("ZS", L * v, L * v + L)
        ts(zs, ZP, M0, add, M0, sub)
        send(A("ZL", L * (v + 1), L * (v + 2)), zs, 5 + v)
        if v == 0:
            for c in range(0, W, 512):
                iota(A("MC", SB + c, SB + c + 512), [[0, 512]], -1)
            dma(A("MC", SB, SB + W, p=0), A("CF"))
            for c in range(0, W, 512):
                gcp(A("MF", c, c + 512), A("MI", c, c + 512))
        g1pe("B0", Z2, 0, GV); g1pe("B0", Z2, GV, L)
        g2("V", GS, L)
        g2("S", GS // 2, GS)
        g2pe(0, GS // 2)
        g2pe(GS, L)
        act(OWN, A("OF"), bias=float(SB))
        for u in range(v + 1):
            mm(A("B6", 0, 12), BK, A("LT", 16 * u, 16 * u + 12), u == 0, u == v)
        g2pe(GS // 2, GS)
        cp(IN(A("XX", 0, PAD), TG), A("XC"))
        act(A("PW"), A("B0", 0, L), AF.Copy)
        act(A("SF", 64, 76), A("B6", 0, 12), scale=-2.0 ** -24, bias=16.0 * (v + 1), acc=ACC)
        act(A("KM"), IN(A("MC", 0, PAD), TG), AF.Relu, bias=1.0)
        mm(FP, A("WF", 0, 128), A("NK"), True, False)
        mm(FP, A("WF", 128, 256), A("CBV"), False, False)
        mm(FP, A("WF", 256, 384), A("KM"), False, True)
        tt(A("V1"), A("B2", 0, L), A("PW"), mul)
        cp(C("AI", 3), ACC)
        ts(A("V2"), A("V1"), 32768, band)
        ts(C("AI", 4), C("AI", 3), 127, band)
        tt(A("V3"), OWN, A("V2"), sub)
        ts(THW, C("AI", 4), T1P, add, 4096.0, mul)
        tt(A("ID"), A("B3", 0, L), A("V3"), mx)

    act(A("B0", 0, 256), A("CF"), AF.Copy)
    act(A("B0", 256, 512), A("C1"), AF.Copy)
    mm(A("B4", 0, 256), IDN, KNEG, True, False)
    mm(A("B5", 0, 256), NIM, A("CF"), True, False)
    mm(A("B6", 0, 256), NIM, A("C1"), True, False); mm(A("B6", 0, 256), IDN, K20, False, False)
    for c in range(4):
        for h, q in enumerate("VS"):
            gat(q, A("FL", 1024 * c + 512 * h, 1024 * c + 512 * h + 512), IN(A("F"), A("LA", 64 * c + 32 * h, 64 * c + 32 * h + 32)))
        for bank, kind in (("B4", ZMK), ("B5", Z345)):
            deal(A(bank, 64 * c, 64 * c + 64), kind, "FL", 1024 * c, 1024 * c + 1024, False, c == 3)
    deal(A("B6", 0, 256), ZSM, "FL", 0, W, False)
    tt(A("FV"), A("B4", 0, 256), A("PWA"), mul)
    ts(A("FB"), A("FV"), 15, shr, 1, band)
    tt(A("FE"), A("B5", 0, 256), A("FB"), mul)
    tt(A("FR"), A("B0", 0, 256), A("FE"), add)
    dma(H(T.yr[:]), A("FR"))
    ts(A("B7", 0, 256), A("FE"), 0.0, eq_)
    tt(A("B3", 256, 512), A("B6", 0, 256), A("YT"), mn)
    tt(A("FT"), A("B3", 256, 512), A("FB"), mul)
    tt(A("FU"), A("B0", 256, 512), A("FT"), add)
    tt(A("FZ"), A("B7", 0, 256), A("FU"), mul)
    dma(H(T.yc[:]), A("FZ"), "S")

    if not PLAN:
        PLAN.extend(plan(ops))
    cnt = {"V": 0, "S": 0, "P": 0, "G": 0, "d": 0, "s": 0}
    for i, need in PLAN:
        for j in need:
            ops[j]["sig"] = True
    for i, need in PLAN:
        o = ops[i]
        if o["k"] == "a":
            o["at"] = (o["sem"], neng)
            continue
        for j in need:
            Q[o["q"]].wait_ge(T.sem[ops[j]["at"][0]], ops[j]["at"][1])
        for fn in o["fn"]:
            ins = fn()
        if o["k"] == "d":
            o["at"] = ("d%d" % cnt["d"], 16)
            cnt["d"] += 1
            ins.then_inc(T.sem[o["at"][0]], 16)
        elif o["k"] == "s":
            cnt["s"] += neng
        elif o.get("sig"):
            cnt[o["q"]] += 1
            o["at"] = ("c" + o["q"], cnt[o["q"]])
            ins.then_inc(T.sem[o["at"][0]], 1)
    for o in ops:
        if o["k"] == "d" and not o.get("sig"):
            g.sync.wait_ge(T.sem[o["at"][0]], 16)
    g.wait_ge(T.sem.sent, cnt["s"])
